import numpy as np
import ml_dtypes


def mxq(x, axis, fmt="e4m3"):
    dtype, down = {"e4m3": (ml_dtypes.float8_e4m3fn, 7), "e5m2": (ml_dtypes.float8_e5m2, 14)}[fmt]
    v = np.moveaxis(np.asarray(x, np.float32).astype(ml_dtypes.bfloat16).astype(np.float64), axis, -1)
    blocks = v.reshape(v.shape[:-1] + (-1, 32))
    amax = np.abs(blocks).max(-1, keepdims=True)
    byte = np.maximum(np.where(amax > 0, np.frexp(amax)[1] - 1 + 127, 0) - down, 1)
    scale = np.exp2(byte - 127.0)
    codes = (blocks / scale).astype(np.float32).astype(dtype).astype(np.float64)
    return np.moveaxis((codes * scale).reshape(v.shape), -1, axis)


WIDE = False


def mx_kscale(k):
    if not WIDE:
        return np.ones(k)
    levels = np.array([10, -10, 5, -5, 0])
    if k % 512:
        return np.exp2(np.random.permutation(np.resize(levels, k // 32))).repeat(32)
    a = np.empty((k // 512, 16))
    for p in range(k // 512):
        a[p, :8] = np.random.permutation(np.resize(levels, 8))
        for g in range(8):
            far = levels[np.abs(levels - a[p, g]) >= 10]
            a[p, g + 8] = far[np.random.randint(len(far))]
    return np.exp2(a.ravel()).repeat(32)


def f64(x):
    return np.asarray(x).astype(np.float64)


def striped(idx):
    return np.tile(idx.reshape(-1, 16).T, (8, 1)).astype(np.uint16)


def unstriped(offs):
    return offs[:16].T.reshape(-1).astype(np.int64)


def striped8(idx):
    return np.concatenate([x.reshape(-1, 16).T for x in idx]).astype(np.uint16)


def runs(offs, k):
    lists = np.stack([offs[16 * r : 16 * r + 16].T.reshape(-1) for r in range(8)]).astype(np.int64)
    return lists[np.arange(k) % 512 // 64]


def pack_weight(w):
    k, n = w.shape
    w = f64(np.asarray(w, np.float32).astype(ml_dtypes.bfloat16)).reshape(k // 32, 32, n)
    amax = np.abs(w).max(1)
    byte = np.clip(np.where(amax > 0, np.frexp(amax)[1] - 1 + 127 - 7, 1), 1, 254)
    scaled = (w * np.exp2(127.0 - byte)[:, None, :]).reshape(k, n).astype(np.float32)
    words = np.ascontiguousarray(scaled.reshape(k // 512, 128, 4, n).transpose(0, 1, 3, 2)).astype(ml_dtypes.float8_e4m3fn).view(np.uint8)
    return words, np.ascontiguousarray(byte.astype(np.uint8).reshape(k // 512, 16, n))


def unpack_weight(words, scales):
    g, p, n, _ = words.shape
    vals = np.ascontiguousarray(words).view(ml_dtypes.float8_e4m3fn).astype(np.float64) * np.repeat(np.exp2(scales.astype(np.float64) - 127.0), 8, axis=1)[..., None]
    return vals.transpose(0, 1, 3, 2).reshape(g * 512, n)


E2M1 = np.array([0.0, 0.5, 1.0, 1.5, 2.0, 3.0, 4.0, 6.0, -0.0, -0.5, -1.0, -1.5, -2.0, -3.0, -4.0, -6.0])


def pack_fp4(w):
    k, n = w.shape
    w = f64(np.asarray(w, np.float32).astype(ml_dtypes.bfloat16)).reshape(k // 32, 32, n)
    amax = np.abs(w).max(1)
    mant, ex = np.frexp(amax / 6.0)
    byte = np.clip(np.where(amax > 0, np.where(mant > 0.5, ex, ex - 1) + 127, 1), 1, 254)
    scaled = (w * np.exp2(127.0 - byte)[:, None, :]).reshape(k, n).astype(np.float32)
    c = np.ascontiguousarray(scaled.reshape(k // 512, 128, 4, n).transpose(0, 1, 3, 2)).astype(ml_dtypes.float4_e2m1fn).view(np.uint8) & 0xF
    words = (c[..., 0::2] | (c[..., 1::2] << 4)).reshape(k // 512, 128, 2 * n)
    return np.ascontiguousarray(words), np.ascontiguousarray(byte.astype(np.uint8).reshape(k // 512, 16, n))


def unpack_fp4(words, scales):
    g, _, n = scales.shape
    words = np.ascontiguousarray(words).reshape(g, 128, n, 2)
    nib = np.empty((g, 128, n, 4), np.uint8)
    nib[..., 0::2] = words & 0xF
    nib[..., 1::2] = words >> 4
    vals = E2M1[nib] * np.repeat(np.exp2(scales.astype(np.float64) - 127.0), 8, axis=1)[..., None]
    return vals.transpose(0, 1, 3, 2).reshape(g * 512, n)


def sigmoid(v):
    return 1.0 / (1.0 + np.exp(-np.maximum(v, -700.0)))

def planes(y):
    n, m = y.shape
    v = y.astype(np.float32).astype(ml_dtypes.bfloat16).astype(np.float64).reshape(n // 32, 32, m)
    top = np.abs(v).max(1)
    byte = np.clip(np.where(top > 0, np.frexp(top)[1] - 1 + 127 - 7, 1), 1, 254)
    codes = (v * np.exp2(127.0 - byte)[:, None, :]).reshape(n, m).astype(np.float32).astype(ml_dtypes.float8_e4m3fn).view(np.uint8)
    words = codes.reshape(n // 512, 128, 4, m).transpose(0, 1, 3, 2)
    return np.ascontiguousarray(words), np.ascontiguousarray(byte.astype(np.uint8).reshape(n // 512, 16, m))


K, T, S, N, H = 512, 2048, 512, 512, 512


def setup_inputs():
    n = np.random.standard_normal
    s = mx_kscale(K)[:, None]
    u = mx_kscale(H)
    packed_xT = pack_weight(n((K, T)) * s)
    packed_w1 = pack_fp4(n((K, H)) / np.sqrt(K) / s)
    packed_w3 = pack_fp4(n((H, N)) / np.sqrt(H) / u[:, None])
    return {
        "x_words": packed_xT[0],
        "x_scales": packed_xT[1],
        "w1_words": packed_w1[0],
        "w1_scales": packed_w1[1],
        "w2": (n((K, H)) / np.sqrt(K) / s * u).astype(np.float32),
        "w3_words": packed_w3[0],
        "w3_scales": packed_w3[1],
        "offs": striped(np.random.permutation(T)[:S]),
        "near": striped8(np.random.randint(0, S, (8, S))),
        "far": striped8(np.random.randint(0, S, (8, S))),
    }


def reference(x_words, x_scales, w1_words, w1_scales, w2, w3_words, w3_scales, offs, near, far):
    xq = unpack_weight(x_words, x_scales)[:, unstriped(offs)]
    b = mxq(f64(w2), 0, "e4m3").T @ xq
    a = sigmoid(unpack_fp4(w1_words, w1_scales).T @ xq)
    b2 = b + a * (b[np.arange(H)[:, None], runs(near, H)])
    a2 = a * (a[np.arange(H)[:, None], runs(near, H)])
    z = b2 + a2 * (b2[np.arange(H)[:, None], runs(far, H)])
    out_0 = unpack_fp4(w3_words, w3_scales).T @ mxq(z, 0, "e4m3")
    return (out_0,) + planes(out_0)

@@ -1,0 +1,217 @@
+from contextlib import ExitStack
+
+import concourse.mybir as mybir
+from concourse.masks import make_identity
+
+K, T, S, H, N = 512, 2048, 512, 512, 512
+FLOPS = 2 * S * (2 * K * H + H * N)
+
+F32 = mybir.dt.float32
+BF16 = mybir.dt.bfloat16
+I32 = mybir.dt.int32
+U32 = mybir.dt.uint32
+U16 = mybir.dt.uint16
+U8 = mybir.dt.uint8
+FP8X4 = mybir.dt.float8_e4m3fn_x4
+FP4X4 = mybir.dt.float4_e2m1fn_x4
+MULT = mybir.AluOpType.mult
+ADD = mybir.AluOpType.add
+SIGMOID = mybir.ActivationFunctionType.Sigmoid
+
+P = 128
+PACK = 4
+HALF = S // 2
+CHUNK = 128
+PER_COL = 16
+
+
+def load_scale_rows(queue, tile, rows):
+    for q in range(4):
+        queue.dma_start(out=tile[32 * q : 32 * q + 4, :].bitcast(I32), in_=rows[4 * q : 4 * q + 4, :].bitcast(I32))
+
+
+def deal_words(eng, dealt, raw):
+    eng.tensor_copy(
+        out=dealt[:].rearrange("p (t m e) -> p t m e", t=PACK, e=2),
+        in_=raw[:].rearrange("p (m t e) -> p t m e", t=PACK, e=2),
+    )
+
+
+def deal_scales(eng, dealt, raw):
+    eng.tensor_copy(
+        out=dealt[:].rearrange("p (t m) -> p t m", t=PACK),
+        in_=raw[:].rearrange("p (m t) -> p t m", t=PACK),
+    )
+
+
+def tile_picked_scan2_none_po_kernel(
+    tc, x_words, x_scales, w1_words, w1_scales, w2, w3_words, w3_scales, offs, near, far, out_0, out_1, out_2
+):
+    nc = tc.nc
+    with ExitStack() as ctx:
+        keep = ctx.enter_context(tc.tile_pool(name="keep", bufs=1))
+        ring = ctx.enter_context(tc.tile_pool(name="ring", bufs=2))
+        psum = ctx.enter_context(tc.psum_pool(name="psum", bufs=1))
+
+        offs_sb = keep.tile([P, S // PER_COL], U16, name="offs_sb")
+        near_sb = keep.tile([P, S // PER_COL], U16, name="near_sb")
+        far_sb = keep.tile([P, S // PER_COL], U16, name="far_sb")
+        xw_raw = keep.tile([P, T], I32, name="xw_raw", align_bytes=64)
+        xs_raw = keep.tile([P, T], U8, name="xs_raw", align_bytes=64)
+        ww_raw = keep.tile([P, 2 * H], U8, name="ww_raw", align_bytes=64)
+        ws_raw = keep.tile([P, H], U8, name="ws_raw", align_bytes=64)
+        w2_raw = [keep.tile([P, PACK, H // 2], F32, name="w2_raw%d" % u, align_bytes=64) for u in range(2)]
+        ident = keep.tile([P, P], F32, name="ident")
+
+        nc.vector.memset(xs_raw[:].bitcast(I32), 0)
+        nc.gpsimd.memset(ws_raw[:].bitcast(I32), 0)
+
+        nc.sync.dma_start(offs_sb[:], offs)
+        nc.sync.dma_start(out=ww_raw[:].bitcast(I32), in_=w1_words[0].bitcast(I32))
+        w2_rows = w2.rearrange("(p j) c -> p j c", j=PACK)
+        for u in range(2):
+            nc.sync.dma_start(out=w2_raw[u][:], in_=w2_rows[:, :, u * H // 2 : (u + 1) * H // 2])
+        nc.sync.dma_start(near_sb[:], near)
+        nc.sync.dma_start(far_sb[:], far)
+        nc.sync.dma_start(out=xw_raw[:], in_=x_words[0].rearrange("p n r -> p (n r)").bitcast(I32))
+        load_scale_rows(nc.scalar, xs_raw, x_scales[0])
+        load_scale_rows(nc.scalar, ws_raw, w1_scales[0])
+
+        w1w = keep.tile([P, 2 * H], U8, name="w1w", align_bytes=64)
+        w1s = keep.tile([P, H], U8, name="w1s", align_bytes=64)
+        w3w = keep.tile([P, 2 * N], U8, name="w3w", align_bytes=64)
+        w3s = keep.tile([P, N], U8, name="w3s", align_bytes=64)
+        xq = keep.tile([P, S], U32, name="xq", align_bytes=64)
+        xqs = keep.tile([P, S], U8, name="xqs", align_bytes=64)
+        w2g = keep.tile([P, PACK, P, PACK], BF16, name="w2g", align_bytes=64)
+        w2q = keep.tile([P, H], U32, name="w2q", align_bytes=64)
+        w2s = keep.tile([P, H], U8, name="w2s", align_bytes=64)
+
+        deal_words(nc.vector, w1w, ww_raw)
+        nc.sync.dma_start(out=ww_raw[:].bitcast(I32), in_=w3_words[0].bitcast(I32))
+        nc.vector.tensor_copy(xqs[:], xs_raw[:].indirect(offs_sb[:]))
+
+        dst = w2g[:].rearrange("p t m j -> p m t j")
+        for u in range(2):
+            nc.scalar.copy(out=dst[:, u * P // 2 : (u + 1) * P // 2], in_=w2_raw[u][:].rearrange("p j (m t) -> p m t j", t=PACK))
+        deal_scales(nc.gpsimd, w1s, ws_raw)
+        load_scale_rows(nc.sync, ws_raw, w3_scales[0])
+        nc.vector.quantize_mx(out=w2q[:].bitcast(FP8X4), scales=w2s[:], in_=w2g[:].rearrange("p t m j -> p (t m j)"))
+        nc.vector.tensor_copy(xq[:], xw_raw[:].bitcast(U32).indirect(offs_sb[:]))
+
+        a = [keep.tile([P, S], F32, name="a%d" % t) for t in range(PACK)]
+        b = [keep.tile([P, S], F32, name="b%d" % t) for t in range(PACK)]
+        b2 = [keep.tile([P, S], F32, name="b2_%d" % t) for t in range(PACK)]
+        g1 = [keep.tile([P, S], F32, name="g1_%d" % t) for t in range(PACK)]
+        for t in range(PACK):
+            cols = slice(t * P, (t + 1) * P)
+            pa = psum.tile([P, S], F32, name="bank%d" % t)
+            pb = psum.tile([P, S], F32, name="bank%d" % (t - 1 if t else PACK))
+            nc.tensor.matmul_mx(
+                out=pa[:], lhsT=w1w[:, 2 * t * P : 2 * (t + 1) * P].bitcast(FP4X4), lhsT_scale=w1s[:, cols],
+                rhs=xq[:].bitcast(FP8X4), rhs_scale=xqs[:], start=True, stop=True,
+            )
+            nc.tensor.matmul_mx(
+                out=pb[:], lhsT=w2q[:, cols].bitcast(FP8X4), lhsT_scale=w2s[:, cols],
+                rhs=xq[:].bitcast(FP8X4), rhs_scale=xqs[:], start=True, stop=True,
+            )
+            nc.scalar.activation(a[t][:], pa[:], SIGMOID)
+            if t == 0:
+                nc.vector.tensor_copy(out=b[t][:], in_=pb[:])
+            else:
+                nc.scalar.copy(out=b[t][:], in_=pb[:])
+        deal_words(nc.gpsimd, w3w, ww_raw)
+        deal_scales(nc.gpsimd, w3s, ws_raw)
+        make_identity(nc, ident[:])
+
+        def entries(lst, lo, hi):
+            return lst[:, lo // PER_COL : hi // PER_COL]
+
+        for t in range(PACK + 1):
+            if t < PACK:
+                for lo in range(0, S, HALF):
+                    nc.vector.tensor_tensor(
+                        g1[t][:, lo : lo + HALF], b[t][:].indirect(entries(near_sb, lo, lo + HALF)), a[t][:, lo : lo + HALF], MULT
+                    )
+            if t > 0:
+                nc.vector.tensor_tensor(b2[t - 1][:], b[t - 1][:], g1[t - 1][:], ADD)
+
+        yq = keep.tile([P, S], U32, name="yq", align_bytes=64)
+        ys = keep.tile([P, S], U8, name="ys", align_bytes=64)
+        out_rows = out_0.rearrange("(p t) j -> p t j", t=PACK)
+        out_words = out_1[0].rearrange("p n r -> p (n r)").bitcast(I32)
+        chunks = S // CHUNK
+
+        def combine(c):
+            lo, hi = c * CHUNK, (c + 1) * CHUNK
+            h = ring.tile([P, PACK, CHUNK], F32, name="h")
+            g2 = ring.tile([P, PACK, CHUNK], F32, name="g2")
+            for t in range(PACK):
+                nc.vector.tensor_tensor(h[:, t, :], b2[t][:].indirect(entries(far_sb, lo, hi)), a[t][:, lo:hi], MULT)
+            for t in range(PACK):
+                nc.vector.tensor_tensor(g2[:, t, :], a[t][:].indirect(entries(near_sb, lo, hi)), h[:, t, :], MULT)
+            zg = ring.tile([P, CHUNK, PACK], BF16, name="zg", align_bytes=64)
+            if c == chunks - 1:
+                z = ring.tile([P, PACK, CHUNK], F32, name="z")
+                for t in range(PACK):
+                    nc.vector.tensor_tensor(z[:, t, :], b2[t][:, lo:hi], g2[:, t, :], ADD)
+                nc.vector.tensor_copy(
+                    out=zg[:].rearrange("p (n i) t -> p n t i", i=4),
+                    in_=z[:].rearrange("p t (n i) -> p n t i", i=4),
+                )
+                return zg
+            zt = psum.tile([P, PACK, P], F32, name="bank%d" % (5 + c % 2))
+            for t in range(PACK):
+                nc.tensor.matmul(zt[:, t, :], lhsT=b2[t][:, lo:hi], rhs=ident[:], start=True, stop=False, is_transpose=True)
+                nc.tensor.matmul(zt[:, t, :], lhsT=g2[:, t, :], rhs=ident[:], start=False, stop=True, is_transpose=True)
+            ztb = ring.tile([P, 2, P, 2], BF16, name="ztb", align_bytes=64)
+            nc.scalar.copy(out=ztb[:], in_=zt[:].rearrange("n (u e) p -> n u p e", e=2))
+            pairs = ztb[:].rearrange("n u p e -> n (u p e)").bitcast(F32)
+            zw = psum.tile([P, 2, CHUNK], F32, name="bank%d" % (7 if c % 2 else 4))
+            for u in range(2):
+                nc.tensor.transpose(zw[:, u, :], pairs[:, u * P : (u + 1) * P], ident[:])
+            nc.scalar.copy(
+                out=zg[:].rearrange("p n t -> p (n t)").bitcast(F32).rearrange("p (n u) -> p n u", u=2),
+                in_=zw[:].rearrange("p u n -> p n u"),
+            )
+            return zg
+
+        def project(c, zg):
+            lo, hi = c * CHUNK, (c + 1) * CHUNK
+            zq = ring.tile([P, CHUNK], U32, name="zq", align_bytes=64)
+            zs = ring.tile([P, CHUNK], U8, name="zs", align_bytes=64)
+            nc.vector.quantize_mx(out=zq[:].bitcast(FP8X4), scales=zs[:], in_=zg[:].rearrange("p n t -> p (n t)"))
+            po = psum.tile([P, PACK, CHUNK], F32, name="bank%d" % c)
+            for t in range(PACK):
+                nc.tensor.matmul_mx(
+                    out=po[:, t, :], lhsT=w3w[:, 2 * t * P : 2 * (t + 1) * P].bitcast(FP4X4),
+                    lhsT_scale=w3s[:, t * P : (t + 1) * P],
+                    rhs=zq[:].bitcast(FP8X4), rhs_scale=zs[:], start=True, stop=True,
+                )
+            y = ring.tile([P, PACK, CHUNK], F32, name="y")
+            yg = ring.tile([P, CHUNK, PACK], BF16, name="yg", align_bytes=64)
+            nc.scalar.copy(out=yg[:], in_=po[:].rearrange("p t n -> p n t"))
+            nc.scalar.copy(out=y[:], in_=po[:])
+            nc.sync.dma_start(out=out_rows[:, :, lo:hi], in_=y[:])
+            return yg
+
+        def hand_on(c, yg):
+            lo, hi = c * CHUNK, (c + 1) * CHUNK
+            nc.vector.quantize_mx(
+                out=yq[:, lo:hi].bitcast(FP8X4), scales=ys[:, lo:hi], in_=yg[:].rearrange("p n t -> p (n t)")
+            )
+
+        zgs, ygs = {}, {}
+        for step in range(chunks + 2):
+            if step < chunks:
+                zgs[step] = combine(step)
+            if 1 <= step <= chunks:
+                ygs[step - 1] = project(step - 1, zgs[step - 1])
+            if step >= 2:
+                hand_on(step - 2, ygs[step - 2])
+        last = S - CHUNK
+        nc.sync.dma_start(out=out_words[:, :last], in_=yq[:, :last].bitcast(I32))
+        nc.sync.dma_start(out=out_words[:, last:], in_=yq[:, last:].bitcast(I32))
+        for q in range(4):
+            queue = nc.scalar if q % 2 else nc.sync
+            queue.dma_start(out=out_2[0][4 * q : 4 * q + 4, :].bitcast(I32), in_=ys[32 * q : 32 * q + 4, :].bitcast(I32))

@@ -22,26 +22,31 @@ P = 128
 PACK = 4
 HALF = S // 2
 CHUNK = 128
+CHUNKS = S // CHUNK
 PER_COL = 16
 
 
-def load_scale_rows(queue, tile, rows):
+def load_scale_rows(queue, plane, rows):
     for q in range(4):
-        queue.dma_start(out=tile[32 * q : 32 * q + 4, :].bitcast(I32), in_=rows[4 * q : 4 * q + 4, :].bitcast(I32))
+        queue.dma_start(out=plane[32 * q : 32 * q + 4, :].bitcast(I32), in_=rows[4 * q : 4 * q + 4, :].bitcast(I32))
 
 
-def deal_words(eng, dealt, raw):
-    eng.tensor_copy(
-        out=dealt[:].rearrange("p (t m e) -> p t m e", t=PACK, e=2),
-        in_=raw[:].rearrange("p (m t e) -> p t m e", t=PACK, e=2),
+def deal_words(nc, dealt, raw):
+    nc.vector.tensor_copy(
+        out=dealt.rearrange("p (t m e) -> p t m e", t=PACK, e=2),
+        in_=raw.rearrange("p (m t e) -> p t m e", t=PACK, e=2),
     )
 
 
-def deal_scales(eng, dealt, raw):
-    eng.tensor_copy(
-        out=dealt[:].rearrange("p (t m) -> p t m", t=PACK),
-        in_=raw[:].rearrange("p (m t) -> p t m", t=PACK),
+def deal_scales(nc, dealt, raw):
+    nc.vector.tensor_copy(
+        out=dealt.rearrange("p (t m) -> p t m", t=PACK),
+        in_=raw.rearrange("p (m t) -> p t m", t=PACK),
     )
+
+
+def entries(lists, lo, hi):
+    return lists[:, lo // PER_COL : hi // PER_COL]
 
 
 def tile_picked_scan2_none_po_kernel(
@@ -58,74 +63,88 @@ def tile_picked_scan2_none_po_kernel(
         far_sb = keep.tile([P, S // PER_COL], U16, name="far_sb")
         xw_raw = keep.tile([P, T], I32, name="xw_raw", align_bytes=64)
         xs_raw = keep.tile([P, T], U8, name="xs_raw", align_bytes=64)
-        ww_raw = keep.tile([P, 2 * H], U8, name="ww_raw", align_bytes=64)
-        ws_raw = keep.tile([P, H], U8, name="ws_raw", align_bytes=64)
-        w2_raw = [keep.tile([P, PACK, H // 2], F32, name="w2_raw%d" % u, align_bytes=64) for u in range(2)]
+        w1w_raw = keep.tile([P, 2 * H], U8, name="w1w_raw", align_bytes=64)
+        w3w_raw = keep.tile([P, 2 * N], U8, name="w3w_raw", align_bytes=64)
+        ws_raw = keep.tile([P, H + N], U8, name="ws_raw", align_bytes=64)
+        w2_raw = [keep.tile([P, PACK, H // 2], F32, name="w2_raw%d" % u, tag="w2_raw%d" % u, align_bytes=64) for u in range(2)]
         ident = keep.tile([P, P], F32, name="ident")
 
         nc.vector.memset(xs_raw[:].bitcast(I32), 0)
         nc.gpsimd.memset(ws_raw[:].bitcast(I32), 0)
 
-        nc.sync.dma_start(offs_sb[:], offs)
-        nc.sync.dma_start(out=ww_raw[:].bitcast(I32), in_=w1_words[0].bitcast(I32))
         w2_rows = w2.rearrange("(p j) c -> p j c", j=PACK)
-        for u in range(2):
-            nc.sync.dma_start(out=w2_raw[u][:], in_=w2_rows[:, :, u * H // 2 : (u + 1) * H // 2])
-        nc.sync.dma_start(near_sb[:], near)
-        nc.sync.dma_start(far_sb[:], far)
+        nc.sync.dma_start(offs_sb[:], offs)
+        nc.sync.dma_start(out=w2_raw[0][:], in_=w2_rows[:, :, : H // 2])
+        load_scale_rows(nc.sync, xs_raw, x_scales[0])
+        nc.sync.dma_start(out=w1w_raw[:].bitcast(I32), in_=w1_words[0].bitcast(I32))
         nc.sync.dma_start(out=xw_raw[:], in_=x_words[0].rearrange("p n r -> p (n r)").bitcast(I32))
-        load_scale_rows(nc.scalar, xs_raw, x_scales[0])
-        load_scale_rows(nc.scalar, ws_raw, w1_scales[0])
+        nc.sync.dma_start(out=w2_raw[1][:], in_=w2_rows[:, :, H // 2 :])
+        load_scale_rows(nc.sync, ws_raw[:, :H], w1_scales[0])
+        nc.sync.dma_start(near_sb[:], near)
+        nc.sync.dma_start(out=w3w_raw[:].bitcast(I32), in_=w3_words[0].bitcast(I32))
+        nc.sync.dma_start(far_sb[:], far)
+        load_scale_rows(nc.gpsimd, ws_raw[:, H:], w3_scales[0])
+        make_identity(nc, ident[:])
 
         w1w = keep.tile([P, 2 * H], U8, name="w1w", align_bytes=64)
         w1s = keep.tile([P, H], U8, name="w1s", align_bytes=64)
-        w3w = keep.tile([P, 2 * N], U8, name="w3w", align_bytes=64)
-        w3s = keep.tile([P, N], U8, name="w3s", align_bytes=64)
         xq = keep.tile([P, S], U32, name="xq", align_bytes=64)
         xqs = keep.tile([P, S], U8, name="xqs", align_bytes=64)
-        w2g = keep.tile([P, PACK, P, PACK], BF16, name="w2g", align_bytes=64)
-        w2q = keep.tile([P, H], U32, name="w2q", align_bytes=64)
-        w2s = keep.tile([P, H], U8, name="w2s", align_bytes=64)
+        w2g = keep.tile([P, PACK, P, PACK], BF16, name="w2g", tag="w2g", align_bytes=64)
+        w2q = [keep.tile([P, P], U32, name="w2q%d" % t, tag="w2q%d" % t, align_bytes=64) for t in range(PACK)]
+        w2s = [keep.tile([P, P], U8, name="w2s%d" % t, tag="w2s%d" % t, align_bytes=64) for t in range(PACK)]
 
-        deal_words(nc.vector, w1w, ww_raw)
-        nc.sync.dma_start(out=ww_raw[:].bitcast(I32), in_=w3_words[0].bitcast(I32))
+        dealt = w2g[:].rearrange("p t m j -> p m j t")
+        halves = [raw[:].rearrange("p j (m t) -> p m j t", t=PACK) for raw in w2_raw]
+        mid = P // 2
         nc.vector.tensor_copy(xqs[:], xs_raw[:].indirect(offs_sb[:]))
-
-        dst = w2g[:].rearrange("p t m j -> p m t j")
-        for u in range(2):
-            nc.scalar.copy(out=dst[:, u * P // 2 : (u + 1) * P // 2], in_=w2_raw[u][:].rearrange("p j (m t) -> p m t j", t=PACK))
-        deal_scales(nc.gpsimd, w1s, ws_raw)
-        load_scale_rows(nc.sync, ws_raw, w3_scales[0])
-        nc.vector.quantize_mx(out=w2q[:].bitcast(FP8X4), scales=w2s[:], in_=w2g[:].rearrange("p t m j -> p (t m j)"))
+        deal_words(nc, w1w[:], w1w_raw[:])
+        nc.vector.tensor_copy(out=dealt[:, :mid], in_=halves[0])
         nc.vector.tensor_copy(xq[:], xw_raw[:].bitcast(U32).indirect(offs_sb[:]))
+        nc.vector.tensor_copy(out=dealt[:, mid:], in_=halves[1])
+        deal_scales(nc, w1s[:], ws_raw[:, :H])
+        for t in range(PACK):
+            nc.vector.quantize_mx(
+                out=w2q[t][:].bitcast(FP8X4), scales=w2s[t][:], in_=w2g[:, t].rearrange("p m j -> p (m j)")
+            )
 
         a = [keep.tile([P, S], F32, name="a%d" % t) for t in range(PACK)]
         b = [keep.tile([P, S], F32, name="b%d" % t) for t in range(PACK)]
         b2 = [keep.tile([P, S], F32, name="b2_%d" % t) for t in range(PACK)]
         g1 = [keep.tile([P, S], F32, name="g1_%d" % t) for t in range(PACK)]
+        a_near = keep.tile([P, PACK, S], F32, name="a_near")
+        pas = []
         for t in range(PACK):
             cols = slice(t * P, (t + 1) * P)
             pa = psum.tile([P, S], F32, name="bank%d" % t)
-            pb = psum.tile([P, S], F32, name="bank%d" % (t - 1 if t else PACK))
+            pb = psum.tile([P, S], F32, name="bank%d" % (PACK + t))
+            pas.append(pa)
             nc.tensor.matmul_mx(
                 out=pa[:], lhsT=w1w[:, 2 * t * P : 2 * (t + 1) * P].bitcast(FP4X4), lhsT_scale=w1s[:, cols],
                 rhs=xq[:].bitcast(FP8X4), rhs_scale=xqs[:], start=True, stop=True,
             )
             nc.tensor.matmul_mx(
-                out=pb[:], lhsT=w2q[:, cols].bitcast(FP8X4), lhsT_scale=w2s[:, cols],
+                out=pb[:], lhsT=w2q[t][:].bitcast(FP8X4), lhsT_scale=w2s[t][:],
                 rhs=xq[:].bitcast(FP8X4), rhs_scale=xqs[:], start=True, stop=True,
             )
             nc.scalar.activation(a[t][:], pa[:], SIGMOID)
-            if t == 0:
-                nc.vector.tensor_copy(out=b[t][:], in_=pb[:])
-            else:
-                nc.scalar.copy(out=b[t][:], in_=pb[:])
-        deal_words(nc.gpsimd, w3w, ww_raw)
-        deal_scales(nc.gpsimd, w3s, ws_raw)
-        make_identity(nc, ident[:])
+            nc.scalar.copy(out=b[t][:], in_=pb[:])
+        w3w = keep.tile([P, 2 * N], U8, name="w3w", tag="w2g", align_bytes=64)
+        w3s = keep.tile([P, N], U8, name="w3s", tag="w2_raw1", align_bytes=64)
+        deal_words(nc, w3w[:], w3w_raw[:])
+        deal_scales(nc, w3s[:], ws_raw[:, H:])
+        logit = [
+            keep.tile([P, S], F32, name="logit%d" % t, tag=("w2q3", "w2s3", "logit2", "logit3")[t], align_bytes=64) for t in range(PACK)
+        ]
+        for t in range(PACK):
+            nc.scalar.copy(out=logit[t][:], in_=pas[t][:])
 
-        def entries(lst, lo, hi):
-            return lst[:, lo // PER_COL : hi // PER_COL]
+        def look_near_gate(lo, hi):
+            for t in range(PACK):
+                nc.scalar.activation(a_near[:, t, lo:hi], logit[t][:].indirect(entries(near_sb, lo, hi)), SIGMOID)
+
+        look_near_gate(0, HALF)
+        look_near_gate(HALF, S - CHUNK)
 
         for t in range(PACK + 1):
             if t < PACK:
@@ -140,60 +159,77 @@ def tile_picked_scan2_none_po_kernel(
         ys = keep.tile([P, S], U8, name="ys", align_bytes=64)
         out_rows = out_0.rearrange("(p t) j -> p t j", t=PACK)
         out_words = out_1[0].rearrange("p n r -> p (n r)").bitcast(I32)
-        chunks = S // CHUNK
 
-        def combine(c):
-            lo, hi = c * CHUNK, (c + 1) * CHUNK
-            h = ring.tile([P, PACK, CHUNK], F32, name="h")
-            g2 = ring.tile([P, PACK, CHUNK], F32, name="g2")
+        def look_far(lo, hi, tag):
+            h = keep.tile([P, PACK, hi - lo], F32, name="h%d" % lo, tag=tag, align_bytes=64)
             for t in range(PACK):
                 nc.vector.tensor_tensor(h[:, t, :], b2[t][:].indirect(entries(far_sb, lo, hi)), a[t][:, lo:hi], MULT)
-            for t in range(PACK):
-                nc.vector.tensor_tensor(g2[:, t, :], a[t][:].indirect(entries(near_sb, lo, hi)), h[:, t, :], MULT)
-            zg = ring.tile([P, CHUNK, PACK], BF16, name="zg", align_bytes=64)
-            if c == chunks - 1:
-                z = ring.tile([P, PACK, CHUNK], F32, name="z")
-                for t in range(PACK):
-                    nc.vector.tensor_tensor(z[:, t, :], b2[t][:, lo:hi], g2[:, t, :], ADD)
-                nc.vector.tensor_copy(
-                    out=zg[:].rearrange("p (n i) t -> p n t i", i=4),
-                    in_=z[:].rearrange("p t (n i) -> p n t i", i=4),
-                )
-                return zg
-            zt = psum.tile([P, PACK, P], F32, name="bank%d" % (5 + c % 2))
+            return h
+
+        def carry(c, h_cols, tag):
+            g2 = keep.tile([P, PACK, CHUNK], F32, name="g2_%d" % c, tag=tag, align_bytes=64)
+            nc.vector.tensor_tensor(g2[:], h_cols, a_near[:, :, c * CHUNK : (c + 1) * CHUNK], MULT)
+            return g2
+
+        def add_on_tensor(c, g2):
+            lo, hi = c * CHUNK, (c + 1) * CHUNK
+            zt = psum.tile([P, PACK, P], F32, name="bank%d" % (2 + c % 2))
             for t in range(PACK):
                 nc.tensor.matmul(zt[:, t, :], lhsT=b2[t][:, lo:hi], rhs=ident[:], start=True, stop=False, is_transpose=True)
                 nc.tensor.matmul(zt[:, t, :], lhsT=g2[:, t, :], rhs=ident[:], start=False, stop=True, is_transpose=True)
             ztb = ring.tile([P, 2, P, 2], BF16, name="ztb", align_bytes=64)
             nc.scalar.copy(out=ztb[:], in_=zt[:].rearrange("n (u e) p -> n u p e", e=2))
             pairs = ztb[:].rearrange("n u p e -> n (u p e)").bitcast(F32)
-            zw = psum.tile([P, 2, CHUNK], F32, name="bank%d" % (7 if c % 2 else 4))
+            zw = psum.tile([P, 2, CHUNK], F32, name="bank%d" % (6 + c % 2))
             for u in range(2):
                 nc.tensor.transpose(zw[:, u, :], pairs[:, u * P : (u + 1) * P], ident[:])
+            zg = keep.tile([P, CHUNK, PACK], BF16, name="zg%d" % c, tag="zg%d" % c, align_bytes=64)
             nc.scalar.copy(
                 out=zg[:].rearrange("p n t -> p (n t)").bitcast(F32).rearrange("p (n u) -> p n u", u=2),
                 in_=zw[:].rearrange("p u n -> p n u"),
             )
             return zg
 
+        def add_on_vector(c, g2, tag):
+            lo, hi = c * CHUNK, (c + 1) * CHUNK
+            z = keep.tile([P, PACK, CHUNK], F32, name="z", tag=tag, align_bytes=64)
+            for t in range(PACK):
+                nc.vector.tensor_tensor(z[:, t, :], b2[t][:, lo:hi], g2[:, t, :], ADD)
+            zg = keep.tile([P, CHUNK, PACK], BF16, name="zg%d" % c, align_bytes=64)
+            nc.vector.tensor_copy(
+                out=zg[:].rearrange("p (n i) t -> p n t i", i=4), in_=z[:].rearrange("p t (n i) -> p n t i", i=4)
+            )
+            return zg
+
         def project(c, zg):
             lo, hi = c * CHUNK, (c + 1) * CHUNK
-            zq = ring.tile([P, CHUNK], U32, name="zq", align_bytes=64)
-            zs = ring.tile([P, CHUNK], U8, name="zs", align_bytes=64)
+            zq = keep.tile([P, CHUNK], U32, name="zq%d" % c, align_bytes=64)
+            zs = keep.tile([P, CHUNK], U8, name="zs%d" % c, align_bytes=64)
             nc.vector.quantize_mx(out=zq[:].bitcast(FP8X4), scales=zs[:], in_=zg[:].rearrange("p n t -> p (n t)"))
-            po = psum.tile([P, PACK, CHUNK], F32, name="bank%d" % c)
+            y = keep.tile([P, PACK, CHUNK], F32, name="y%d" % c)
+            yg = keep.tile([P, CHUNK, PACK], BF16, name="yg%d" % c, align_bytes=64)
+            last = c == CHUNKS - 1
+            parts = 2 if last else 1
+            planes = PACK // parts
+            banks = [psum.tile([P, planes, CHUNK], F32, name="bank%d" % (0, 1, 4, 5, 0)[c + u]) for u in range(parts)]
             for t in range(PACK):
                 nc.tensor.matmul_mx(
-                    out=po[:, t, :], lhsT=w3w[:, 2 * t * P : 2 * (t + 1) * P].bitcast(FP4X4),
+                    out=banks[t // planes][:, t % planes, :], lhsT=w3w[:, 2 * t * P : 2 * (t + 1) * P].bitcast(FP4X4),
                     lhsT_scale=w3s[:, t * P : (t + 1) * P],
                     rhs=zq[:].bitcast(FP8X4), rhs_scale=zs[:], start=True, stop=True,
                 )
-            y = ring.tile([P, PACK, CHUNK], F32, name="y")
-            yg = ring.tile([P, CHUNK, PACK], BF16, name="yg", align_bytes=64)
-            nc.scalar.copy(out=yg[:], in_=po[:].rearrange("p t n -> p n t"))
-            nc.scalar.copy(out=y[:], in_=po[:])
+            if last:
+                nc.scalar.copy(out=y[:, :planes], in_=banks[0][:])
+                nc.vector.tensor_copy(out=yg[:, :, planes:], in_=banks[1][:].rearrange("p t n -> p n t"))
+                nc.vector.tensor_copy(out=yg[:, :, :planes], in_=banks[0][:].rearrange("p t n -> p n t"))
+                nc.scalar.copy(out=y[:, planes:], in_=banks[1][:])
+            elif c == CHUNKS - 2:
+                nc.scalar.copy(out=y[:], in_=banks[0][:])
+            else:
+                nc.scalar.copy(out=yg[:], in_=banks[0][:].rearrange("p t n -> p n t"))
+                nc.scalar.copy(out=y[:], in_=banks[0][:])
             nc.sync.dma_start(out=out_rows[:, :, lo:hi], in_=y[:])
-            return yg
+            return y, yg
 
         def hand_on(c, yg):
             lo, hi = c * CHUNK, (c + 1) * CHUNK
@@ -201,17 +237,26 @@ def tile_picked_scan2_none_po_kernel(
                 out=yq[:, lo:hi].bitcast(FP8X4), scales=ys[:, lo:hi], in_=yg[:].rearrange("p n t -> p (n t)")
             )
 
-        zgs, ygs = {}, {}
-        for step in range(chunks + 2):
-            if step < chunks:
-                zgs[step] = combine(step)
-            if 1 <= step <= chunks:
-                ygs[step - 1] = project(step - 1, zgs[step - 1])
-            if step >= 2:
-                hand_on(step - 2, ygs[step - 2])
-        last = S - CHUNK
-        nc.sync.dma_start(out=out_words[:, :last], in_=yq[:, :last].bitcast(I32))
-        nc.sync.dma_start(out=out_words[:, last:], in_=yq[:, last:].bitcast(I32))
+        zg = []
+        for c in range(CHUNKS - 1):
+            zg.append(add_on_tensor(c, carry(c, look_far(c * CHUNK, (c + 1) * CHUNK, "h")[:], "g2_%d" % c)))
+            if c == 0:
+                look_near_gate(S - CHUNK, S)
+        y0, yg0 = project(0, zg[0])
+        h3 = look_far(3 * CHUNK, S, "zg0")
+        y1, yg1 = project(1, zg[1])
+        zg3 = add_on_vector(3, carry(3, h3[:], "zg1"), "z")
+        hand_on(0, yg0)
+        y2, yg2 = project(2, zg[2])
+        y3, yg3 = project(3, zg3)
+        hand_on(1, yg1)
+        nc.vector.tensor_copy(
+            out=yg2[:].rearrange("p (n i) t -> p n t i", i=4), in_=y2[:].rearrange("p t (n i) -> p n t i", i=4)
+        )
+        hand_on(3, yg3)
+        hand_on(2, yg2)
+        nc.sync.dma_start(out=out_words[:, :HALF], in_=yq[:, :HALF].bitcast(I32))
+        nc.sync.dma_start(out=out_words[:, HALF:], in_=yq[:, HALF:].bitcast(I32))
         for q in range(4):
             queue = nc.scalar if q % 2 else nc.sync
             queue.dma_start(out=out_2[0][4 * q : 4 * q + 4, :].bitcast(I32), in_=ys[32 * q : 32 * q + 4, :].bitcast(I32))

@@ -20,15 +20,19 @@ SIGMOID = mybir.ActivationFunctionType.Sigmoid
 
 P = 128
 PACK = 4
+LIST_ROWS = 16
 HALF = S // 2
 CHUNK = 128
 CHUNKS = S // CHUNK
-PER_COL = 16
+LINE = 4
+OUT_BANKS = (0, 1, 4, 5, 6)
 
 
-def load_scale_rows(queue, plane, rows):
-    for q in range(4):
-        queue.dma_start(out=plane[32 * q : 32 * q + 4, :].bitcast(I32), in_=rows[4 * q : 4 * q + 4, :].bitcast(I32))
+def load_scale_rows(queue, scale_tile, rows):
+    for q in (0, 2, 1, 3):
+        queue.dma_start(
+            out=scale_tile[32 * q : 32 * q + 4, :].bitcast(I32), in_=rows[4 * q : 4 * q + 4, :].bitcast(I32)
+        )
 
 
 def deal_words(nc, dealt, raw):
@@ -46,7 +50,7 @@ def deal_scales(nc, dealt, raw):
 
 
 def entries(lists, lo, hi):
-    return lists[:, lo // PER_COL : hi // PER_COL]
+    return lists[:, lo // LIST_ROWS : hi // LIST_ROWS]
 
 
 def tile_picked_scan2_none_po_kernel(
@@ -58,15 +62,17 @@ def tile_picked_scan2_none_po_kernel(
         ring = ctx.enter_context(tc.tile_pool(name="ring", bufs=2))
         psum = ctx.enter_context(tc.psum_pool(name="psum", bufs=1))
 
-        offs_sb = keep.tile([P, S // PER_COL], U16, name="offs_sb")
-        near_sb = keep.tile([P, S // PER_COL], U16, name="near_sb")
-        far_sb = keep.tile([P, S // PER_COL], U16, name="far_sb")
+        offs_sb = keep.tile([P, S // LIST_ROWS], U16, name="offs_sb")
+        near_sb = keep.tile([P, S // LIST_ROWS], U16, name="near_sb")
+        far_sb = keep.tile([P, S // LIST_ROWS], U16, name="far_sb")
         xw_raw = keep.tile([P, T], I32, name="xw_raw", align_bytes=64)
         xs_raw = keep.tile([P, T], U8, name="xs_raw", align_bytes=64)
         w1w_raw = keep.tile([P, 2 * H], U8, name="w1w_raw", align_bytes=64)
         w3w_raw = keep.tile([P, 2 * N], U8, name="w3w_raw", align_bytes=64)
         ws_raw = keep.tile([P, H + N], U8, name="ws_raw", align_bytes=64)
-        w2_raw = [keep.tile([P, PACK, H // 2], F32, name="w2_raw%d" % u, tag="w2_raw%d" % u, align_bytes=64) for u in range(2)]
+        w2_raw = [
+            keep.tile([P, PACK, H // 2], F32, name="w2_raw%d" % u, tag="w2_raw%d" % u, align_bytes=64) for u in range(2)
+        ]
         ident = keep.tile([P, P], F32, name="ident")
 
         nc.vector.memset(xs_raw[:].bitcast(I32), 0)
@@ -94,14 +100,13 @@ def tile_picked_scan2_none_po_kernel(
         w2q = [keep.tile([P, P], U32, name="w2q%d" % t, tag="w2q%d" % t, align_bytes=64) for t in range(PACK)]
         w2s = [keep.tile([P, P], U8, name="w2s%d" % t, tag="w2s%d" % t, align_bytes=64) for t in range(PACK)]
 
-        dealt = w2g[:].rearrange("p t m j -> p m j t")
-        halves = [raw[:].rearrange("p j (m t) -> p m j t", t=PACK) for raw in w2_raw]
-        mid = P // 2
+        w2_dealt = w2g[:].rearrange("p t m j -> p m j t")
+        w2_halves = [raw[:].rearrange("p j (m t) -> p m j t", t=PACK) for raw in w2_raw]
         nc.vector.tensor_copy(xqs[:], xs_raw[:].indirect(offs_sb[:]))
         deal_words(nc, w1w[:], w1w_raw[:])
-        nc.vector.tensor_copy(out=dealt[:, :mid], in_=halves[0])
+        nc.vector.tensor_copy(out=w2_dealt[:, : P // 2], in_=w2_halves[0])
         nc.vector.tensor_copy(xq[:], xw_raw[:].bitcast(U32).indirect(offs_sb[:]))
-        nc.vector.tensor_copy(out=dealt[:, mid:], in_=halves[1])
+        nc.vector.tensor_copy(out=w2_dealt[:, P // 2 :], in_=w2_halves[1])
         deal_scales(nc, w1s[:], ws_raw[:, :H])
         for t in range(PACK):
             nc.vector.quantize_mx(
@@ -111,93 +116,117 @@ def tile_picked_scan2_none_po_kernel(
         a = [keep.tile([P, S], F32, name="a%d" % t) for t in range(PACK)]
         b = [keep.tile([P, S], F32, name="b%d" % t) for t in range(PACK)]
         b2 = [keep.tile([P, S], F32, name="b2_%d" % t) for t in range(PACK)]
-        g1 = [keep.tile([P, S], F32, name="g1_%d" % t) for t in range(PACK)]
+        near_term = [keep.tile([P, S], F32, name="near_term%d" % t) for t in range(PACK)]
         a_near = keep.tile([P, PACK, S], F32, name="a_near")
-        pas = []
+        logit_banks = []
         for t in range(PACK):
-            cols = slice(t * P, (t + 1) * P)
-            pa = psum.tile([P, S], F32, name="bank%d" % t)
-            pb = psum.tile([P, S], F32, name="bank%d" % (PACK + t))
-            pas.append(pa)
+            logit_bank = psum.tile([P, S], F32, name="bank%d" % t)
+            b_bank = psum.tile([P, S], F32, name="bank%d" % (PACK + t))
+            logit_banks.append(logit_bank)
             nc.tensor.matmul_mx(
-                out=pa[:], lhsT=w1w[:, 2 * t * P : 2 * (t + 1) * P].bitcast(FP4X4), lhsT_scale=w1s[:, cols],
-                rhs=xq[:].bitcast(FP8X4), rhs_scale=xqs[:], start=True, stop=True,
+                out=logit_bank[:],
+                lhsT=w1w[:, 2 * t * P : 2 * (t + 1) * P].bitcast(FP4X4),
+                lhsT_scale=w1s[:, t * P : (t + 1) * P],
+                rhs=xq[:].bitcast(FP8X4),
+                rhs_scale=xqs[:],
+                start=True,
+                stop=True,
             )
             nc.tensor.matmul_mx(
-                out=pb[:], lhsT=w2q[t][:].bitcast(FP8X4), lhsT_scale=w2s[t][:],
-                rhs=xq[:].bitcast(FP8X4), rhs_scale=xqs[:], start=True, stop=True,
+                out=b_bank[:],
+                lhsT=w2q[t][:].bitcast(FP8X4),
+                lhsT_scale=w2s[t][:],
+                rhs=xq[:].bitcast(FP8X4),
+                rhs_scale=xqs[:],
+                start=True,
+                stop=True,
             )
-            nc.scalar.activation(a[t][:], pa[:], SIGMOID)
-            nc.scalar.copy(out=b[t][:], in_=pb[:])
+            nc.scalar.activation(a[t][:], logit_bank[:], SIGMOID)
+            nc.scalar.copy(out=b[t][:], in_=b_bank[:])
+
         w3w = keep.tile([P, 2 * N], U8, name="w3w", tag="w2g", align_bytes=64)
         w3s = keep.tile([P, N], U8, name="w3s", tag="w2_raw1", align_bytes=64)
         deal_words(nc, w3w[:], w3w_raw[:])
         deal_scales(nc, w3s[:], ws_raw[:, H:])
-        logit = [
-            keep.tile([P, S], F32, name="logit%d" % t, tag=("w2q3", "w2s3", "logit2", "logit3")[t], align_bytes=64) for t in range(PACK)
-        ]
-        for t in range(PACK):
-            nc.scalar.copy(out=logit[t][:], in_=pas[t][:])
 
-        def look_near_gate(lo, hi):
+        logit_tags = ("w2q%d" % (PACK - 1), "w2s%d" % (PACK - 1), "logit2", "logit3")
+        logit = [keep.tile([P, S], F32, name="logit%d" % t, tag=logit_tags[t], align_bytes=64) for t in range(PACK)]
+        for t in range(PACK):
+            nc.scalar.copy(out=logit[t][:], in_=logit_banks[t][:])
+
+        def look_up_a_near(lo, hi):
             for t in range(PACK):
                 nc.scalar.activation(a_near[:, t, lo:hi], logit[t][:].indirect(entries(near_sb, lo, hi)), SIGMOID)
 
-        look_near_gate(0, HALF)
-        look_near_gate(HALF, S - CHUNK)
+        look_up_a_near(0, HALF)
+        look_up_a_near(HALF, S - CHUNK)
 
         for t in range(PACK + 1):
             if t < PACK:
                 for lo in range(0, S, HALF):
                     nc.vector.tensor_tensor(
-                        g1[t][:, lo : lo + HALF], b[t][:].indirect(entries(near_sb, lo, lo + HALF)), a[t][:, lo : lo + HALF], MULT
+                        near_term[t][:, lo : lo + HALF],
+                        b[t][:].indirect(entries(near_sb, lo, lo + HALF)),
+                        a[t][:, lo : lo + HALF],
+                        MULT,
                     )
             if t > 0:
-                nc.vector.tensor_tensor(b2[t - 1][:], b[t - 1][:], g1[t - 1][:], ADD)
+                nc.vector.tensor_tensor(b2[t - 1][:], b[t - 1][:], near_term[t - 1][:], ADD)
 
         yq = keep.tile([P, S], U32, name="yq", align_bytes=64)
         ys = keep.tile([P, S], U8, name="ys", align_bytes=64)
         out_rows = out_0.rearrange("(p t) j -> p t j", t=PACK)
         out_words = out_1[0].rearrange("p n r -> p (n r)").bitcast(I32)
 
-        def look_far(lo, hi, tag):
-            h = keep.tile([P, PACK, hi - lo], F32, name="h%d" % lo, tag=tag, align_bytes=64)
-            for t in range(PACK):
-                nc.vector.tensor_tensor(h[:, t, :], b2[t][:].indirect(entries(far_sb, lo, hi)), a[t][:, lo:hi], MULT)
-            return h
-
-        def carry(c, h_cols, tag):
-            g2 = keep.tile([P, PACK, CHUNK], F32, name="g2_%d" % c, tag=tag, align_bytes=64)
-            nc.vector.tensor_tensor(g2[:], h_cols, a_near[:, :, c * CHUNK : (c + 1) * CHUNK], MULT)
-            return g2
-
-        def add_on_tensor(c, g2):
+        def look_up_far(c, tag):
             lo, hi = c * CHUNK, (c + 1) * CHUNK
-            zt = psum.tile([P, PACK, P], F32, name="bank%d" % (2 + c % 2))
+            gated = keep.tile([P, PACK, CHUNK], F32, name="gated%d" % c, tag=tag, align_bytes=64)
             for t in range(PACK):
-                nc.tensor.matmul(zt[:, t, :], lhsT=b2[t][:, lo:hi], rhs=ident[:], start=True, stop=False, is_transpose=True)
-                nc.tensor.matmul(zt[:, t, :], lhsT=g2[:, t, :], rhs=ident[:], start=False, stop=True, is_transpose=True)
-            ztb = ring.tile([P, 2, P, 2], BF16, name="ztb", align_bytes=64)
-            nc.scalar.copy(out=ztb[:], in_=zt[:].rearrange("n (u e) p -> n u p e", e=2))
-            pairs = ztb[:].rearrange("n u p e -> n (u p e)").bitcast(F32)
-            zw = psum.tile([P, 2, CHUNK], F32, name="bank%d" % (6 + c % 2))
+                nc.vector.tensor_tensor(
+                    gated[:, t, :], b2[t][:].indirect(entries(far_sb, lo, hi)), a[t][:, lo:hi], MULT
+                )
+            return gated
+
+        def times_a_near(c, gated, tag):
+            far_term = keep.tile([P, PACK, CHUNK], F32, name="far_term%d" % c, tag=tag, align_bytes=64)
+            for pair in (slice(0, 2), slice(2, 4)):
+                nc.vector.tensor_tensor(
+                    far_term[:, pair], gated[:, pair], a_near[:, pair, c * CHUNK : (c + 1) * CHUNK], MULT
+                )
+            return far_term
+
+        def add_on_tensor(c, far_term):
+            lo, hi = c * CHUNK, (c + 1) * CHUNK
+            z_turned = psum.tile([P, PACK, P], F32, name="bank%d" % (2 + c))
+            for t in range(PACK):
+                nc.tensor.matmul(
+                    z_turned[:, t, :], lhsT=b2[t][:, lo:hi], rhs=ident[:], start=True, stop=False, is_transpose=True
+                )
+                nc.tensor.matmul(
+                    z_turned[:, t, :], lhsT=far_term[:, t, :], rhs=ident[:], start=False, stop=True, is_transpose=True
+                )
+            rounded = ring.tile([P, 2, P, 2], BF16, name="rounded", align_bytes=64)
+            nc.scalar.copy(out=rounded[:], in_=z_turned[:].rearrange("n (u e) p -> n u p e", e=2))
+            pairs = rounded[:].rearrange("n u p e -> n (u p e)").bitcast(F32)
+            pairs_back = psum.tile([P, 2, CHUNK], F32, name="bank%d" % (6 + c))
             for u in range(2):
-                nc.tensor.transpose(zw[:, u, :], pairs[:, u * P : (u + 1) * P], ident[:])
+                nc.tensor.transpose(pairs_back[:, u, :], pairs[:, u * P : (u + 1) * P], ident[:])
             zg = keep.tile([P, CHUNK, PACK], BF16, name="zg%d" % c, tag="zg%d" % c, align_bytes=64)
             nc.scalar.copy(
                 out=zg[:].rearrange("p n t -> p (n t)").bitcast(F32).rearrange("p (n u) -> p n u", u=2),
-                in_=zw[:].rearrange("p u n -> p n u"),
+                in_=pairs_back[:].rearrange("p u n -> p n u"),
             )
             return zg
 
-        def add_on_vector(c, g2, tag):
+        def add_on_vector(c, far_term):
             lo, hi = c * CHUNK, (c + 1) * CHUNK
-            z = keep.tile([P, PACK, CHUNK], F32, name="z", tag=tag, align_bytes=64)
+            z = keep.tile([P, PACK, CHUNK], F32, name="z%d" % c, align_bytes=64)
             for t in range(PACK):
-                nc.vector.tensor_tensor(z[:, t, :], b2[t][:, lo:hi], g2[:, t, :], ADD)
+                nc.vector.tensor_tensor(z[:, t, :], b2[t][:, lo:hi], far_term[:, t, :], ADD)
             zg = keep.tile([P, CHUNK, PACK], BF16, name="zg%d" % c, align_bytes=64)
             nc.vector.tensor_copy(
-                out=zg[:].rearrange("p (n i) t -> p n t i", i=4), in_=z[:].rearrange("p t (n i) -> p n t i", i=4)
+                out=zg[:].rearrange("p (n i) t -> p n t i", i=LINE),
+                in_=z[:].rearrange("p t (n i) -> p n t i", i=LINE),
             )
             return zg
 
@@ -211,52 +240,49 @@ def tile_picked_scan2_none_po_kernel(
             last = c == CHUNKS - 1
             parts = 2 if last else 1
             planes = PACK // parts
-            banks = [psum.tile([P, planes, CHUNK], F32, name="bank%d" % (0, 1, 4, 5, 0)[c + u]) for u in range(parts)]
+            banks = [psum.tile([P, planes, CHUNK], F32, name="bank%d" % OUT_BANKS[c + u]) for u in range(parts)]
             for t in range(PACK):
                 nc.tensor.matmul_mx(
-                    out=banks[t // planes][:, t % planes, :], lhsT=w3w[:, 2 * t * P : 2 * (t + 1) * P].bitcast(FP4X4),
+                    out=banks[t // planes][:, t % planes, :],
+                    lhsT=w3w[:, 2 * t * P : 2 * (t + 1) * P].bitcast(FP4X4),
                     lhsT_scale=w3s[:, t * P : (t + 1) * P],
-                    rhs=zq[:].bitcast(FP8X4), rhs_scale=zs[:], start=True, stop=True,
+                    rhs=zq[:].bitcast(FP8X4),
+                    rhs_scale=zs[:],
+                    start=True,
+                    stop=True,
                 )
             if last:
                 nc.scalar.copy(out=y[:, :planes], in_=banks[0][:])
+                nc.sync.dma_start(out=out_rows[:, :planes, lo:hi], in_=y[:, :planes])
                 nc.vector.tensor_copy(out=yg[:, :, planes:], in_=banks[1][:].rearrange("p t n -> p n t"))
                 nc.vector.tensor_copy(out=yg[:, :, :planes], in_=banks[0][:].rearrange("p t n -> p n t"))
                 nc.scalar.copy(out=y[:, planes:], in_=banks[1][:])
-            elif c == CHUNKS - 2:
-                nc.scalar.copy(out=y[:], in_=banks[0][:])
-            else:
-                nc.scalar.copy(out=yg[:], in_=banks[0][:].rearrange("p t n -> p n t"))
-                nc.scalar.copy(out=y[:], in_=banks[0][:])
+                nc.sync.dma_start(out=out_rows[:, planes:, lo:hi], in_=y[:, planes:])
+                return yg
+            nc.scalar.copy(out=yg[:], in_=banks[0][:].rearrange("p t n -> p n t"))
+            nc.scalar.copy(out=y[:], in_=banks[0][:])
             nc.sync.dma_start(out=out_rows[:, :, lo:hi], in_=y[:])
-            return y, yg
+            return yg
 
-        def hand_on(c, yg):
-            lo, hi = c * CHUNK, (c + 1) * CHUNK
+        zg0 = add_on_tensor(0, times_a_near(0, look_up_far(0, "gated"), "far_term0"))
+        look_up_a_near(S - CHUNK, S)
+        zg1 = add_on_tensor(1, times_a_near(1, look_up_far(1, "gated"), "far_term1"))
+        zg2 = add_on_vector(2, times_a_near(2, look_up_far(2, "gated"), "far_term2"))
+        yg0 = project(0, zg0)
+        yg2 = project(2, zg2)
+        gated3 = look_up_far(3, "zg0")
+        yg1 = project(1, zg1)
+        yg3 = project(3, add_on_vector(3, times_a_near(3, gated3, "zg1")))
+
+        for c, yg in enumerate((yg0, yg1, yg2, yg3)):
+            cols = slice(c * CHUNK, (c + 1) * CHUNK)
             nc.vector.quantize_mx(
-                out=yq[:, lo:hi].bitcast(FP8X4), scales=ys[:, lo:hi], in_=yg[:].rearrange("p n t -> p (n t)")
+                out=yq[:, cols].bitcast(FP8X4), scales=ys[:, cols], in_=yg[:].rearrange("p n t -> p (n t)")
             )
-
-        zg = []
-        for c in range(CHUNKS - 1):
-            zg.append(add_on_tensor(c, carry(c, look_far(c * CHUNK, (c + 1) * CHUNK, "h")[:], "g2_%d" % c)))
-            if c == 0:
-                look_near_gate(S - CHUNK, S)
-        y0, yg0 = project(0, zg[0])
-        h3 = look_far(3 * CHUNK, S, "zg0")
-        y1, yg1 = project(1, zg[1])
-        zg3 = add_on_vector(3, carry(3, h3[:], "zg1"), "z")
-        hand_on(0, yg0)
-        y2, yg2 = project(2, zg[2])
-        y3, yg3 = project(3, zg3)
-        hand_on(1, yg1)
-        nc.vector.tensor_copy(
-            out=yg2[:].rearrange("p (n i) t -> p n t i", i=4), in_=y2[:].rearrange("p t (n i) -> p n t i", i=4)
-        )
-        hand_on(3, yg3)
-        hand_on(2, yg2)
-        nc.sync.dma_start(out=out_words[:, :HALF], in_=yq[:, :HALF].bitcast(I32))
-        nc.sync.dma_start(out=out_words[:, HALF:], in_=yq[:, HALF:].bitcast(I32))
+        nc.sync.dma_start(out=out_words[:, : S - CHUNK], in_=yq[:, : S - CHUNK].bitcast(I32))
+        nc.sync.dma_start(out=out_words[:, S - CHUNK :], in_=yq[:, S - CHUNK :].bitcast(I32))
         for q in range(4):
             queue = nc.scalar if q % 2 else nc.sync
-            queue.dma_start(out=out_2[0][4 * q : 4 * q + 4, :].bitcast(I32), in_=ys[32 * q : 32 * q + 4, :].bitcast(I32))
+            queue.dma_start(
+                out=out_2[0][4 * q : 4 * q + 4, :].bitcast(I32), in_=ys[32 * q : 32 * q + 4, :].bitcast(I32)
+            )

@@ -25,11 +25,11 @@ HALF = S // 2
 CHUNK = 128
 CHUNKS = S // CHUNK
 LINE = 4
-OUT_BANKS = (0, 1, 4, 5, 6)
+OUT_BANKS = (4, 5, 6, 7, 0)
 
 
-def load_scale_rows(queue, scale_tile, rows):
-    for q in (0, 2, 1, 3):
+def load_scale_rows(queue, scale_tile, rows, quadrants=(0, 2, 1, 3)):
+    for q in quadrants:
         queue.dma_start(
             out=scale_tile[32 * q : 32 * q + 4, :].bitcast(I32), in_=rows[4 * q : 4 * q + 4, :].bitcast(I32)
         )
@@ -65,35 +65,36 @@ def tile_picked_scan2_none_po_kernel(
         offs_sb = keep.tile([P, S // LIST_ROWS], U16, name="offs_sb")
         near_sb = keep.tile([P, S // LIST_ROWS], U16, name="near_sb")
         far_sb = keep.tile([P, S // LIST_ROWS], U16, name="far_sb")
-        xw_raw = keep.tile([P, T], I32, name="xw_raw", align_bytes=64)
+        xw_raw = keep.tile([P, T], I32, name="xw_raw", tag="xw_raw", align_bytes=64)
         xs_raw = keep.tile([P, T], U8, name="xs_raw", align_bytes=64)
         w1w_raw = keep.tile([P, 2 * H], U8, name="w1w_raw", align_bytes=64)
         w3w_raw = keep.tile([P, 2 * N], U8, name="w3w_raw", align_bytes=64)
-        ws_raw = keep.tile([P, H + N], U8, name="ws_raw", align_bytes=64)
+        w1s_raw = keep.tile([P, H], U8, name="w1s_raw", align_bytes=64)
+        w3s_raw = keep.tile([P, N], U8, name="w3s_raw", align_bytes=64)
         w2_raw = [
             keep.tile([P, PACK, H // 2], F32, name="w2_raw%d" % u, tag="w2_raw%d" % u, align_bytes=64) for u in range(2)
         ]
         ident = keep.tile([P, P], F32, name="ident")
 
-        nc.vector.memset(xs_raw[:].bitcast(I32), 0)
-        nc.gpsimd.memset(ws_raw[:].bitcast(I32), 0)
+        nc.gpsimd.memset(xs_raw[:].bitcast(I32), 0)
+        nc.gpsimd.memset(w1s_raw[:].bitcast(I32), 0)
+        nc.vector.memset(w3s_raw[:].bitcast(I32), 0)
 
         w2_rows = w2.rearrange("(p j) c -> p j c", j=PACK)
         nc.sync.dma_start(offs_sb[:], offs)
-        nc.sync.dma_start(out=w2_raw[0][:], in_=w2_rows[:, :, : H // 2])
-        load_scale_rows(nc.sync, xs_raw, x_scales[0])
         nc.sync.dma_start(out=w1w_raw[:].bitcast(I32), in_=w1_words[0].bitcast(I32))
-        nc.sync.dma_start(out=xw_raw[:], in_=x_words[0].rearrange("p n r -> p (n r)").bitcast(I32))
-        nc.sync.dma_start(out=w2_raw[1][:], in_=w2_rows[:, :, H // 2 :])
-        load_scale_rows(nc.sync, ws_raw[:, :H], w1_scales[0])
         nc.sync.dma_start(near_sb[:], near)
+        load_scale_rows(nc.sync, xs_raw, x_scales[0])
+        nc.sync.dma_start(out=xw_raw[:], in_=x_words[0].rearrange("p n r -> p (n r)").bitcast(I32))
+        load_scale_rows(nc.sync, w1s_raw, w1_scales[0])
+        nc.sync.dma_start(out=w2_raw[0][:], in_=w2_rows[:, :, : H // 2])
+        nc.sync.dma_start(out=w2_raw[1][:], in_=w2_rows[:, :, H // 2 :])
         nc.sync.dma_start(out=w3w_raw[:].bitcast(I32), in_=w3_words[0].bitcast(I32))
         nc.sync.dma_start(far_sb[:], far)
-        load_scale_rows(nc.gpsimd, ws_raw[:, H:], w3_scales[0])
+        load_scale_rows(nc.sync, w3s_raw, w3_scales[0])
         make_identity(nc, ident[:])
 
         w1w = keep.tile([P, 2 * H], U8, name="w1w", align_bytes=64)
-        w1s = keep.tile([P, H], U8, name="w1s", align_bytes=64)
         xq = keep.tile([P, S], U32, name="xq", align_bytes=64)
         xqs = keep.tile([P, S], U8, name="xqs", align_bytes=64)
         w2g = keep.tile([P, PACK, P, PACK], BF16, name="w2g", tag="w2g", align_bytes=64)
@@ -104,62 +105,74 @@ def tile_picked_scan2_none_po_kernel(
         w2_halves = [raw[:].rearrange("p j (m t) -> p m j t", t=PACK) for raw in w2_raw]
         nc.vector.tensor_copy(xqs[:], xs_raw[:].indirect(offs_sb[:]))
         deal_words(nc, w1w[:], w1w_raw[:])
-        nc.vector.tensor_copy(out=w2_dealt[:, : P // 2], in_=w2_halves[0])
         nc.vector.tensor_copy(xq[:], xw_raw[:].bitcast(U32).indirect(offs_sb[:]))
+        w1s = [
+            keep.tile([P, 2 * P], U8, name="w1s%d" % u, tag=("w1s0", "w2_raw1")[u], align_bytes=64) for u in range(2)
+        ]
+        w1s_planes = w1s_raw[:].rearrange("p (m t) -> p t m", t=PACK)
+        nc.vector.tensor_copy(out=w1s[0][:].rearrange("p (t m) -> p t m", t=2), in_=w1s_planes[:, :2])
+        nc.vector.tensor_copy(out=w2_dealt[:, : P // 2], in_=w2_halves[0])
         nc.vector.tensor_copy(out=w2_dealt[:, P // 2 :], in_=w2_halves[1])
-        deal_scales(nc, w1s[:], ws_raw[:, :H])
         for t in range(PACK):
             nc.vector.quantize_mx(
                 out=w2q[t][:].bitcast(FP8X4), scales=w2s[t][:], in_=w2g[:, t].rearrange("p m j -> p (m j)")
             )
+            if t == 0:
+                nc.vector.tensor_copy(out=w1s[1][:].rearrange("p (t m) -> p t m", t=2), in_=w1s_planes[:, 2:])
 
-        a = [keep.tile([P, S], F32, name="a%d" % t) for t in range(PACK)]
+        a_all = keep.tile([P, PACK, S], F32, name="a_all")
+        a = [a_all[:, t, :] for t in range(PACK)]
         b = [keep.tile([P, S], F32, name="b%d" % t) for t in range(PACK)]
         b2 = [keep.tile([P, S], F32, name="b2_%d" % t) for t in range(PACK)]
         near_term = [keep.tile([P, S], F32, name="near_term%d" % t) for t in range(PACK)]
-        a_near = keep.tile([P, PACK, S], F32, name="a_near")
-        logit_banks = []
+        a2 = keep.tile([P, PACK, S], F32, name="a2")
+        b2_late = keep.tile([P, PACK, HALF], F32, name="b2_late")
+
+        def product(bank, words, scales):
+            nc.tensor.matmul_mx(
+                out=bank[:], lhsT=words, lhsT_scale=scales, rhs=xq[:].bitcast(FP8X4), rhs_scale=xqs[:], start=True, stop=True
+            )
+
+        logit_banks = [psum.tile([P, S], F32, name="bank%d" % t) for t in range(PACK)]
+        b_banks = [psum.tile([P, S], F32, name="bank%d" % (PACK + t)) for t in range(PACK)]
+
+
+        def gate(t):
+            scales = w1s[t // 2][:, t % 2 * P : (t % 2 + 1) * P]
+            product(logit_banks[t], w1w[:, 2 * t * P : 2 * (t + 1) * P].bitcast(FP4X4), scales)
+            nc.scalar.activation(a[t], logit_banks[t][:], SIGMOID)
+
+        logit_tags = ("logit0", "w2q1", "w2q3", "w2s3")
+        logit = [keep.tile([P, S], F32, name="logit%d" % t, tag=logit_tags[t], align_bytes=64) for t in range(PACK)]
+        gate(0)
+        nc.scalar.copy(out=logit[0][:], in_=logit_banks[0][:])
         for t in range(PACK):
-            logit_bank = psum.tile([P, S], F32, name="bank%d" % t)
-            b_bank = psum.tile([P, S], F32, name="bank%d" % (PACK + t))
-            logit_banks.append(logit_bank)
-            nc.tensor.matmul_mx(
-                out=logit_bank[:],
-                lhsT=w1w[:, 2 * t * P : 2 * (t + 1) * P].bitcast(FP4X4),
-                lhsT_scale=w1s[:, t * P : (t + 1) * P],
-                rhs=xq[:].bitcast(FP8X4),
-                rhs_scale=xqs[:],
-                start=True,
-                stop=True,
-            )
-            nc.tensor.matmul_mx(
-                out=b_bank[:],
-                lhsT=w2q[t][:].bitcast(FP8X4),
-                lhsT_scale=w2s[t][:],
-                rhs=xq[:].bitcast(FP8X4),
-                rhs_scale=xqs[:],
-                start=True,
-                stop=True,
-            )
-            nc.scalar.activation(a[t][:], logit_bank[:], SIGMOID)
-            nc.scalar.copy(out=b[t][:], in_=b_bank[:])
+            if t + 1 < PACK:
+                gate(t + 1)
+            product(b_banks[t], w2q[t][:].bitcast(FP8X4), w2s[t][:])
+            nc.scalar.copy(out=b[t][:], in_=b_banks[t][:])
 
         w3w = keep.tile([P, 2 * N], U8, name="w3w", tag="w2g", align_bytes=64)
-        w3s = keep.tile([P, N], U8, name="w3s", tag="w2_raw1", align_bytes=64)
+        w3s = keep.tile([P, N], U8, name="w3s", tag="w2s0", align_bytes=64)
         deal_words(nc, w3w[:], w3w_raw[:])
-        deal_scales(nc, w3s[:], ws_raw[:, H:])
+        deal_scales(nc, w3s[:], w3s_raw[:])
 
-        logit_tags = ("w2q%d" % (PACK - 1), "w2s%d" % (PACK - 1), "logit2", "logit3")
-        logit = [keep.tile([P, S], F32, name="logit%d" % t, tag=logit_tags[t], align_bytes=64) for t in range(PACK)]
-        for t in range(PACK):
+        for t in range(1, PACK):
             nc.scalar.copy(out=logit[t][:], in_=logit_banks[t][:])
 
-        def look_up_a_near(lo, hi):
+        def look_up_a_near(c, tag):
+            a_near = keep.tile([P, PACK, CHUNK], F32, name="a_near%d" % c, tag=tag, align_bytes=64)
             for t in range(PACK):
-                nc.scalar.activation(a_near[:, t, lo:hi], logit[t][:].indirect(entries(near_sb, lo, hi)), SIGMOID)
+                nc.scalar.activation(
+                    a_near[:, t, :], logit[t][:].indirect(entries(near_sb, c * CHUNK, (c + 1) * CHUNK)), SIGMOID
+                )
+            return a_near
 
-        look_up_a_near(0, HALF)
-        look_up_a_near(HALF, S - CHUNK)
+        a_near = [look_up_a_near(c, "a_near%d" % c) for c in range(CHUNKS - 1)]
+
+        def decay(c):
+            cols = slice(c * CHUNK, (c + 1) * CHUNK)
+            nc.vector.tensor_tensor(a2[:, :, cols], a_all[:, :, cols], a_near[c][:], MULT)
 
         for t in range(PACK + 1):
             if t < PACK:
@@ -170,8 +183,12 @@ def tile_picked_scan2_none_po_kernel(
                         a[t][:, lo : lo + HALF],
                         MULT,
                     )
+            else:
+                decay(0)
             if t > 0:
                 nc.vector.tensor_tensor(b2[t - 1][:], b[t - 1][:], near_term[t - 1][:], ADD)
+                nc.sync.dma_start(out=b2_late[:, t - 1, :], in_=b2[t - 1][:, HALF:])
+        decay(1)
 
         yq = keep.tile([P, S], U32, name="yq", align_bytes=64)
         ys = keep.tile([P, S], U8, name="ys", align_bytes=64)
@@ -180,24 +197,16 @@ def tile_picked_scan2_none_po_kernel(
 
         def look_up_far(c, tag):
             lo, hi = c * CHUNK, (c + 1) * CHUNK
-            gated = keep.tile([P, PACK, CHUNK], F32, name="gated%d" % c, tag=tag, align_bytes=64)
+            far_term = keep.tile([P, PACK, CHUNK], F32, name="far_term%d" % c, tag=tag, align_bytes=64)
             for t in range(PACK):
                 nc.vector.tensor_tensor(
-                    gated[:, t, :], b2[t][:].indirect(entries(far_sb, lo, hi)), a[t][:, lo:hi], MULT
-                )
-            return gated
-
-        def times_a_near(c, gated, tag):
-            far_term = keep.tile([P, PACK, CHUNK], F32, name="far_term%d" % c, tag=tag, align_bytes=64)
-            for pair in (slice(0, 2), slice(2, 4)):
-                nc.vector.tensor_tensor(
-                    far_term[:, pair], gated[:, pair], a_near[:, pair, c * CHUNK : (c + 1) * CHUNK], MULT
+                    far_term[:, t, :], b2[t][:].indirect(entries(far_sb, lo, hi)), a2[:, t, lo:hi], MULT
                 )
             return far_term
 
         def add_on_tensor(c, far_term):
             lo, hi = c * CHUNK, (c + 1) * CHUNK
-            z_turned = psum.tile([P, PACK, P], F32, name="bank%d" % (2 + c))
+            z_turned = psum.tile([P, PACK, P], F32, name="bank%d" % c)
             for t in range(PACK):
                 nc.tensor.matmul(
                     z_turned[:, t, :], lhsT=b2[t][:, lo:hi], rhs=ident[:], start=True, stop=False, is_transpose=True
@@ -208,7 +217,7 @@ def tile_picked_scan2_none_po_kernel(
             rounded = ring.tile([P, 2, P, 2], BF16, name="rounded", align_bytes=64)
             nc.scalar.copy(out=rounded[:], in_=z_turned[:].rearrange("n (u e) p -> n u p e", e=2))
             pairs = rounded[:].rearrange("n u p e -> n (u p e)").bitcast(F32)
-            pairs_back = psum.tile([P, 2, CHUNK], F32, name="bank%d" % (6 + c))
+            pairs_back = psum.tile([P, 2, CHUNK], F32, name="bank%d" % (2 + c))
             for u in range(2):
                 nc.tensor.transpose(pairs_back[:, u, :], pairs[:, u * P : (u + 1) * P], ident[:])
             zg = keep.tile([P, CHUNK, PACK], BF16, name="zg%d" % c, tag="zg%d" % c, align_bytes=64)
@@ -219,14 +228,13 @@ def tile_picked_scan2_none_po_kernel(
             return zg
 
         def add_on_vector(c, far_term):
-            lo, hi = c * CHUNK, (c + 1) * CHUNK
-            z = keep.tile([P, PACK, CHUNK], F32, name="z%d" % c, align_bytes=64)
-            for t in range(PACK):
-                nc.vector.tensor_tensor(z[:, t, :], b2[t][:, lo:hi], far_term[:, t, :], ADD)
+            lo = c * CHUNK - HALF
             zg = keep.tile([P, CHUNK, PACK], BF16, name="zg%d" % c, align_bytes=64)
-            nc.vector.tensor_copy(
-                out=zg[:].rearrange("p (n i) t -> p n t i", i=LINE),
-                in_=z[:].rearrange("p t (n i) -> p n t i", i=LINE),
+            nc.vector.tensor_tensor(
+                zg[:].rearrange("p (n i) t -> p n t i", i=LINE),
+                b2_late[:, :, lo : lo + CHUNK].rearrange("p t (n i) -> p n t i", i=LINE),
+                far_term[:].rearrange("p t (n i) -> p n t i", i=LINE),
+                ADD,
             )
             return zg
 
@@ -264,15 +272,18 @@ def tile_picked_scan2_none_po_kernel(
             nc.sync.dma_start(out=out_rows[:, :, lo:hi], in_=y[:])
             return yg
 
-        zg0 = add_on_tensor(0, times_a_near(0, look_up_far(0, "gated"), "far_term0"))
-        look_up_a_near(S - CHUNK, S)
-        zg1 = add_on_tensor(1, times_a_near(1, look_up_far(1, "gated"), "far_term1"))
-        zg2 = add_on_vector(2, times_a_near(2, look_up_far(2, "gated"), "far_term2"))
+        zg0 = add_on_tensor(0, look_up_far(0, "far_term0"))
+        a_near.append(look_up_a_near(CHUNKS - 1, "far_term0"))
+        zg1 = add_on_tensor(1, look_up_far(1, "far_term1"))
+        decay(2)
+        far2 = look_up_far(2, "far_term2")
         yg0 = project(0, zg0)
-        yg2 = project(2, zg2)
-        gated3 = look_up_far(3, "zg0")
+        zg2 = add_on_vector(2, far2)
+        decay(3)
         yg1 = project(1, zg1)
-        yg3 = project(3, add_on_vector(3, times_a_near(3, gated3, "zg1")))
+        yg2 = project(2, zg2)
+        far3 = look_up_far(3, "zg0")
+        yg3 = project(3, add_on_vector(3, far3))
 
         for c, yg in enumerate((yg0, yg1, yg2, yg3)):
             cols = slice(c * CHUNK, (c + 1) * CHUNK)

@@ -168,7 +168,7 @@ def tile_picked_scan2_none_po_kernel(
                 )
             return a_near
 
-        a_near = [look_up_a_near(c, "a_near%d" % c) for c in range(CHUNKS - 1)]
+        a_near = [look_up_a_near(c, "a_near%d" % c) for c in range(CHUNKS)]
 
         def decay(c):
             cols = slice(c * CHUNK, (c + 1) * CHUNK)
@@ -227,9 +227,9 @@ def tile_picked_scan2_none_po_kernel(
             )
             return zg
 
-        def add_on_vector(c, far_term):
+        def add_on_vector(c, far_term, tag):
             lo = c * CHUNK - HALF
-            zg = keep.tile([P, CHUNK, PACK], BF16, name="zg%d" % c, align_bytes=64)
+            zg = keep.tile([P, CHUNK, PACK], BF16, name="zg%d" % c, tag=tag, align_bytes=64)
             nc.vector.tensor_tensor(
                 zg[:].rearrange("p (n i) t -> p n t i", i=LINE),
                 b2_late[:, :, lo : lo + CHUNK].rearrange("p t (n i) -> p n t i", i=LINE),
@@ -237,6 +237,12 @@ def tile_picked_scan2_none_po_kernel(
                 ADD,
             )
             return zg
+
+        def quantise_result(c, yg):
+            cols = slice(c * CHUNK, (c + 1) * CHUNK)
+            nc.vector.quantize_mx(
+                out=yq[:, cols].bitcast(FP8X4), scales=ys[:, cols], in_=yg[:].rearrange("p n t -> p (n t)")
+            )
 
         def project(c, zg):
             lo, hi = c * CHUNK, (c + 1) * CHUNK
@@ -260,38 +266,35 @@ def tile_picked_scan2_none_po_kernel(
                     stop=True,
                 )
             if last:
+                nc.vector.tensor_copy(out=yg[:, :, :planes], in_=banks[0][:].rearrange("p t n -> p n t"))
+                nc.scalar.copy(out=yg[:, :, planes:], in_=banks[1][:].rearrange("p t n -> p n t"))
+                quantise_result(c, yg)
                 nc.scalar.copy(out=y[:, :planes], in_=banks[0][:])
                 nc.sync.dma_start(out=out_rows[:, :planes, lo:hi], in_=y[:, :planes])
-                nc.vector.tensor_copy(out=yg[:, :, planes:], in_=banks[1][:].rearrange("p t n -> p n t"))
-                nc.vector.tensor_copy(out=yg[:, :, :planes], in_=banks[0][:].rearrange("p t n -> p n t"))
-                nc.scalar.copy(out=y[:, planes:], in_=banks[1][:])
+                nc.vector.tensor_copy(out=y[:, planes:], in_=banks[1][:])
                 nc.sync.dma_start(out=out_rows[:, planes:, lo:hi], in_=y[:, planes:])
-                return yg
+                return
             nc.scalar.copy(out=yg[:], in_=banks[0][:].rearrange("p t n -> p n t"))
             nc.scalar.copy(out=y[:], in_=banks[0][:])
             nc.sync.dma_start(out=out_rows[:, :, lo:hi], in_=y[:])
             return yg
 
         zg0 = add_on_tensor(0, look_up_far(0, "far_term0"))
-        a_near.append(look_up_a_near(CHUNKS - 1, "far_term0"))
         zg1 = add_on_tensor(1, look_up_far(1, "far_term1"))
         decay(2)
         far2 = look_up_far(2, "far_term2")
         yg0 = project(0, zg0)
-        zg2 = add_on_vector(2, far2)
         decay(3)
+        zg2 = add_on_vector(2, far2, "zg0")
         yg1 = project(1, zg1)
         yg2 = project(2, zg2)
-        far3 = look_up_far(3, "zg0")
-        yg3 = project(3, add_on_vector(3, far3))
-
-        for c, yg in enumerate((yg0, yg1, yg2, yg3)):
-            cols = slice(c * CHUNK, (c + 1) * CHUNK)
-            nc.vector.quantize_mx(
-                out=yq[:, cols].bitcast(FP8X4), scales=ys[:, cols], in_=yg[:].rearrange("p n t -> p (n t)")
-            )
-        nc.sync.dma_start(out=out_words[:, : S - CHUNK], in_=yq[:, : S - CHUNK].bitcast(I32))
-        nc.sync.dma_start(out=out_words[:, S - CHUNK :], in_=yq[:, S - CHUNK :].bitcast(I32))
+        far3 = look_up_far(3, "zg1")
+        zg3 = add_on_vector(3, far3, "zg3")
+        project(3, zg3)
+        for c, yg in enumerate((yg0, yg1, yg2)):
+            quantise_result(c, yg)
+        nc.sync.dma_start(out=out_words[:, :HALF], in_=yq[:, :HALF].bitcast(I32))
+        nc.sync.dma_start(out=out_words[:, HALF:], in_=yq[:, HALF:].bitcast(I32))
         for q in range(4):
             queue = nc.scalar if q % 2 else nc.sync
             queue.dma_start(

@@ -24,7 +24,7 @@ LIST_ROWS = 16
 HALF = S // 2
 CHUNK = 128
 CHUNKS = S // CHUNK
-LINE = 4
+LINE = 2
 OUT_BANKS = (4, 5, 6, 7, 0)
 
 
@@ -172,7 +172,8 @@ def tile_picked_scan2_none_po_kernel(
 
         def decay(c):
             cols = slice(c * CHUNK, (c + 1) * CHUNK)
-            nc.vector.tensor_tensor(a2[:, :, cols], a_all[:, :, cols], a_near[c][:], MULT)
+            for pair in (slice(0, 2), slice(2, 4)) if c == 2 else (slice(0, 4),):
+                nc.vector.tensor_tensor(a2[:, pair, cols], a_all[:, pair, cols], a_near[c][:, pair], MULT)
 
         for t in range(PACK + 1):
             if t < PACK:
@@ -238,10 +239,13 @@ def tile_picked_scan2_none_po_kernel(
             )
             return zg
 
-        def quantise_result(c, yg):
-            cols = slice(c * CHUNK, (c + 1) * CHUNK)
+        yg_all = keep.tile([P, S, PACK], BF16, name="yg_all", align_bytes=64)
+
+        def quantise_result(lo, hi):
             nc.vector.quantize_mx(
-                out=yq[:, cols].bitcast(FP8X4), scales=ys[:, cols], in_=yg[:].rearrange("p n t -> p (n t)")
+                out=yq[:, lo:hi].bitcast(FP8X4),
+                scales=ys[:, lo:hi],
+                in_=yg_all[:, lo:hi, :].rearrange("p n t -> p (n t)"),
             )
 
         def project(c, zg):
@@ -250,7 +254,7 @@ def tile_picked_scan2_none_po_kernel(
             zs = keep.tile([P, CHUNK], U8, name="zs%d" % c, align_bytes=64)
             nc.vector.quantize_mx(out=zq[:].bitcast(FP8X4), scales=zs[:], in_=zg[:].rearrange("p n t -> p (n t)"))
             y = keep.tile([P, PACK, CHUNK], F32, name="y%d" % c)
-            yg = keep.tile([P, CHUNK, PACK], BF16, name="yg%d" % c, align_bytes=64)
+            yg = yg_all[:, lo:hi, :]
             last = c == CHUNKS - 1
             parts = 2 if last else 1
             planes = PACK // parts
@@ -267,33 +271,32 @@ def tile_picked_scan2_none_po_kernel(
                 )
             if last:
                 nc.vector.tensor_copy(out=yg[:, :, :planes], in_=banks[0][:].rearrange("p t n -> p n t"))
-                nc.scalar.copy(out=yg[:, :, planes:], in_=banks[1][:].rearrange("p t n -> p n t"))
-                quantise_result(c, yg)
-                nc.scalar.copy(out=y[:, :planes], in_=banks[0][:])
+                nc.vector.tensor_copy(out=y[:, :planes], in_=banks[0][:])
                 nc.sync.dma_start(out=out_rows[:, :planes, lo:hi], in_=y[:, :planes])
-                nc.vector.tensor_copy(out=y[:, planes:], in_=banks[1][:])
+                nc.scalar.copy(out=yg[:, :, planes:], in_=banks[1][:].rearrange("p t n -> p n t"))
+                nc.scalar.copy(out=y[:, planes:], in_=banks[1][:])
                 nc.sync.dma_start(out=out_rows[:, planes:, lo:hi], in_=y[:, planes:])
+                quantise_result(lo, hi)
                 return
-            nc.scalar.copy(out=yg[:], in_=banks[0][:].rearrange("p t n -> p n t"))
+            nc.scalar.copy(out=yg, in_=banks[0][:].rearrange("p t n -> p n t"))
             nc.scalar.copy(out=y[:], in_=banks[0][:])
             nc.sync.dma_start(out=out_rows[:, :, lo:hi], in_=y[:])
-            return yg
 
         zg0 = add_on_tensor(0, look_up_far(0, "far_term0"))
         zg1 = add_on_tensor(1, look_up_far(1, "far_term1"))
         decay(2)
         far2 = look_up_far(2, "far_term2")
-        yg0 = project(0, zg0)
+        project(0, zg0)
         decay(3)
         zg2 = add_on_vector(2, far2, "zg0")
-        yg1 = project(1, zg1)
-        yg2 = project(2, zg2)
+        project(1, zg1)
+        project(2, zg2)
         far3 = look_up_far(3, "zg1")
+        quantise_result(0, HALF)
+        nc.sync.dma_start(out=out_words[:, :HALF], in_=yq[:, :HALF].bitcast(I32))
         zg3 = add_on_vector(3, far3, "zg3")
         project(3, zg3)
-        for c, yg in enumerate((yg0, yg1, yg2)):
-            quantise_result(c, yg)
-        nc.sync.dma_start(out=out_words[:, :HALF], in_=yq[:, :HALF].bitcast(I32))
+        quantise_result(HALF, HALF + CHUNK)
         nc.sync.dma_start(out=out_words[:, HALF:], in_=yq[:, HALF:].bitcast(I32))
         for q in range(4):
             queue = nc.scalar if q % 2 else nc.sync

@@ -122,10 +122,9 @@ def tile_picked_scan2_none_po_kernel(
 
         a_all = keep.tile([P, PACK, S], F32, name="a_all")
         a = [a_all[:, t, :] for t in range(PACK)]
-        b = [keep.tile([P, S], F32, name="b%d" % t) for t in range(PACK)]
-        b2 = [keep.tile([P, S], F32, name="b2_%d" % t) for t in range(PACK)]
-        near_term = [keep.tile([P, S], F32, name="near_term%d" % t) for t in range(PACK)]
-        a2 = keep.tile([P, PACK, S], F32, name="a2")
+        b = [keep.tile([P, S], F32, name="b%d" % t, tag="b%d" % t) for t in range(PACK)]
+        near_term = [keep.tile([P, S], F32, name="near_term%d" % t, tag="near_term%d" % t) for t in range(PACK)]
+        a2_late = keep.tile([P, PACK, S], F32, name="a2_late")
         b2_late = keep.tile([P, PACK, HALF], F32, name="b2_late")
 
         def product(bank, words, scales):
@@ -137,10 +136,10 @@ def tile_picked_scan2_none_po_kernel(
         b_banks = [psum.tile([P, S], F32, name="bank%d" % (PACK + t)) for t in range(PACK)]
 
 
-        def gate(t):
+        def gate(t, cols=slice(0, S)):
             scales = w1s[t // 2][:, t % 2 * P : (t % 2 + 1) * P]
             product(logit_banks[t], w1w[:, 2 * t * P : 2 * (t + 1) * P].bitcast(FP4X4), scales)
-            nc.scalar.activation(a[t], logit_banks[t][:], SIGMOID)
+            nc.scalar.activation(a[t][:, cols], logit_banks[t][:, cols], SIGMOID)
 
         logit_tags = ("logit0", "w2q1", "w2q3", "w2s3")
         logit = [keep.tile([P, S], F32, name="logit%d" % t, tag=logit_tags[t], align_bytes=64) for t in range(PACK)]
@@ -148,62 +147,70 @@ def tile_picked_scan2_none_po_kernel(
         nc.scalar.copy(out=logit[0][:], in_=logit_banks[0][:])
         for t in range(PACK):
             if t + 1 < PACK:
-                gate(t + 1)
+                gate(t + 1, slice(0, HALF if t + 1 == 2 else S))
             product(b_banks[t], w2q[t][:].bitcast(FP8X4), w2s[t][:])
             nc.scalar.copy(out=b[t][:], in_=b_banks[t][:])
+        nc.scalar.activation(a[2][:, HALF:], logit_banks[2][:, HALF:], SIGMOID)
 
         w3w = keep.tile([P, 2 * N], U8, name="w3w", tag="w2g", align_bytes=64)
         w3s = keep.tile([P, N], U8, name="w3s", tag="w2s0", align_bytes=64)
         deal_words(nc, w3w[:], w3w_raw[:])
         deal_scales(nc, w3s[:], w3s_raw[:])
 
-        for t in range(1, PACK):
+        a_near = keep.tile([P, PACK, S], F32, name="a_near")
+
+        def look_up_a_near(t, lo, hi):
+            nc.scalar.activation(a_near[:, t, lo:hi], logit[t][:].indirect(entries(near_sb, lo, hi)), SIGMOID)
+
+        look_up_a_near(0, 0, HALF)
+        look_up_a_near(0, HALF, S)
+        nc.scalar.copy(out=logit[1][:], in_=logit_banks[1][:])
+        look_up_a_near(1, 0, HALF)
+        for t in range(2, PACK):
             nc.scalar.copy(out=logit[t][:], in_=logit_banks[t][:])
+        for c in range(CHUNKS):
+            for t in range(2 if c < 2 else 1, PACK):
+                look_up_a_near(t, c * CHUNK, (c + 1) * CHUNK)
 
-        def look_up_a_near(c, tag):
-            a_near = keep.tile([P, PACK, CHUNK], F32, name="a_near%d" % c, tag=tag, align_bytes=64)
-            for t in range(PACK):
-                nc.scalar.activation(
-                    a_near[:, t, :], logit[t][:].indirect(entries(near_sb, c * CHUNK, (c + 1) * CHUNK)), SIGMOID
-                )
-            return a_near
+        for t, lo in ((0, 0), (0, HALF), (1, 0), (1, HALF), (2, 0), (3, 0), (3, HALF), (2, HALF)):
+            nc.vector.tensor_tensor(
+                near_term[t][:, lo : lo + HALF],
+                b[t][:].indirect(entries(near_sb, lo, lo + HALF)),
+                a[t][:, lo : lo + HALF],
+                MULT,
+            )
+        a2_early = keep.tile([P, S + HALF], F32, name="a2_early", tag="b2")
+        nc.gpsimd.tensor_tensor(a2_early[:, :S], a[0], a_near[:, 0, :], MULT)
+        nc.gpsimd.tensor_tensor(a2_early[:, S:], a[1][:, :HALF], a_near[:, 1, :HALF], MULT)
+        b2_tags = ("b3", "near_term0", "b2_2", "b2_3")
+        b2 = [keep.tile([P, S], F32, name="b2_%d" % t, tag=b2_tags[t]) for t in range(PACK)]
+        for t in (0, 3, 1, 2):
+            nc.vector.tensor_tensor(b2[t][:], b_banks[t][:], near_term[t][:], ADD)
+            nc.sync.dma_start(out=b2_late[:, t, :], in_=b2[t][:, HALF:])
 
-        a_near = [look_up_a_near(c, "a_near%d" % c) for c in range(CHUNKS)]
+        def a2(t, lo, hi):
+            early = t * S + hi <= S + HALF
+            return a2_early[:, t * S + lo : t * S + hi] if early else a2_late[:, t, lo:hi]
 
         def decay(c):
             cols = slice(c * CHUNK, (c + 1) * CHUNK)
-            for pair in (slice(0, 2), slice(2, 4)) if c == 2 else (slice(0, 4),):
-                nc.vector.tensor_tensor(a2[:, pair, cols], a_all[:, pair, cols], a_near[c][:, pair], MULT)
-
-        for t in range(PACK + 1):
-            if t < PACK:
-                for lo in range(0, S, HALF):
-                    nc.vector.tensor_tensor(
-                        near_term[t][:, lo : lo + HALF],
-                        b[t][:].indirect(entries(near_sb, lo, lo + HALF)),
-                        a[t][:, lo : lo + HALF],
-                        MULT,
-                    )
-            else:
-                decay(0)
-            if t > 0:
-                nc.vector.tensor_tensor(b2[t - 1][:], b[t - 1][:], near_term[t - 1][:], ADD)
-                nc.sync.dma_start(out=b2_late[:, t - 1, :], in_=b2[t - 1][:, HALF:])
-        decay(1)
+            planes = slice(2 if c < 2 else 1, PACK)
+            nc.vector.tensor_tensor(a2_late[:, planes, cols], a_all[:, planes, cols], a_near[:, planes, cols], MULT)
 
         yq = keep.tile([P, S], U32, name="yq", align_bytes=64)
         ys = keep.tile([P, S], U8, name="ys", align_bytes=64)
         out_rows = out_0.rearrange("(p t) j -> p t j", t=PACK)
         out_words = out_1[0].rearrange("p n r -> p (n r)").bitcast(I32)
 
-        def look_up_far(c, tag):
+        def look_up_far(c, far_term, planes):
             lo, hi = c * CHUNK, (c + 1) * CHUNK
-            far_term = keep.tile([P, PACK, CHUNK], F32, name="far_term%d" % c, tag=tag, align_bytes=64)
-            for t in range(PACK):
+            for t in planes:
                 nc.vector.tensor_tensor(
-                    far_term[:, t, :], b2[t][:].indirect(entries(far_sb, lo, hi)), a2[:, t, lo:hi], MULT
+                    far_term[:, t, :], b2[t][:].indirect(entries(far_sb, lo, hi)), a2(t, lo, hi), MULT
                 )
-            return far_term
+
+        def far_tile(c, tag):
+            return keep.tile([P, PACK, CHUNK], F32, name="far_term%d" % c, tag=tag, align_bytes=64)
 
         def add_on_tensor(c, far_term):
             lo, hi = c * CHUNK, (c + 1) * CHUNK
@@ -282,16 +289,24 @@ def tile_picked_scan2_none_po_kernel(
             nc.scalar.copy(out=y[:], in_=banks[0][:])
             nc.sync.dma_start(out=out_rows[:, :, lo:hi], in_=y[:])
 
-        zg0 = add_on_tensor(0, look_up_far(0, "far_term0"))
-        zg1 = add_on_tensor(1, look_up_far(1, "far_term1"))
+        far0, far1, far2 = [far_tile(c, "far_term%d" % c) for c in range(3)]
+        look_up_far(0, far0, (0,))
+        look_up_far(1, far1, (0,))
+        decay(0)
+        look_up_far(0, far0, (1, 2, 3))
+        zg0 = add_on_tensor(0, far0)
+        decay(1)
+        look_up_far(1, far1, (1, 2, 3))
+        zg1 = add_on_tensor(1, far1)
         decay(2)
-        far2 = look_up_far(2, "far_term2")
+        look_up_far(2, far2, range(PACK))
         project(0, zg0)
         decay(3)
         zg2 = add_on_vector(2, far2, "zg0")
         project(1, zg1)
         project(2, zg2)
-        far3 = look_up_far(3, "zg1")
+        far3 = far_tile(3, "zg1")
+        look_up_far(3, far3, range(PACK))
         quantise_result(0, HALF)
         nc.sync.dma_start(out=out_words[:, :HALF], in_=yq[:, :HALF].bitcast(I32))
         zg3 = add_on_vector(3, far3, "zg3")

@@ -25,7 +25,6 @@ HALF = S // 2
 CHUNK = 128
 CHUNKS = S // CHUNK
 LINE = 2
-OUT_BANKS = (4, 5, 6, 7, 0)
 
 
 def load_scale_rows(queue, scale_tile, rows, quadrants=(0, 2, 1, 3)):
@@ -62,19 +61,23 @@ def tile_picked_scan2_none_po_kernel(
         ring = ctx.enter_context(tc.tile_pool(name="ring", bufs=2))
         psum = ctx.enter_context(tc.psum_pool(name="psum", bufs=1))
 
+        def tile(shape, dtype, name, tag=None):
+            return keep.tile(shape, dtype, name=name, tag=tag or name, align_bytes=64)
+
+        def bank(i, shape):
+            return psum.tile(shape, F32, name="bank%d" % i)
+
         offs_sb = keep.tile([P, S // LIST_ROWS], U16, name="offs_sb")
         near_sb = keep.tile([P, S // LIST_ROWS], U16, name="near_sb")
         far_sb = keep.tile([P, S // LIST_ROWS], U16, name="far_sb")
-        xw_raw = keep.tile([P, T], I32, name="xw_raw", tag="xw_raw", align_bytes=64)
-        xs_raw = keep.tile([P, T], U8, name="xs_raw", align_bytes=64)
-        w1w_raw = keep.tile([P, 2 * H], U8, name="w1w_raw", align_bytes=64)
-        w3w_raw = keep.tile([P, 2 * N], U8, name="w3w_raw", align_bytes=64)
-        w1s_raw = keep.tile([P, H], U8, name="w1s_raw", align_bytes=64)
-        w3s_raw = keep.tile([P, N], U8, name="w3s_raw", align_bytes=64)
-        w2_raw = [
-            keep.tile([P, PACK, H // 2], F32, name="w2_raw%d" % u, tag="w2_raw%d" % u, align_bytes=64) for u in range(2)
-        ]
-        ident = keep.tile([P, P], F32, name="ident")
+        xw_raw = tile([P, T], I32, "xw_raw")
+        xs_raw = tile([P, T], U8, "xs_raw")
+        w1w_raw = tile([P, 2 * H], U8, "w1w_raw")
+        w3w_raw = tile([P, 2 * N], U8, "w3w_raw")
+        w1s_raw = tile([P, H], U8, "w1s_raw")
+        w3s_raw = tile([P, N], U8, "w3s_raw")
+        w2_raw = [tile([P, PACK, H // 2], F32, "w2_raw%d" % u) for u in range(2)]
+        ident = tile([P, P], F32, "ident")
 
         nc.gpsimd.memset(xs_raw[:].bitcast(I32), 0)
         nc.gpsimd.memset(w1s_raw[:].bitcast(I32), 0)
@@ -94,70 +97,94 @@ def tile_picked_scan2_none_po_kernel(
         load_scale_rows(nc.sync, w3s_raw, w3_scales[0])
         make_identity(nc, ident[:])
 
-        w1w = keep.tile([P, 2 * H], U8, name="w1w", align_bytes=64)
-        xq = keep.tile([P, S], U32, name="xq", align_bytes=64)
-        xqs = keep.tile([P, S], U8, name="xqs", align_bytes=64)
-        w2g = keep.tile([P, PACK, P, PACK], BF16, name="w2g", tag="w2g", align_bytes=64)
-        w2q = [keep.tile([P, P], U32, name="w2q%d" % t, tag="w2q%d" % t, align_bytes=64) for t in range(PACK)]
-        w2s = [keep.tile([P, P], U8, name="w2s%d" % t, tag="w2s%d" % t, align_bytes=64) for t in range(PACK)]
+        halves = (slice(0, HALF), slice(HALF, S))
+        whole = slice(0, S)
 
+        w1w = [tile([P, H], U8, "w1w%d" % u, (None, "w2_raw1")[u]) for u in range(2)]
+        w1w_planes = w1w_raw[:].rearrange("p (m t e) -> p t m e", t=PACK, e=2)
+        w1s = tile([P, H], U8, "w1s")
+        xqs = tile([P, S], U8, "xqs")
+        nc.vector.tensor_copy(out=w1w[0][:].rearrange("p (t m e) -> p t m e", t=2, e=2), in_=w1w_planes[:, :2])
+        nc.vector.tensor_copy(xqs[:], xs_raw[:].indirect(offs_sb[:]))
+        xq = [tile([P, HALF], U32, "xq0")]
+        nc.vector.tensor_copy(xq[0][:], xw_raw[:].bitcast(U32).indirect(entries(offs_sb, 0, HALF)))
+        deal_scales(nc, w1s[:], w1s_raw[:])
+        xq.append(tile([P, HALF], U32, "xq1", "w1s_raw"))
+        nc.vector.tensor_copy(xq[1][:], xw_raw[:].bitcast(U32).indirect(entries(offs_sb, HALF, S)))
+
+        w2g = tile([P, PACK, P, PACK], BF16, "w2g")
+        w2q = [tile([P, P], U32, "w2q%d" % t) for t in range(PACK)]
+        w2s = [tile([P, P], U8, "w2s%d" % t) for t in range(PACK)]
         w2_dealt = w2g[:].rearrange("p t m j -> p m j t")
         w2_halves = [raw[:].rearrange("p j (m t) -> p m j t", t=PACK) for raw in w2_raw]
-        nc.vector.tensor_copy(xqs[:], xs_raw[:].indirect(offs_sb[:]))
-        deal_words(nc, w1w[:], w1w_raw[:])
-        nc.vector.tensor_copy(xq[:], xw_raw[:].bitcast(U32).indirect(offs_sb[:]))
-        w1s = [
-            keep.tile([P, 2 * P], U8, name="w1s%d" % u, tag=("w1s0", "w2_raw1")[u], align_bytes=64) for u in range(2)
-        ]
-        w1s_planes = w1s_raw[:].rearrange("p (m t) -> p t m", t=PACK)
-        nc.vector.tensor_copy(out=w1s[0][:].rearrange("p (t m) -> p t m", t=2), in_=w1s_planes[:, :2])
         nc.vector.tensor_copy(out=w2_dealt[:, : P // 2], in_=w2_halves[0])
-        nc.vector.tensor_copy(out=w2_dealt[:, P // 2 :], in_=w2_halves[1])
+        for pair in (slice(0, 2), slice(2, 4)):
+            nc.vector.tensor_copy(out=w2_dealt[:, P // 2 :, :, pair], in_=w2_halves[1][:, :, :, pair])
         for t in range(PACK):
             nc.vector.quantize_mx(
                 out=w2q[t][:].bitcast(FP8X4), scales=w2s[t][:], in_=w2g[:, t].rearrange("p m j -> p (m j)")
             )
-            if t == 0:
-                nc.vector.tensor_copy(out=w1s[1][:].rearrange("p (t m) -> p t m", t=2), in_=w1s_planes[:, 2:])
-
-        a_all = keep.tile([P, PACK, S], F32, name="a_all")
-        a = [a_all[:, t, :] for t in range(PACK)]
-        b = [keep.tile([P, S], F32, name="b%d" % t, tag="b%d" % t) for t in range(PACK)]
-        near_term = [keep.tile([P, S], F32, name="near_term%d" % t, tag="near_term%d" % t) for t in range(PACK)]
-        a2_late = keep.tile([P, PACK, S], F32, name="a2_late")
-        b2_late = keep.tile([P, PACK, HALF], F32, name="b2_late")
-
-        def product(bank, words, scales):
-            nc.tensor.matmul_mx(
-                out=bank[:], lhsT=words, lhsT_scale=scales, rhs=xq[:].bitcast(FP8X4), rhs_scale=xqs[:], start=True, stop=True
-            )
-
-        logit_banks = [psum.tile([P, S], F32, name="bank%d" % t) for t in range(PACK)]
-        b_banks = [psum.tile([P, S], F32, name="bank%d" % (PACK + t)) for t in range(PACK)]
-
-
-        def gate(t, cols=slice(0, S)):
-            scales = w1s[t // 2][:, t % 2 * P : (t % 2 + 1) * P]
-            product(logit_banks[t], w1w[:, 2 * t * P : 2 * (t + 1) * P].bitcast(FP4X4), scales)
-            nc.scalar.activation(a[t][:, cols], logit_banks[t][:, cols], SIGMOID)
-
-        logit_tags = ("logit0", "w2q1", "w2q3", "w2s3")
-        logit = [keep.tile([P, S], F32, name="logit%d" % t, tag=logit_tags[t], align_bytes=64) for t in range(PACK)]
-        gate(0)
-        nc.scalar.copy(out=logit[0][:], in_=logit_banks[0][:])
-        for t in range(PACK):
-            if t + 1 < PACK:
-                gate(t + 1, slice(0, HALF if t + 1 == 2 else S))
-            product(b_banks[t], w2q[t][:].bitcast(FP8X4), w2s[t][:])
-            nc.scalar.copy(out=b[t][:], in_=b_banks[t][:])
-        nc.scalar.activation(a[2][:, HALF:], logit_banks[2][:, HALF:], SIGMOID)
-
-        w3w = keep.tile([P, 2 * N], U8, name="w3w", tag="w2g", align_bytes=64)
-        w3s = keep.tile([P, N], U8, name="w3s", tag="w2s0", align_bytes=64)
+            if t == 1:
+                nc.vector.tensor_copy(out=w1w[1][:].rearrange("p (t m e) -> p t m e", t=2, e=2), in_=w1w_planes[:, 2:])
+        w3w = tile([P, 2 * N], U8, "w3w", "w2g")
+        w3s = tile([P, N], U8, "w3s", "w2s0")
         deal_words(nc, w3w[:], w3w_raw[:])
         deal_scales(nc, w3s[:], w3s_raw[:])
 
-        a_near = keep.tile([P, PACK, S], F32, name="a_near")
+        def product(out, words, scales, u):
+            nc.tensor.matmul_mx(
+                out=out,
+                lhsT=words,
+                lhsT_scale=scales,
+                rhs=xq[u][:].bitcast(FP8X4),
+                rhs_scale=xqs[:, halves[u]],
+                start=True,
+                stop=True,
+            )
+
+        def gate_product(t, out, u):
+            product(out, w1w[t // 2][:, t % 2 * 2 * P : (t % 2 + 1) * 2 * P].bitcast(FP4X4), w1s[:, t * P : (t + 1) * P], u)
+
+        def b_product(t, out, u):
+            product(out, w2q[t][:].bitcast(FP8X4), w2s[t][:], u)
+
+        a0 = tile([P, S], F32, "a0")
+        a_low = tile([P, PACK - 1, HALF], F32, "a_low")
+        b = [tile([P, S], F32, "b%d" % t) for t in range(PACK)]
+        logit = [tile([P, S], F32, "logit%d" % t, (None, "w2s1", "w2s3", "xqs")[t]) for t in range(PACK)]
+
+        for u in range(2):
+            half_bank = bank(u, [P, HALF])
+            gate_product(0, half_bank[:], u)
+            nc.scalar.activation(a0[:, halves[u]], half_bank[:], SIGMOID)
+            nc.scalar.copy(out=logit[0][:, halves[u]], in_=half_bank[:])
+        logit_banks = [None, bank(2, [P, S]), bank(0, [P, S]), bank(1, [P, S])]
+        b0_banks = [bank(3 + u, [P, HALF]) for u in range(2)]
+        b_banks = [None] + [bank(PACK + t, [P, S]) for t in range(1, PACK)]
+
+        def gate_low(t):
+            for u in range(2):
+                gate_product(t, logit_banks[t][:, halves[u]], u)
+            nc.scalar.activation(a_low[:, t - 1, :], logit_banks[t][:, :HALF], SIGMOID)
+
+        gate_low(1)
+        for u in range(2):
+            b_product(0, b0_banks[u][:], u)
+            nc.scalar.copy(out=b[0][:, halves[u]], in_=b0_banks[u][:])
+        for t in range(1, PACK):
+            if t > 1:
+                gate_low(t)
+            for u in range(2):
+                b_product(t, b_banks[t][:, halves[u]], u)
+            nc.scalar.copy(out=b[t][:], in_=b_banks[t][:])
+        a_high = tile([P, PACK - 1, HALF], F32, "a_high", "w2q3")
+        for t in (3, 1, 2):
+            nc.scalar.activation(a_high[:, t - 1, :], logit_banks[t][:, HALF:], SIGMOID)
+
+        def a(t, u):
+            return a0[:, halves[u]] if t == 0 else (a_low, a_high)[u][:, t - 1, :]
+
+        a_near = tile([P, PACK, S], F32, "a_near", "w2s2")
 
         def look_up_a_near(t, lo, hi):
             nc.scalar.activation(a_near[:, t, lo:hi], logit[t][:].indirect(entries(near_sb, lo, hi)), SIGMOID)
@@ -166,39 +193,50 @@ def tile_picked_scan2_none_po_kernel(
         look_up_a_near(0, HALF, S)
         nc.scalar.copy(out=logit[1][:], in_=logit_banks[1][:])
         look_up_a_near(1, 0, HALF)
-        for t in range(2, PACK):
+        for t in (2, 3):
             nc.scalar.copy(out=logit[t][:], in_=logit_banks[t][:])
         for c in range(CHUNKS):
             for t in range(2 if c < 2 else 1, PACK):
                 look_up_a_near(t, c * CHUNK, (c + 1) * CHUNK)
 
-        for t, lo in ((0, 0), (0, HALF), (1, 0), (1, HALF), (2, 0), (3, 0), (3, HALF), (2, HALF)):
+        near_term = [tile([P, S], F32, "near_term%d" % t) for t in range(PACK)]
+        for t, u in ((0, 0), (0, 1), (1, 0), (2, 0), (3, 0), (3, 1), (1, 1), (2, 1)):
             nc.vector.tensor_tensor(
-                near_term[t][:, lo : lo + HALF],
-                b[t][:].indirect(entries(near_sb, lo, lo + HALF)),
-                a[t][:, lo : lo + HALF],
+                near_term[t][:, halves[u]],
+                b[t][:].indirect(entries(near_sb, u * HALF, (u + 1) * HALF)),
+                a(t, u),
                 MULT,
             )
-        a2_early = keep.tile([P, S + HALF], F32, name="a2_early", tag="b2")
-        nc.gpsimd.tensor_tensor(a2_early[:, :S], a[0], a_near[:, 0, :], MULT)
-        nc.gpsimd.tensor_tensor(a2_early[:, S:], a[1][:, :HALF], a_near[:, 1, :HALF], MULT)
-        b2_tags = ("b3", "near_term0", "b2_2", "b2_3")
-        b2 = [keep.tile([P, S], F32, name="b2_%d" % t, tag=b2_tags[t]) for t in range(PACK)]
-        for t in (0, 3, 1, 2):
-            nc.vector.tensor_tensor(b2[t][:], b_banks[t][:], near_term[t][:], ADD)
+
+        a2_early = tile([P, S + HALF], F32, "a2_early", "b2")
+        nc.gpsimd.tensor_tensor(a2_early[:, :S], a0[:], a_near[:, 0, :], MULT)
+        nc.gpsimd.tensor_tensor(a2_early[:, S:], a(1, 0), a_near[:, 1, :HALF], MULT)
+        b2 = [tile([P, S], F32, "b2_%d" % t, ("b1", "near_term3", None, "b3")[t]) for t in range(PACK)]
+        b2_late = tile([P, PACK, HALF], F32, "b2_late")
+        for t in (3, 0, 1, 2):
+            if t == 0:
+                for u in range(2):
+                    nc.vector.tensor_tensor(b2[0][:, halves[u]], b0_banks[u][:], near_term[0][:, halves[u]], ADD)
+            else:
+                nc.vector.tensor_tensor(b2[t][:], b_banks[t][:], near_term[t][:], ADD)
             nc.sync.dma_start(out=b2_late[:, t, :], in_=b2[t][:, HALF:])
 
+        a2_late = tile([P, PACK - 1, S], F32, "a2_late")
+
         def a2(t, lo, hi):
-            early = t * S + hi <= S + HALF
-            return a2_early[:, t * S + lo : t * S + hi] if early else a2_late[:, t, lo:hi]
+            if t * S + hi <= S + HALF:
+                return a2_early[:, t * S + lo : t * S + hi]
+            return a2_late[:, t - 1, lo:hi]
 
         def decay(c):
-            cols = slice(c * CHUNK, (c + 1) * CHUNK)
-            planes = slice(2 if c < 2 else 1, PACK)
-            nc.vector.tensor_tensor(a2_late[:, planes, cols], a_all[:, planes, cols], a_near[:, planes, cols], MULT)
+            first = 2 if c < 2 else 1
+            lo, hi = c * CHUNK, (c + 1) * CHUNK
+            gates = (a_low, a_high)[c // 2][:, first - 1 :, lo % HALF : lo % HALF + CHUNK]
+            nc.vector.tensor_tensor(a2_late[:, first - 1 :, lo:hi], gates, a_near[:, first:, lo:hi], MULT)
 
-        yq = keep.tile([P, S], U32, name="yq", align_bytes=64)
-        ys = keep.tile([P, S], U8, name="ys", align_bytes=64)
+        yq = tile([P, S], U32, "yq")
+        ys = tile([P, S], U8, "ys")
+        yg_all = tile([P, S, PACK], BF16, "yg_all")
         out_rows = out_0.rearrange("(p t) j -> p t j", t=PACK)
         out_words = out_1[0].rearrange("p n r -> p (n r)").bitcast(I32)
 
@@ -209,12 +247,9 @@ def tile_picked_scan2_none_po_kernel(
                     far_term[:, t, :], b2[t][:].indirect(entries(far_sb, lo, hi)), a2(t, lo, hi), MULT
                 )
 
-        def far_tile(c, tag):
-            return keep.tile([P, PACK, CHUNK], F32, name="far_term%d" % c, tag=tag, align_bytes=64)
-
         def add_on_tensor(c, far_term):
             lo, hi = c * CHUNK, (c + 1) * CHUNK
-            z_turned = psum.tile([P, PACK, P], F32, name="bank%d" % c)
+            z_turned = bank(c, [P, PACK, P])
             for t in range(PACK):
                 nc.tensor.matmul(
                     z_turned[:, t, :], lhsT=b2[t][:, lo:hi], rhs=ident[:], start=True, stop=False, is_transpose=True
@@ -222,13 +257,16 @@ def tile_picked_scan2_none_po_kernel(
                 nc.tensor.matmul(
                     z_turned[:, t, :], lhsT=far_term[:, t, :], rhs=ident[:], start=False, stop=True, is_transpose=True
                 )
+            return z_turned
+
+        def turn_back(c, z_turned):
             rounded = ring.tile([P, 2, P, 2], BF16, name="rounded", align_bytes=64)
             nc.scalar.copy(out=rounded[:], in_=z_turned[:].rearrange("n (u e) p -> n u p e", e=2))
             pairs = rounded[:].rearrange("n u p e -> n (u p e)").bitcast(F32)
-            pairs_back = psum.tile([P, 2, CHUNK], F32, name="bank%d" % (2 + c))
+            pairs_back = bank(2 + c, [P, 2, CHUNK])
             for u in range(2):
                 nc.tensor.transpose(pairs_back[:, u, :], pairs[:, u * P : (u + 1) * P], ident[:])
-            zg = keep.tile([P, CHUNK, PACK], BF16, name="zg%d" % c, tag="zg%d" % c, align_bytes=64)
+            zg = tile([P, CHUNK, PACK], BF16, "zg%d" % c)
             nc.scalar.copy(
                 out=zg[:].rearrange("p n t -> p (n t)").bitcast(F32).rearrange("p (n u) -> p n u", u=2),
                 in_=pairs_back[:].rearrange("p u n -> p n u"),
@@ -237,7 +275,7 @@ def tile_picked_scan2_none_po_kernel(
 
         def add_on_vector(c, far_term, tag):
             lo = c * CHUNK - HALF
-            zg = keep.tile([P, CHUNK, PACK], BF16, name="zg%d" % c, tag=tag, align_bytes=64)
+            zg = tile([P, CHUNK, PACK], BF16, "zg%d" % c, tag)
             nc.vector.tensor_tensor(
                 zg[:].rearrange("p (n i) t -> p n t i", i=LINE),
                 b2_late[:, :, lo : lo + CHUNK].rearrange("p t (n i) -> p n t i", i=LINE),
@@ -246,8 +284,6 @@ def tile_picked_scan2_none_po_kernel(
             )
             return zg
 
-        yg_all = keep.tile([P, S, PACK], BF16, name="yg_all", align_bytes=64)
-
         def quantise_result(lo, hi):
             nc.vector.quantize_mx(
                 out=yq[:, lo:hi].bitcast(FP8X4),
@@ -255,17 +291,12 @@ def tile_picked_scan2_none_po_kernel(
                 in_=yg_all[:, lo:hi, :].rearrange("p n t -> p (n t)"),
             )
 
-        def project(c, zg):
-            lo, hi = c * CHUNK, (c + 1) * CHUNK
-            zq = keep.tile([P, CHUNK], U32, name="zq%d" % c, align_bytes=64)
-            zs = keep.tile([P, CHUNK], U8, name="zs%d" % c, align_bytes=64)
+        def project(c, zg, out_banks):
+            zq = tile([P, CHUNK], U32, "zq%d" % c)
+            zs = tile([P, CHUNK], U8, "zs%d" % c)
             nc.vector.quantize_mx(out=zq[:].bitcast(FP8X4), scales=zs[:], in_=zg[:].rearrange("p n t -> p (n t)"))
-            y = keep.tile([P, PACK, CHUNK], F32, name="y%d" % c)
-            yg = yg_all[:, lo:hi, :]
-            last = c == CHUNKS - 1
-            parts = 2 if last else 1
-            planes = PACK // parts
-            banks = [psum.tile([P, planes, CHUNK], F32, name="bank%d" % OUT_BANKS[c + u]) for u in range(parts)]
+            planes = PACK // len(out_banks)
+            banks = [bank(i, [P, planes, CHUNK]) for i in out_banks]
             for t in range(PACK):
                 nc.tensor.matmul_mx(
                     out=banks[t // planes][:, t % planes, :],
@@ -276,42 +307,49 @@ def tile_picked_scan2_none_po_kernel(
                     start=True,
                     stop=True,
                 )
-            if last:
-                nc.vector.tensor_copy(out=yg[:, :, :planes], in_=banks[0][:].rearrange("p t n -> p n t"))
-                nc.vector.tensor_copy(out=y[:, :planes], in_=banks[0][:])
-                nc.sync.dma_start(out=out_rows[:, :planes, lo:hi], in_=y[:, :planes])
-                nc.scalar.copy(out=yg[:, :, planes:], in_=banks[1][:].rearrange("p t n -> p n t"))
-                nc.scalar.copy(out=y[:, planes:], in_=banks[1][:])
-                nc.sync.dma_start(out=out_rows[:, planes:, lo:hi], in_=y[:, planes:])
-                quantise_result(lo, hi)
-                return
-            nc.scalar.copy(out=yg, in_=banks[0][:].rearrange("p t n -> p n t"))
-            nc.scalar.copy(out=y[:], in_=banks[0][:])
-            nc.sync.dma_start(out=out_rows[:, :, lo:hi], in_=y[:])
+            return banks
 
-        far0, far1, far2 = [far_tile(c, "far_term%d" % c) for c in range(3)]
-        look_up_far(0, far0, (0,))
-        look_up_far(1, far1, (0,))
+        y = [tile([P, PACK, CHUNK], F32, "y%d" % c) for c in range(CHUNKS)]
+
+        def round_result(copy, c, source, planes):
+            copy(out=yg_all[:, c * CHUNK : (c + 1) * CHUNK, planes], in_=source[:].rearrange("p t n -> p n t"))
+
+        def store_result(copy, c, source, planes):
+            copy(out=y[c][:, planes], in_=source[:])
+            nc.sync.dma_start(out=out_rows[:, planes, c * CHUNK : (c + 1) * CHUNK], in_=y[c][:, planes])
+
+        every = slice(0, PACK)
+        far_term = [tile([P, PACK, CHUNK], F32, "far_term%d" % c) for c in range(3)]
+        look_up_far(0, far_term[0], (0,))
+        look_up_far(1, far_term[1], (0,))
         decay(0)
-        look_up_far(0, far0, (1, 2, 3))
-        zg0 = add_on_tensor(0, far0)
+        look_up_far(0, far_term[0], (1, 2, 3))
+        zg0 = turn_back(0, add_on_tensor(0, far_term[0]))
         decay(1)
-        look_up_far(1, far1, (1, 2, 3))
-        zg1 = add_on_tensor(1, far1)
+        look_up_far(1, far_term[1], (1, 2, 3))
+        zg1 = turn_back(1, add_on_tensor(1, far_term[1]))
         decay(2)
-        look_up_far(2, far2, range(PACK))
-        project(0, zg0)
+        look_up_far(2, far_term[2], range(PACK))
+
+        def empty_on_scalar(c, banks):
+            round_result(nc.scalar.copy, c, banks[0], every)
+            store_result(nc.scalar.copy, c, banks[0], every)
+
+        empty_on_scalar(0, project(0, zg0, (4,)))
         decay(3)
-        zg2 = add_on_vector(2, far2, "zg0")
-        project(1, zg1)
-        project(2, zg2)
-        far3 = far_tile(3, "zg1")
-        look_up_far(3, far3, range(PACK))
+        zg2 = add_on_vector(2, far_term[2], "zg0")
+        empty_on_scalar(1, project(1, zg1, (5,)))
+        empty_on_scalar(2, project(2, zg2, (6,)))
+        far_last = tile([P, PACK, CHUNK], F32, "far_last", "zg1")
+        look_up_far(3, far_last, range(PACK))
         quantise_result(0, HALF)
         nc.sync.dma_start(out=out_words[:, :HALF], in_=yq[:, :HALF].bitcast(I32))
-        zg3 = add_on_vector(3, far3, "zg3")
-        project(3, zg3)
-        quantise_result(HALF, HALF + CHUNK)
+        y3_banks = project(3, add_on_vector(3, far_last, None), (7, 0))
+        for copy, source, planes in zip((nc.vector.tensor_copy, nc.scalar.copy), y3_banks, (slice(0, 2), slice(2, 4))):
+            round_result(copy, 3, source, planes)
+            store_result(copy, 3, source, planes)
+        quantise_result(S - CHUNK, S)
+        quantise_result(HALF, S - CHUNK)
         nc.sync.dma_start(out=out_words[:, HALF:], in_=yq[:, HALF:].bitcast(I32))
         for q in range(4):
             queue = nc.scalar if q % 2 else nc.sync

@@ -86,13 +86,13 @@ def tile_picked_scan2_none_po_kernel(
         w2_rows = w2.rearrange("(p j) c -> p j c", j=PACK)
         nc.sync.dma_start(offs_sb[:], offs)
         nc.sync.dma_start(out=w1w_raw[:].bitcast(I32), in_=w1_words[0].bitcast(I32))
-        nc.sync.dma_start(near_sb[:], near)
+        nc.sync.dma_start(out=w3w_raw[:].bitcast(I32), in_=w3_words[0].bitcast(I32))
         load_scale_rows(nc.sync, xs_raw, x_scales[0])
         nc.sync.dma_start(out=xw_raw[:], in_=x_words[0].rearrange("p n r -> p (n r)").bitcast(I32))
         load_scale_rows(nc.sync, w1s_raw, w1_scales[0])
         nc.sync.dma_start(out=w2_raw[0][:], in_=w2_rows[:, :, : H // 2])
         nc.sync.dma_start(out=w2_raw[1][:], in_=w2_rows[:, :, H // 2 :])
-        nc.sync.dma_start(out=w3w_raw[:].bitcast(I32), in_=w3_words[0].bitcast(I32))
+        nc.sync.dma_start(near_sb[:], near)
         nc.sync.dma_start(far_sb[:], far)
         load_scale_rows(nc.sync, w3s_raw, w3_scales[0])
         make_identity(nc, ident[:])
@@ -100,17 +100,17 @@ def tile_picked_scan2_none_po_kernel(
         halves = (slice(0, HALF), slice(HALF, S))
         whole = slice(0, S)
 
-        w1w = [tile([P, H], U8, "w1w%d" % u, (None, "w2_raw1")[u]) for u in range(2)]
-        w1w_planes = w1w_raw[:].rearrange("p (m t e) -> p t m e", t=PACK, e=2)
-        w1s = tile([P, H], U8, "w1s")
+        w1w = tile([P, 2 * H], U8, "w1w")
+        xq = tile([P, S], U32, "xq")
         xqs = tile([P, S], U8, "xqs")
-        nc.vector.tensor_copy(out=w1w[0][:].rearrange("p (t m e) -> p t m e", t=2, e=2), in_=w1w_planes[:, :2])
+        w3w = tile([P, 2 * N], U8, "w3w")
+        deal_words(nc, w1w[:], w1w_raw[:])
+        deal_words(nc, w3w[:], w3w_raw[:])
         nc.vector.tensor_copy(xqs[:], xs_raw[:].indirect(offs_sb[:]))
-        xq = [tile([P, HALF], U32, "xq0")]
-        nc.vector.tensor_copy(xq[0][:], xw_raw[:].bitcast(U32).indirect(entries(offs_sb, 0, HALF)))
-        deal_scales(nc, w1s[:], w1s_raw[:])
-        xq.append(tile([P, HALF], U32, "xq1", "w1s_raw"))
-        nc.vector.tensor_copy(xq[1][:], xw_raw[:].bitcast(U32).indirect(entries(offs_sb, HALF, S)))
+        nc.vector.tensor_copy(xq[:], xw_raw[:].bitcast(U32).indirect(offs_sb[:]))
+        w1s = [tile([P, 2 * P], U8, "w1s%d" % u, (None, "w2_raw1")[u]) for u in range(2)]
+        w1s_planes = w1s_raw[:].rearrange("p (m t) -> p t m", t=PACK)
+        nc.vector.tensor_copy(out=w1s[0][:].rearrange("p (t m) -> p t m", t=2), in_=w1s_planes[:, :2])
 
         w2g = tile([P, PACK, P, PACK], BF16, "w2g")
         w2q = [tile([P, P], U32, "w2q%d" % t) for t in range(PACK)]
@@ -124,115 +124,87 @@ def tile_picked_scan2_none_po_kernel(
             nc.vector.quantize_mx(
                 out=w2q[t][:].bitcast(FP8X4), scales=w2s[t][:], in_=w2g[:, t].rearrange("p m j -> p (m j)")
             )
-            if t == 1:
-                nc.vector.tensor_copy(out=w1w[1][:].rearrange("p (t m e) -> p t m e", t=2, e=2), in_=w1w_planes[:, 2:])
-        w3w = tile([P, 2 * N], U8, "w3w", "w2g")
-        w3s = tile([P, N], U8, "w3s", "w2s0")
-        deal_words(nc, w3w[:], w3w_raw[:])
-        deal_scales(nc, w3s[:], w3s_raw[:])
+            if t == 0:
+                nc.vector.tensor_copy(out=w1s[1][:].rearrange("p (t m) -> p t m", t=2), in_=w1s_planes[:, 2:])
 
-        def product(out, words, scales, u):
+        def product(out, words, scales):
             nc.tensor.matmul_mx(
-                out=out,
-                lhsT=words,
-                lhsT_scale=scales,
-                rhs=xq[u][:].bitcast(FP8X4),
-                rhs_scale=xqs[:, halves[u]],
-                start=True,
-                stop=True,
+                out=out[:], lhsT=words, lhsT_scale=scales, rhs=xq[:].bitcast(FP8X4), rhs_scale=xqs[:], start=True, stop=True
             )
 
-        def gate_product(t, out, u):
-            product(out, w1w[t // 2][:, t % 2 * 2 * P : (t % 2 + 1) * 2 * P].bitcast(FP4X4), w1s[:, t * P : (t + 1) * P], u)
-
-        def b_product(t, out, u):
-            product(out, w2q[t][:].bitcast(FP8X4), w2s[t][:], u)
-
+        b = [tile([P, S if t == 2 else 2 * S], F32, "b%d" % t) for t in range(PACK)]
         a0 = tile([P, S], F32, "a0")
-        a_low = tile([P, PACK - 1, HALF], F32, "a_low")
-        b = [tile([P, S], F32, "b%d" % t) for t in range(PACK)]
-        logit = [tile([P, S], F32, "logit%d" % t, (None, "w2s1", "w2s3", "xqs")[t]) for t in range(PACK)]
+        a_late = tile([P, 2, S], F32, "a_late")
+        a = [a0[:], b[0][:, S:], a_late[:, 0, :], a_late[:, 1, :]]
+        a2_first = b[1][:, S:]
+        near_term = [b[3][:, S:]] + [tile([P, S], F32, "near_term%d" % t)[:] for t in range(1, PACK)]
+        logit = [None] + [tile([P, S], F32, "logit%d" % t, ("w2q1", "w2q3", "w2s3")[t - 1]) for t in range(1, PACK)]
+        a0_table = tile([P, 2 * S], F32, "a0_table")
+        nc.gpsimd.memset(a0_table[:, S:], 0.0)
+        logit_banks = [bank(t, [P, S]) for t in range(PACK)]
+        b_banks = [bank(PACK + t, [P, S]) for t in range(PACK)]
 
-        for u in range(2):
-            half_bank = bank(u, [P, HALF])
-            gate_product(0, half_bank[:], u)
-            nc.scalar.activation(a0[:, halves[u]], half_bank[:], SIGMOID)
-            nc.scalar.copy(out=logit[0][:, halves[u]], in_=half_bank[:])
-        logit_banks = [None, bank(2, [P, S]), bank(0, [P, S]), bank(1, [P, S])]
-        b0_banks = [bank(3 + u, [P, HALF]) for u in range(2)]
-        b_banks = [None] + [bank(PACK + t, [P, S]) for t in range(1, PACK)]
+        def gate(t, cols):
+            scales = w1s[t // 2][:, t % 2 * P : (t % 2 + 1) * P]
+            product(logit_banks[t], w1w[:, 2 * t * P : 2 * (t + 1) * P].bitcast(FP4X4), scales)
+            nc.scalar.activation(a[t][:, cols], logit_banks[t][:, cols], SIGMOID)
 
-        def gate_low(t):
-            for u in range(2):
-                gate_product(t, logit_banks[t][:, halves[u]], u)
-            nc.scalar.activation(a_low[:, t - 1, :], logit_banks[t][:, :HALF], SIGMOID)
+        gate(0, whole)
+        nc.scalar.activation(a0_table[:, :S], logit_banks[0][:], SIGMOID)
+        for t in range(PACK):
+            if t + 1 < PACK:
+                gate(t + 1, halves[0] if t + 1 == 2 else whole)
+            product(b_banks[t], w2q[t][:].bitcast(FP8X4), w2s[t][:])
+            nc.scalar.copy(out=b[t][:, :S], in_=b_banks[t][:])
+        nc.scalar.activation(a[2][:, HALF:], logit_banks[2][:, HALF:], SIGMOID)
 
-        gate_low(1)
-        for u in range(2):
-            b_product(0, b0_banks[u][:], u)
-            nc.scalar.copy(out=b[0][:, halves[u]], in_=b0_banks[u][:])
-        for t in range(1, PACK):
-            if t > 1:
-                gate_low(t)
-            for u in range(2):
-                b_product(t, b_banks[t][:, halves[u]], u)
-            nc.scalar.copy(out=b[t][:], in_=b_banks[t][:])
-        a_high = tile([P, PACK - 1, HALF], F32, "a_high", "w2q3")
-        for t in (3, 1, 2):
-            nc.scalar.activation(a_high[:, t - 1, :], logit_banks[t][:, HALF:], SIGMOID)
-
-        def a(t, u):
-            return a0[:, halves[u]] if t == 0 else (a_low, a_high)[u][:, t - 1, :]
-
-        a_near = tile([P, PACK, S], F32, "a_near", "w2s2")
+        a_near = tile([P, PACK - 1, S], F32, "a_near")
 
         def look_up_a_near(t, lo, hi):
-            nc.scalar.activation(a_near[:, t, lo:hi], logit[t][:].indirect(entries(near_sb, lo, hi)), SIGMOID)
+            nc.scalar.activation(a_near[:, t - 1, lo:hi], logit[t][:].indirect(entries(near_sb, lo, hi)), SIGMOID)
 
-        look_up_a_near(0, 0, HALF)
-        look_up_a_near(0, HALF, S)
         nc.scalar.copy(out=logit[1][:], in_=logit_banks[1][:])
         look_up_a_near(1, 0, HALF)
-        for t in (2, 3):
-            nc.scalar.copy(out=logit[t][:], in_=logit_banks[t][:])
+        look_up_a_near(1, HALF, S)
+        nc.scalar.copy(out=logit[2][:], in_=logit_banks[2][:])
+        look_up_a_near(2, 0, HALF)
+        nc.scalar.copy(out=logit[3][:], in_=logit_banks[3][:])
         for c in range(CHUNKS):
-            for t in range(2 if c < 2 else 1, PACK):
+            for t in range(3 if c < 2 else 2, PACK):
                 look_up_a_near(t, c * CHUNK, (c + 1) * CHUNK)
 
-        near_term = [tile([P, S], F32, "near_term%d" % t) for t in range(PACK)]
-        for t, u in ((0, 0), (0, 1), (1, 0), (2, 0), (3, 0), (3, 1), (1, 1), (2, 1)):
+        nc.vector.tensor_tensor(a2_first, a0_table[:].indirect(near_sb[:]), a[0], MULT)
+        for t, cols in ((0, whole), (1, whole), (2, halves[0]), (3, whole), (2, halves[1])):
             nc.vector.tensor_tensor(
-                near_term[t][:, halves[u]],
-                b[t][:].indirect(entries(near_sb, u * HALF, (u + 1) * HALF)),
-                a(t, u),
-                MULT,
+                near_term[t][:, cols], b[t][:].indirect(entries(near_sb, cols.start, cols.stop)), a[t][:, cols], MULT
             )
+            if t == 0:
+                w3s = tile([P, N], U8, "w3s", "a0")
+                deal_scales(nc, w3s[:], w3s_raw[:])
 
         a2_early = tile([P, S + HALF], F32, "a2_early", "b2")
-        nc.gpsimd.tensor_tensor(a2_early[:, :S], a0[:], a_near[:, 0, :], MULT)
-        nc.gpsimd.tensor_tensor(a2_early[:, S:], a(1, 0), a_near[:, 1, :HALF], MULT)
-        b2 = [tile([P, S], F32, "b2_%d" % t, ("b1", "near_term3", None, "b3")[t]) for t in range(PACK)]
+        nc.gpsimd.tensor_tensor(a2_early[:, :S], a[1], a_near[:, 0, :], MULT)
+        nc.gpsimd.tensor_tensor(a2_early[:, S:], a[2][:, :HALF], a_near[:, 1, :HALF], MULT)
         b2_late = tile([P, PACK, HALF], F32, "b2_late")
-        for t in (3, 0, 1, 2):
-            if t == 0:
-                for u in range(2):
-                    nc.vector.tensor_tensor(b2[0][:, halves[u]], b0_banks[u][:], near_term[0][:, halves[u]], ADD)
-            else:
-                nc.vector.tensor_tensor(b2[t][:], b_banks[t][:], near_term[t][:], ADD)
+        b2 = {}
+        for t, tag in ((3, None), (2, None), (0, "near_term3"), (1, "near_term2")):
+            b2[t] = tile([P, S], F32, "b2_%d" % t, tag)
+            nc.vector.tensor_tensor(b2[t][:], b_banks[t][:], near_term[t], ADD)
             nc.sync.dma_start(out=b2_late[:, t, :], in_=b2[t][:, HALF:])
 
-        a2_late = tile([P, PACK - 1, S], F32, "a2_late")
+        a2_late = tile([P, 2, S], F32, "a2_late")
 
         def a2(t, lo, hi):
-            if t * S + hi <= S + HALF:
-                return a2_early[:, t * S + lo : t * S + hi]
-            return a2_late[:, t - 1, lo:hi]
+            if t == 0:
+                return a2_first[:, lo:hi]
+            if (t - 1) * S + hi <= S + HALF:
+                return a2_early[:, (t - 1) * S + lo : (t - 1) * S + hi]
+            return a2_late[:, t - 2, lo:hi]
 
         def decay(c):
-            first = 2 if c < 2 else 1
-            lo, hi = c * CHUNK, (c + 1) * CHUNK
-            gates = (a_low, a_high)[c // 2][:, first - 1 :, lo % HALF : lo % HALF + CHUNK]
-            nc.vector.tensor_tensor(a2_late[:, first - 1 :, lo:hi], gates, a_near[:, first:, lo:hi], MULT)
+            first = 1 if c < 2 else 0
+            cols = slice(c * CHUNK, (c + 1) * CHUNK)
+            nc.vector.tensor_tensor(a2_late[:, first:, cols], a_late[:, first:, cols], a_near[:, first + 1 :, cols], MULT)
 
         yq = tile([P, S], U32, "yq")
         ys = tile([P, S], U8, "ys")

@@ -79,9 +79,10 @@ def tile_picked_scan2_none_po_kernel(
         w2_raw = [tile([P, PACK, H // 2], F32, "w2_raw%d" % u) for u in range(2)]
         ident = tile([P, P], F32, "ident")
 
-        nc.gpsimd.memset(xs_raw[:].bitcast(I32), 0)
-        nc.gpsimd.memset(w1s_raw[:].bitcast(I32), 0)
+        nc.vector.memset(xs_raw[:].bitcast(I32), 0)
+        nc.vector.memset(w1s_raw[:].bitcast(I32), 0)
         nc.vector.memset(w3s_raw[:].bitcast(I32), 0)
+        nc.vector.memset(ident[:], 0.0)
 
         w2_rows = w2.rearrange("(p j) c -> p j c", j=PACK)
         nc.sync.dma_start(offs_sb[:], offs)
@@ -95,7 +96,7 @@ def tile_picked_scan2_none_po_kernel(
         nc.sync.dma_start(near_sb[:], near)
         nc.sync.dma_start(far_sb[:], far)
         load_scale_rows(nc.sync, w3s_raw, w3_scales[0])
-        make_identity(nc, ident[:])
+        make_identity(nc, ident[:], nomemset=True)
 
         halves = (slice(0, HALF), slice(HALF, S))
         whole = slice(0, S)

@@ -141,7 +141,7 @@ def tile_picked_scan2_none_po_kernel(
         near_term = [b[3][:, S:]] + [tile([P, S], F32, "near_term%d" % t)[:] for t in range(1, PACK)]
         logit = [None] + [tile([P, S], F32, "logit%d" % t, ("w2q1", "w2q3", "w2s3")[t - 1]) for t in range(1, PACK)]
         a0_table = tile([P, 2 * S], F32, "a0_table")
-        nc.gpsimd.memset(a0_table[:, S:], 0.0)
+        nc.vector.memset(a0_table[:, S:], 0.0)
         logit_banks = [bank(t, [P, S]) for t in range(PACK)]
         b_banks = [bank(PACK + t, [P, S]) for t in range(PACK)]
 
@@ -318,9 +318,10 @@ def tile_picked_scan2_none_po_kernel(
         quantise_result(0, HALF)
         nc.sync.dma_start(out=out_words[:, :HALF], in_=yq[:, :HALF].bitcast(I32))
         y3_banks = project(3, add_on_vector(3, far_last, None), (7, 0))
-        for copy, source, planes in zip((nc.vector.tensor_copy, nc.scalar.copy), y3_banks, (slice(0, 2), slice(2, 4))):
-            round_result(copy, 3, source, planes)
-            store_result(copy, 3, source, planes)
+        round_result(nc.vector.tensor_copy, 3, y3_banks[0], slice(0, 2))
+        store_result(nc.scalar.copy, 3, y3_banks[1], slice(2, 4))
+        store_result(nc.vector.tensor_copy, 3, y3_banks[0], slice(0, 2))
+        round_result(nc.scalar.copy, 3, y3_banks[1], slice(2, 4))
         quantise_result(S - CHUNK, S)
         quantise_result(HALF, S - CHUNK)
         nc.sync.dma_start(out=out_words[:, HALF:], in_=yq[:, HALF:].bitcast(I32))

@@ -313,6 +313,9 @@ def tile_picked_scan2_none_po_kernel(
         zg2 = add_on_vector(2, far_term[2], "zg0")
         empty_on_scalar(1, project(1, zg1, (5,)))
         empty_on_scalar(2, project(2, zg2, (6,)))
+        warm_up = bank(4, [P, S])
+        for t in range(2):
+            product(warm_up, w3w[:, 2 * t * P : 2 * (t + 1) * P].bitcast(FP4X4), w3s[:, t * P : (t + 1) * P])
         far_last = tile([P, PACK, CHUNK], F32, "far_last", "zg1")
         look_up_far(3, far_last, range(PACK))
         quantise_result(0, HALF)

@@ -93,9 +93,9 @@ def tile_picked_scan2_none_po_kernel(
         load_scale_rows(nc.sync, w1s_raw, w1_scales[0])
         nc.sync.dma_start(out=w2_raw[0][:], in_=w2_rows[:, :, : H // 2])
         nc.sync.dma_start(out=w2_raw[1][:], in_=w2_rows[:, :, H // 2 :])
+        load_scale_rows(nc.sync, w3s_raw, w3_scales[0])
         nc.sync.dma_start(near_sb[:], near)
         nc.sync.dma_start(far_sb[:], far)
-        load_scale_rows(nc.sync, w3s_raw, w3_scales[0])
         make_identity(nc, ident[:], nomemset=True)
 
         halves = (slice(0, HALF), slice(HALF, S))
@@ -109,9 +109,13 @@ def tile_picked_scan2_none_po_kernel(
         deal_words(nc, w3w[:], w3w_raw[:])
         nc.vector.tensor_copy(xqs[:], xs_raw[:].indirect(offs_sb[:]))
         nc.vector.tensor_copy(xq[:], xw_raw[:].bitcast(U32).indirect(offs_sb[:]))
-        w1s = [tile([P, 2 * P], U8, "w1s%d" % u, (None, "w2_raw1")[u]) for u in range(2)]
-        w1s_planes = w1s_raw[:].rearrange("p (m t) -> p t m", t=PACK)
-        nc.vector.tensor_copy(out=w1s[0][:].rearrange("p (t m) -> p t m", t=2), in_=w1s_planes[:, :2])
+        w1s_first = tile([P, P], U8, "w1s_first")
+        w1s_early = tile([P, 2 * P], U8, "w1s_early")
+        w1s_last = tile([P, P], U8, "w1s_last", "w2_raw1")
+        w1s = [w1s_first[:], w1s_early[:, :P], w1s_early[:, P:], w1s_last[:]]
+        w1s_planes = w1s_raw[:].rearrange("p (h m t) -> p h t m", h=2, t=PACK)
+        nc.vector.tensor_copy(out=w1s_first[:].rearrange("p (h m) -> p h m", h=2), in_=w1s_planes[:, :, 0])
+        nc.vector.tensor_copy(out=w1s_early[:].rearrange("p (t h m) -> p h t m", t=2, h=2), in_=w1s_planes[:, :, 1:3])
 
         w2g = tile([P, PACK, P, PACK], BF16, "w2g")
         w2q = [tile([P, P], U32, "w2q%d" % t) for t in range(PACK)]
@@ -126,7 +130,10 @@ def tile_picked_scan2_none_po_kernel(
                 out=w2q[t][:].bitcast(FP8X4), scales=w2s[t][:], in_=w2g[:, t].rearrange("p m j -> p (m j)")
             )
             if t == 0:
-                nc.vector.tensor_copy(out=w1s[1][:].rearrange("p (t m) -> p t m", t=2), in_=w1s_planes[:, 2:])
+                nc.vector.tensor_copy(out=w1s_last[:].rearrange("p (h m) -> p h m", h=2), in_=w1s_planes[:, :, 3])
+
+        w3s = tile([P, N], U8, "w3s")
+        deal_scales(nc, w3s[:], w3s_raw[:])
 
         def product(out, words, scales):
             nc.tensor.matmul_mx(
@@ -134,30 +141,44 @@ def tile_picked_scan2_none_po_kernel(
             )
 
         b = [tile([P, S if t == 2 else 2 * S], F32, "b%d" % t) for t in range(PACK)]
-        a0 = tile([P, S], F32, "a0")
-        a_late = tile([P, 2, S], F32, "a_late")
-        a = [a0[:], b[0][:, S:], a_late[:, 0, :], a_late[:, 1, :]]
+        a2_gate = tile([P, HALF], F32, "a2_gate")
+        a_late = tile([P, 3 * HALF], F32, "a_late", "w2q0")
+        gate_parts = {(0, 0): b[3][:, S:], (1, 0): b[0][:, S:], (2, 0): a2_gate[:], (2, HALF): a_late[:, :HALF], (3, 0): a_late[:, HALF:]}
+
+        def a(t, cols):
+            return gate_parts[t, cols.start][:, : cols.stop - cols.start]
+
         a2_first = b[1][:, S:]
-        near_term = [b[3][:, S:]] + [tile([P, S], F32, "near_term%d" % t)[:] for t in range(1, PACK)]
+        near_term = [tile([P, S], F32, "near_term%d" % t)[:] for t in range(PACK)]
         logit = [None] + [tile([P, S], F32, "logit%d" % t, ("w2q1", "w2q3", "w2s3")[t - 1]) for t in range(1, PACK)]
         a0_table = tile([P, 2 * S], F32, "a0_table")
         nc.vector.memset(a0_table[:, S:], 0.0)
         logit_banks = [bank(t, [P, S]) for t in range(PACK)]
         b_banks = [bank(PACK + t, [P, S]) for t in range(PACK)]
 
-        def gate(t, cols):
-            scales = w1s[t // 2][:, t % 2 * P : (t % 2 + 1) * P]
-            product(logit_banks[t], w1w[:, 2 * t * P : 2 * (t + 1) * P].bitcast(FP4X4), scales)
-            nc.scalar.activation(a[t][:, cols], logit_banks[t][:, cols], SIGMOID)
+        def gate_product(t):
+            product(logit_banks[t], w1w[:, 2 * t * P : 2 * (t + 1) * P].bitcast(FP4X4), w1s[t])
 
-        gate(0, whole)
-        nc.scalar.activation(a0_table[:, :S], logit_banks[0][:], SIGMOID)
-        for t in range(PACK):
-            if t + 1 < PACK:
-                gate(t + 1, halves[0] if t + 1 == 2 else whole)
+        def gate(t, cols):
+            nc.scalar.activation(a(t, cols), logit_banks[t][:, cols], SIGMOID)
+
+        def make_b(t):
             product(b_banks[t], w2q[t][:].bitcast(FP8X4), w2s[t][:])
             nc.scalar.copy(out=b[t][:, :S], in_=b_banks[t][:])
-        nc.scalar.activation(a[2][:, HALF:], logit_banks[2][:, HALF:], SIGMOID)
+
+        for t in range(3):
+            gate_product(t)
+        gate(0, whole)
+        nc.scalar.activation(a0_table[:, :S], logit_banks[0][:], SIGMOID)
+        gate(1, whole)
+        gate(2, halves[0])
+        make_b(0)
+        make_b(1)
+        gate_product(3)
+        gate(3, whole)
+        make_b(2)
+        make_b(3)
+        gate(2, halves[1])
 
         a_near = tile([P, PACK - 1, S], F32, "a_near")
 
@@ -174,18 +195,15 @@ def tile_picked_scan2_none_po_kernel(
             for t in range(3 if c < 2 else 2, PACK):
                 look_up_a_near(t, c * CHUNK, (c + 1) * CHUNK)
 
-        nc.vector.tensor_tensor(a2_first, a0_table[:].indirect(near_sb[:]), a[0], MULT)
+        nc.vector.tensor_tensor(a2_first, a0_table[:].indirect(near_sb[:]), a(0, whole), MULT)
         for t, cols in ((0, whole), (1, whole), (2, halves[0]), (3, whole), (2, halves[1])):
             nc.vector.tensor_tensor(
-                near_term[t][:, cols], b[t][:].indirect(entries(near_sb, cols.start, cols.stop)), a[t][:, cols], MULT
+                near_term[t][:, cols], b[t][:].indirect(entries(near_sb, cols.start, cols.stop)), a(t, cols), MULT
             )
-            if t == 0:
-                w3s = tile([P, N], U8, "w3s", "a0")
-                deal_scales(nc, w3s[:], w3s_raw[:])
 
-        a2_early = tile([P, S + HALF], F32, "a2_early", "b2")
-        nc.gpsimd.tensor_tensor(a2_early[:, :S], a[1], a_near[:, 0, :], MULT)
-        nc.gpsimd.tensor_tensor(a2_early[:, S:], a[2][:, :HALF], a_near[:, 1, :HALF], MULT)
+        a2_early = tile([P, S + HALF], F32, "a2_early", "b3")
+        nc.gpsimd.tensor_tensor(a2_early[:, :S], a(1, whole), a_near[:, 0, :], MULT)
+        nc.gpsimd.tensor_tensor(a2_early[:, S:], a(2, halves[0]), a_near[:, 1, :HALF], MULT)
         b2_late = tile([P, PACK, HALF], F32, "b2_late")
         b2 = {}
         for t, tag in ((3, None), (2, None), (0, "near_term3"), (1, "near_term2")):
@@ -205,7 +223,10 @@ def tile_picked_scan2_none_po_kernel(
         def decay(c):
             first = 1 if c < 2 else 0
             cols = slice(c * CHUNK, (c + 1) * CHUNK)
-            nc.vector.tensor_tensor(a2_late[:, first:, cols], a_late[:, first:, cols], a_near[:, first + 1 :, cols], MULT)
+            lo = c * CHUNK % HALF
+            thirds = a_late[:].rearrange("p (u n) -> p u n", u=3)[:, :, lo : lo + CHUNK]
+            gates = thirds[:, 1:2] if c < 2 else thirds[:, 0:3:2]
+            nc.vector.tensor_tensor(a2_late[:, first:, cols], gates, a_near[:, first + 1 :, cols], MULT)
 
         yq = tile([P, S], U32, "yq")
         ys = tile([P, S], U8, "ys")

@@ -24,6 +24,7 @@ LIST_ROWS = 16
 HALF = S // 2
 CHUNK = 128
 CHUNKS = S // CHUNK
+ROW_PARTS = 2
 LINE = 2
 
 
@@ -75,13 +76,15 @@ def tile_picked_scan2_none_po_kernel(
         w1w_raw = tile([P, 2 * H], U8, "w1w_raw")
         w3w_raw = tile([P, 2 * N], U8, "w3w_raw")
         w1s_raw = tile([P, H], U8, "w1s_raw")
-        w3s_raw = tile([P, N], U8, "w3s_raw")
+        w3s_raw = tile([P, N // ROW_PARTS], U8, "w3s_raw")
+        w3s = tile([P, N], U8, "w3s")
         w2_raw = [tile([P, PACK, H // 2], F32, "w2_raw%d" % u) for u in range(2)]
         ident = tile([P, P], F32, "ident")
 
         nc.vector.memset(xs_raw[:].bitcast(I32), 0)
         nc.vector.memset(w1s_raw[:].bitcast(I32), 0)
         nc.vector.memset(w3s_raw[:].bitcast(I32), 0)
+        nc.vector.memset(w3s[:].bitcast(I32), 0)
         nc.vector.memset(ident[:], 0.0)
 
         w2_rows = w2.rearrange("(p j) c -> p j c", j=PACK)
@@ -91,9 +94,12 @@ def tile_picked_scan2_none_po_kernel(
         load_scale_rows(nc.sync, xs_raw, x_scales[0])
         nc.sync.dma_start(out=xw_raw[:], in_=x_words[0].rearrange("p n r -> p (n r)").bitcast(I32))
         load_scale_rows(nc.sync, w1s_raw, w1_scales[0])
+        nc.sync.dma_start(
+            out=w3s_raw[: 16 * ROW_PARTS, :].bitcast(I32),
+            in_=w3_scales[0].rearrange("j (s n) -> (j s) n", s=ROW_PARTS).bitcast(I32),
+        )
         nc.sync.dma_start(out=w2_raw[0][:], in_=w2_rows[:, :, : H // 2])
         nc.sync.dma_start(out=w2_raw[1][:], in_=w2_rows[:, :, H // 2 :])
-        load_scale_rows(nc.sync, w3s_raw, w3_scales[0])
         nc.sync.dma_start(near_sb[:], near)
         nc.sync.dma_start(far_sb[:], far)
         make_identity(nc, ident[:], nomemset=True)
@@ -123,6 +129,8 @@ def tile_picked_scan2_none_po_kernel(
         w2_dealt = w2g[:].rearrange("p t m j -> p m j t")
         w2_halves = [raw[:].rearrange("p j (m t) -> p m j t", t=PACK) for raw in w2_raw]
         nc.vector.tensor_copy(out=w2_dealt[:, : P // 2], in_=w2_halves[0])
+        w3s_parts = tile([P, N // ROW_PARTS], U8, "w3s_parts")
+        deal_scales(nc, w3s_parts[:], w3s_raw[:])
         for pair in (slice(0, 2), slice(2, 4)):
             nc.vector.tensor_copy(out=w2_dealt[:, P // 2 :, :, pair], in_=w2_halves[1][:, :, :, pair])
         for t in range(PACK):
@@ -132,8 +140,11 @@ def tile_picked_scan2_none_po_kernel(
             if t == 0:
                 nc.vector.tensor_copy(out=w1s_last[:].rearrange("p (h m) -> p h m", h=2), in_=w1s_planes[:, :, 3])
 
-        w3s = tile([P, N], U8, "w3s")
-        deal_scales(nc, w3s[:], w3s_raw[:])
+        for q in range(4):
+            places = w3s[32 * q : 32 * q + 4, :].bitcast(I32).rearrange("p (t s m) -> p s t m", t=PACK, s=ROW_PARTS)
+            for part in range(ROW_PARTS):
+                rows = w3s_parts[4 * ROW_PARTS * q + part : 4 * ROW_PARTS * (q + 1) : ROW_PARTS, :]
+                nc.sync.dma_start(out=places[:, part], in_=rows.bitcast(I32).rearrange("p (t m) -> p t m", t=PACK))
 
         def product(out, words, scales):
             nc.tensor.matmul_mx(

@@ -24,6 +24,7 @@ LIST_ROWS = 16
 HALF = S // 2
 CHUNK = 128
 CHUNKS = S // CHUNK
+W2_FIRST = 320
 ROW_PARTS = 2
 LINE = 2
 
@@ -78,7 +79,7 @@ def tile_picked_scan2_none_po_kernel(
         w1s_raw = tile([P, H], U8, "w1s_raw")
         w3s_raw = tile([P, N // ROW_PARTS], U8, "w3s_raw")
         w3s = tile([P, N], U8, "w3s")
-        w2_raw = [tile([P, PACK, H // 2], F32, "w2_raw%d" % u) for u in range(2)]
+        w2_raw = [tile([P, PACK, width], F32, "w2_raw%d" % u) for u, width in enumerate((W2_FIRST, H - W2_FIRST))]
         ident = tile([P, P], F32, "ident")
 
         nc.vector.memset(xs_raw[:].bitcast(I32), 0)
@@ -98,8 +99,8 @@ def tile_picked_scan2_none_po_kernel(
             out=w3s_raw[: 16 * ROW_PARTS, :].bitcast(I32),
             in_=w3_scales[0].rearrange("j (s n) -> (j s) n", s=ROW_PARTS).bitcast(I32),
         )
-        nc.sync.dma_start(out=w2_raw[0][:], in_=w2_rows[:, :, : H // 2])
-        nc.sync.dma_start(out=w2_raw[1][:], in_=w2_rows[:, :, H // 2 :])
+        nc.sync.dma_start(out=w2_raw[0][:], in_=w2_rows[:, :, :W2_FIRST])
+        nc.sync.dma_start(out=w2_raw[1][:], in_=w2_rows[:, :, W2_FIRST:])
         nc.sync.dma_start(near_sb[:], near)
         nc.sync.dma_start(far_sb[:], far)
         make_identity(nc, ident[:], nomemset=True)
@@ -128,11 +129,11 @@ def tile_picked_scan2_none_po_kernel(
         w2s = [tile([P, P], U8, "w2s%d" % t) for t in range(PACK)]
         w2_dealt = w2g[:].rearrange("p t m j -> p m j t")
         w2_halves = [raw[:].rearrange("p j (m t) -> p m j t", t=PACK) for raw in w2_raw]
-        nc.vector.tensor_copy(out=w2_dealt[:, : P // 2], in_=w2_halves[0])
+        nc.vector.tensor_copy(out=w2_dealt[:, : W2_FIRST // PACK], in_=w2_halves[0])
         w3s_parts = tile([P, N // ROW_PARTS], U8, "w3s_parts")
         deal_scales(nc, w3s_parts[:], w3s_raw[:])
         for pair in (slice(0, 2), slice(2, 4)):
-            nc.vector.tensor_copy(out=w2_dealt[:, P // 2 :, :, pair], in_=w2_halves[1][:, :, :, pair])
+            nc.vector.tensor_copy(out=w2_dealt[:, W2_FIRST // PACK :, :, pair], in_=w2_halves[1][:, :, :, pair])
         for t in range(PACK):
             nc.vector.quantize_mx(
                 out=w2q[t][:].bitcast(FP8X4), scales=w2s[t][:], in_=w2g[:, t].rearrange("p m j -> p (m j)")

@@ -16,6 +16,7 @@ FP8X4 = mybir.dt.float8_e4m3fn_x4
 FP4X4 = mybir.dt.float4_e2m1fn_x4
 MULT = mybir.AluOpType.mult
 ADD = mybir.AluOpType.add
+COPY = mybir.ActivationFunctionType.Copy
 SIGMOID = mybir.ActivationFunctionType.Sigmoid
 
 P = 128
@@ -119,9 +120,9 @@ def tile_picked_scan2_none_po_kernel(
         w1s_first = tile([P, P], U8, "w1s_first")
         w1s_early = tile([P, 2 * P], U8, "w1s_early")
         w1s_last = tile([P, P], U8, "w1s_last", "w2_raw1")
-        w1s = [w1s_first[:], w1s_early[:, :P], w1s_early[:, P:], w1s_last[:]]
+        w1s = [w1s_last[:], w1s_early[:, :P], w1s_early[:, P:], w1s_first[:]]
         w1s_planes = w1s_raw[:].rearrange("p (h m t) -> p h t m", h=2, t=PACK)
-        nc.vector.tensor_copy(out=w1s_first[:].rearrange("p (h m) -> p h m", h=2), in_=w1s_planes[:, :, 0])
+        nc.vector.tensor_copy(out=w1s_first[:].rearrange("p (h m) -> p h m", h=2), in_=w1s_planes[:, :, 3])
         nc.vector.tensor_copy(out=w1s_early[:].rearrange("p (t h m) -> p h t m", t=2, h=2), in_=w1s_planes[:, :, 1:3])
 
         w2g = tile([P, PACK, P, PACK], BF16, "w2g")
@@ -132,14 +133,14 @@ def tile_picked_scan2_none_po_kernel(
         nc.vector.tensor_copy(out=w2_dealt[:, : W2_FIRST // PACK], in_=w2_halves[0])
         w3s_parts = tile([P, N // ROW_PARTS], U8, "w3s_parts")
         deal_scales(nc, w3s_parts[:], w3s_raw[:])
-        for pair in (slice(0, 2), slice(2, 4)):
+        for pair in (slice(2, 4), slice(0, 2)):
             nc.vector.tensor_copy(out=w2_dealt[:, W2_FIRST // PACK :, :, pair], in_=w2_halves[1][:, :, :, pair])
-        for t in range(PACK):
+        for t in reversed(range(PACK)):
             nc.vector.quantize_mx(
                 out=w2q[t][:].bitcast(FP8X4), scales=w2s[t][:], in_=w2g[:, t].rearrange("p m j -> p (m j)")
             )
-            if t == 0:
-                nc.vector.tensor_copy(out=w1s_last[:].rearrange("p (h m) -> p h m", h=2), in_=w1s_planes[:, :, 3])
+            if t == 3:
+                nc.vector.tensor_copy(out=w1s_last[:].rearrange("p (h m) -> p h m", h=2), in_=w1s_planes[:, :, 0])
 
         for q in range(4):
             places = w3s[32 * q : 32 * q + 4, :].bitcast(I32).rearrange("p (t s m) -> p s t m", t=PACK, s=ROW_PARTS)
@@ -152,19 +153,12 @@ def tile_picked_scan2_none_po_kernel(
                 out=out[:], lhsT=words, lhsT_scale=scales, rhs=xq[:].bitcast(FP8X4), rhs_scale=xqs[:], start=True, stop=True
             )
 
-        b = [tile([P, S if t == 2 else 2 * S], F32, "b%d" % t) for t in range(PACK)]
-        a2_gate = tile([P, HALF], F32, "a2_gate")
-        a_late = tile([P, 3 * HALF], F32, "a_late", "w2q0")
-        gate_parts = {(0, 0): b[3][:, S:], (1, 0): b[0][:, S:], (2, 0): a2_gate[:], (2, HALF): a_late[:, :HALF], (3, 0): a_late[:, HALF:]}
-
-        def a(t, cols):
-            return gate_parts[t, cols.start][:, : cols.stop - cols.start]
-
-        a2_first = b[1][:, S:]
+        decay = tile([P, PACK, S], F32, "decay")
+        b_tables = {t: tile([P, 2 * S], F32, "b%d" % t)[:] for t in (0, 2, 3)}
+        b_tables[1] = decay[:].rearrange("p t n -> p (t n)")
+        a = [tile([P, S], F32, "a%d" % t) for t in range(PACK)]
+        a3_table = tile([P, 2 * S], F32, "a3_table")
         near_term = [tile([P, S], F32, "near_term%d" % t)[:] for t in range(PACK)]
-        logit = [None] + [tile([P, S], F32, "logit%d" % t, ("w2q1", "w2q3", "w2s3")[t - 1]) for t in range(1, PACK)]
-        a0_table = tile([P, 2 * S], F32, "a0_table")
-        nc.vector.memset(a0_table[:, S:], 0.0)
         logit_banks = [bank(t, [P, S]) for t in range(PACK)]
         b_banks = [bank(PACK + t, [P, S]) for t in range(PACK)]
 
@@ -172,73 +166,45 @@ def tile_picked_scan2_none_po_kernel(
             product(logit_banks[t], w1w[:, 2 * t * P : 2 * (t + 1) * P].bitcast(FP4X4), w1s[t])
 
         def gate(t, cols):
-            nc.scalar.activation(a(t, cols), logit_banks[t][:, cols], SIGMOID)
+            nc.scalar.activation(a[t][:, cols], logit_banks[t][:, cols], SIGMOID)
 
         def make_b(t):
             product(b_banks[t], w2q[t][:].bitcast(FP8X4), w2s[t][:])
-            nc.scalar.copy(out=b[t][:, :S], in_=b_banks[t][:])
+            nc.scalar.copy(out=b_tables[t][:, :S], in_=b_banks[t][:])
 
-        for t in range(3):
+        for t in (3, 2, 1):
             gate_product(t)
-        gate(0, whole)
-        nc.scalar.activation(a0_table[:, :S], logit_banks[0][:], SIGMOID)
+        gate(3, whole)
+        nc.scalar.activation(a3_table[:, :S], logit_banks[3][:], SIGMOID)
+        gate(2, whole)
         gate(1, whole)
-        gate(2, halves[0])
+        nc.vector.tensor_tensor(decay[:, 3, :], a3_table[:].indirect(near_sb[:]), a[3][:], MULT)
+        make_b(3)
+        make_b(2)
+        gate_product(0)
+        gate(0, whole)
         make_b(0)
         make_b(1)
-        gate_product(3)
-        gate(3, whole)
-        make_b(2)
-        make_b(3)
-        gate(2, halves[1])
 
-        a_near = tile([P, PACK - 1, S], F32, "a_near")
+        a_near = [tile([P, S], F32, "a_near%d" % t, ("w2s0", "w2s1", "w2q1")[t]) for t in range(3)]
+        for t, cols in ((2, halves[0]), (2, halves[1]), (1, halves[0]), (0, halves[0]), (0, halves[1]), (1, halves[1])):
+            nc.scalar.activation(a_near[t][:, cols], a[t][:].indirect(entries(near_sb, cols.start, cols.stop)), COPY)
 
-        def look_up_a_near(t, lo, hi):
-            nc.scalar.activation(a_near[:, t - 1, lo:hi], logit[t][:].indirect(entries(near_sb, lo, hi)), SIGMOID)
+        for t, cols in ((3, whole), (2, whole), (0, whole), (1, whole)):
+            nc.vector.tensor_tensor(near_term[t][:, cols], b_tables[t].indirect(near_sb[:]), a[t][:, cols], MULT)
 
-        nc.scalar.copy(out=logit[1][:], in_=logit_banks[1][:])
-        look_up_a_near(1, 0, HALF)
-        look_up_a_near(1, HALF, S)
-        nc.scalar.copy(out=logit[2][:], in_=logit_banks[2][:])
-        look_up_a_near(2, 0, HALF)
-        nc.scalar.copy(out=logit[3][:], in_=logit_banks[3][:])
-        for c in range(CHUNKS):
-            for t in range(3 if c < 2 else 2, PACK):
-                look_up_a_near(t, c * CHUNK, (c + 1) * CHUNK)
-
-        nc.vector.tensor_tensor(a2_first, a0_table[:].indirect(near_sb[:]), a(0, whole), MULT)
-        for t, cols in ((0, whole), (1, whole), (2, halves[0]), (3, whole), (2, halves[1])):
-            nc.vector.tensor_tensor(
-                near_term[t][:, cols], b[t][:].indirect(entries(near_sb, cols.start, cols.stop)), a(t, cols), MULT
-            )
-
-        a2_early = tile([P, S + HALF], F32, "a2_early", "b3")
-        nc.gpsimd.tensor_tensor(a2_early[:, :S], a(1, whole), a_near[:, 0, :], MULT)
-        nc.gpsimd.tensor_tensor(a2_early[:, S:], a(2, halves[0]), a_near[:, 1, :HALF], MULT)
-        b2_late = tile([P, PACK, HALF], F32, "b2_late")
+        nc.gpsimd.tensor_tensor(decay[:, 2, :], a[2][:], a_near[2][:], MULT)
+        nc.gpsimd.tensor_tensor(decay[:, 1, :HALF], a[1][:, :HALF], a_near[1][:, :HALF], MULT)
+        b2_late = tile([P, PACK, S - CHUNK], F32, "b2_late")
         b2 = {}
-        for t, tag in ((3, None), (2, None), (0, "near_term3"), (1, "near_term2")):
+        sum_order = (0, 1, 3, 2)
+        for t, tag in zip(sum_order, (None, None, "near_term0", "near_term1")):
             b2[t] = tile([P, S], F32, "b2_%d" % t, tag)
             nc.vector.tensor_tensor(b2[t][:], b_banks[t][:], near_term[t], ADD)
-            nc.sync.dma_start(out=b2_late[:, t, :], in_=b2[t][:, HALF:])
+            nc.sync.dma_start(out=b2_late[:, t, :], in_=b2[t][:, CHUNK:])
 
-        a2_late = tile([P, 2, S], F32, "a2_late")
-
-        def a2(t, lo, hi):
-            if t == 0:
-                return a2_first[:, lo:hi]
-            if (t - 1) * S + hi <= S + HALF:
-                return a2_early[:, (t - 1) * S + lo : (t - 1) * S + hi]
-            return a2_late[:, t - 2, lo:hi]
-
-        def decay(c):
-            first = 1 if c < 2 else 0
-            cols = slice(c * CHUNK, (c + 1) * CHUNK)
-            lo = c * CHUNK % HALF
-            thirds = a_late[:].rearrange("p (u n) -> p u n", u=3)[:, :, lo : lo + CHUNK]
-            gates = thirds[:, 1:2] if c < 2 else thirds[:, 0:3:2]
-            nc.vector.tensor_tensor(a2_late[:, first:, cols], gates, a_near[:, first + 1 :, cols], MULT)
+        def make_decay(t, cols):
+            nc.vector.tensor_tensor(decay[:, t, cols], a[t][:, cols], a_near[t][:, cols], MULT)
 
         yq = tile([P, S], U32, "yq")
         ys = tile([P, S], U8, "ys")
@@ -246,17 +212,32 @@ def tile_picked_scan2_none_po_kernel(
         out_rows = out_0.rearrange("(p t) j -> p t j", t=PACK)
         out_words = out_1[0].rearrange("p n r -> p (n r)").bitcast(I32)
 
-        def look_up_far(c, far_term, planes):
+        b2_far = {}
+        for c in (1, 2):
+            b2_far[c] = tile([P, PACK, CHUNK], F32, "b2_far%d" % c)
+            for t in sum_order:
+                nc.scalar.activation(
+                    b2_far[c][:, t, :], b2[t][:].indirect(entries(far_sb, c * CHUNK, (c + 1) * CHUNK)), COPY
+                )
+
+        def weigh(c, tag):
+            far_term = tile([P, PACK, CHUNK], F32, "far_term%d" % c, tag)
+            nc.vector.tensor_tensor(far_term[:], b2_far[c][:], decay[:, :, c * CHUNK : (c + 1) * CHUNK], MULT)
+            return far_term
+
+        def look_up_far(c, tag, planes):
             lo, hi = c * CHUNK, (c + 1) * CHUNK
+            far_term = tile([P, PACK, CHUNK], F32, "far_term%d" % c, tag)
             for t in planes:
                 nc.vector.tensor_tensor(
-                    far_term[:, t, :], b2[t][:].indirect(entries(far_sb, lo, hi)), a2(t, lo, hi), MULT
+                    far_term[:, t, :], b2[t][:].indirect(entries(far_sb, lo, hi)), decay[:, t, lo:hi], MULT
                 )
+            return far_term
 
         def add_on_tensor(c, far_term):
             lo, hi = c * CHUNK, (c + 1) * CHUNK
             z_turned = bank(c, [P, PACK, P])
-            for t in range(PACK):
+            for t in (3, 0, 2, 1):
                 nc.tensor.matmul(
                     z_turned[:, t, :], lhsT=b2[t][:, lo:hi], rhs=ident[:], start=True, stop=False, is_transpose=True
                 )
@@ -279,9 +260,9 @@ def tile_picked_scan2_none_po_kernel(
             )
             return zg
 
-        def add_on_vector(c, far_term, tag):
-            lo = c * CHUNK - HALF
-            zg = tile([P, CHUNK, PACK], BF16, "zg%d" % c, tag)
+        def add_on_vector(c, far_term):
+            lo = (c - 1) * CHUNK
+            zg = tile([P, CHUNK, PACK], BF16, "zg%d" % c)
             nc.vector.tensor_tensor(
                 zg[:].rearrange("p (n i) t -> p n t i", i=LINE),
                 b2_late[:, :, lo : lo + CHUNK].rearrange("p t (n i) -> p n t i", i=LINE),
@@ -297,8 +278,8 @@ def tile_picked_scan2_none_po_kernel(
                 in_=yg_all[:, lo:hi, :].rearrange("p n t -> p (n t)"),
             )
 
-        def project(c, zg, out_banks):
-            zq = tile([P, CHUNK], U32, "zq%d" % c)
+        def project(c, zg, out_banks, tag=None):
+            zq = tile([P, CHUNK], U32, "zq%d" % c, tag)
             zs = tile([P, CHUNK], U8, "zs%d" % c)
             nc.vector.quantize_mx(out=zq[:].bitcast(FP8X4), scales=zs[:], in_=zg[:].rearrange("p n t -> p (n t)"))
             planes = PACK // len(out_banks)
@@ -325,35 +306,33 @@ def tile_picked_scan2_none_po_kernel(
             nc.sync.dma_start(out=out_rows[:, planes, c * CHUNK : (c + 1) * CHUNK], in_=y[c][:, planes])
 
         every = slice(0, PACK)
-        far_term = [tile([P, PACK, CHUNK], F32, "far_term%d" % c) for c in range(3)]
-        look_up_far(0, far_term[0], (0,))
-        look_up_far(1, far_term[1], (0,))
-        decay(0)
-        look_up_far(0, far_term[0], (1, 2, 3))
-        zg0 = turn_back(0, add_on_tensor(0, far_term[0]))
-        decay(1)
-        look_up_far(1, far_term[1], (1, 2, 3))
-        zg1 = turn_back(1, add_on_tensor(1, far_term[1]))
-        decay(2)
-        look_up_far(2, far_term[2], range(PACK))
 
         def empty_on_scalar(c, banks):
             round_result(nc.scalar.copy, c, banks[0], every)
             store_result(nc.scalar.copy, c, banks[0], every)
 
-        empty_on_scalar(0, project(0, zg0, (4,)))
-        decay(3)
-        zg2 = add_on_vector(2, far_term[2], "zg0")
+        make_decay(0, halves[0])
+        zg0 = turn_back(0, add_on_tensor(0, look_up_far(0, None, (3, 0, 2, 1))))
+        b2_far_last = tile([P, 2, CHUNK], F32, "b2_far_last", "far_term0")
+        for t in range(2):
+            nc.scalar.activation(b2_far_last[:, t, :], b2[t][:].indirect(entries(far_sb, S - CHUNK, S)), COPY)
+        far1 = weigh(1, None)
+        make_decay(0, halves[1])
+        zg1 = add_on_vector(1, far1)
+        make_decay(1, halves[1])
         empty_on_scalar(1, project(1, zg1, (5,)))
+        far2 = weigh(2, "far_term1")
+        empty_on_scalar(0, project(0, zg0, (4,), "zg1"))
+        zg2 = add_on_vector(2, far2)
         empty_on_scalar(2, project(2, zg2, (6,)))
-        warm_up = bank(4, [P, S])
+        warm_up = bank(5, [P, S])
         for t in range(2):
             product(warm_up, w3w[:, 2 * t * P : 2 * (t + 1) * P].bitcast(FP4X4), w3s[:, t * P : (t + 1) * P])
-        far_last = tile([P, PACK, CHUNK], F32, "far_last", "zg1")
-        look_up_far(3, far_last, range(PACK))
+        far3 = look_up_far(3, "zg0", (3, 2))
+        nc.vector.tensor_tensor(far3[:, :2, :], b2_far_last[:], decay[:, :2, S - CHUNK :], MULT)
         quantise_result(0, HALF)
         nc.sync.dma_start(out=out_words[:, :HALF], in_=yq[:, :HALF].bitcast(I32))
-        y3_banks = project(3, add_on_vector(3, far_last, None), (7, 0))
+        y3_banks = project(3, add_on_vector(3, far3), (7, 0))
         round_result(nc.vector.tensor_copy, 3, y3_banks[0], slice(0, 2))
         store_result(nc.scalar.copy, 3, y3_banks[1], slice(2, 4))
         store_result(nc.vector.tensor_copy, 3, y3_banks[0], slice(0, 2))

@@ -156,7 +156,8 @@ def tile_picked_scan2_none_po_kernel(
         decay = tile([P, PACK, S], F32, "decay")
         b_tables = {t: tile([P, 2 * S], F32, "b%d" % t)[:] for t in (0, 2, 3)}
         b_tables[1] = decay[:].rearrange("p t n -> p (t n)")
-        a = [tile([P, S], F32, "a%d" % t) for t in range(PACK)]
+        a_tables = [tile([P, 2 * S], F32, "a%d" % t) for t in range(3)]
+        a = [table[:, :S] for table in a_tables] + [tile([P, S], F32, "a3")[:]]
         a3_table = tile([P, 2 * S], F32, "a3_table")
         near_term = [tile([P, S], F32, "near_term%d" % t)[:] for t in range(PACK)]
         logit_banks = [bank(t, [P, S]) for t in range(PACK)]
@@ -178,7 +179,7 @@ def tile_picked_scan2_none_po_kernel(
         nc.scalar.activation(a3_table[:, :S], logit_banks[3][:], SIGMOID)
         gate(2, whole)
         gate(1, whole)
-        nc.vector.tensor_tensor(decay[:, 3, :], a3_table[:].indirect(near_sb[:]), a[3][:], MULT)
+        nc.vector.tensor_tensor(decay[:, 3, :], a3_table[:].indirect(near_sb[:]), a[3], MULT)
         make_b(3)
         make_b(2)
         gate_product(0)
@@ -187,42 +188,44 @@ def tile_picked_scan2_none_po_kernel(
         make_b(1)
 
         a_near = [tile([P, S], F32, "a_near%d" % t, ("w2s0", "w2s1", "w2q1")[t]) for t in range(3)]
-        for t, cols in ((2, halves[0]), (2, halves[1]), (1, halves[0]), (0, halves[0]), (0, halves[1]), (1, halves[1])):
-            nc.scalar.activation(a_near[t][:, cols], a[t][:].indirect(entries(near_sb, cols.start, cols.stop)), COPY)
+        for t in (2, 1, 0):
+            nc.scalar.activation(a_near[t][:], a_tables[t][:].indirect(near_sb[:]), COPY)
 
         for t, cols in ((3, whole), (2, whole), (0, whole), (1, whole)):
             nc.vector.tensor_tensor(near_term[t][:, cols], b_tables[t].indirect(near_sb[:]), a[t][:, cols], MULT)
 
-        nc.gpsimd.tensor_tensor(decay[:, 2, :], a[2][:], a_near[2][:], MULT)
-        nc.gpsimd.tensor_tensor(decay[:, 1, :HALF], a[1][:, :HALF], a_near[1][:, :HALF], MULT)
+        nc.gpsimd.tensor_tensor(decay[:, 2, :], a[2], a_near[2][:], MULT)
+
+        def outer(row):
+            return row.rearrange("p (c n) -> p c n", n=CHUNK)[:, 0 : CHUNKS : CHUNKS - 1]
+
+        nc.gpsimd.tensor_tensor(outer(decay[:, 1, :]), outer(a[1]), outer(a_near[1][:]), MULT)
         b2_late = tile([P, PACK, S - CHUNK], F32, "b2_late")
         b2 = {}
         sum_order = (0, 1, 3, 2)
         for t, tag in zip(sum_order, (None, None, "near_term0", "near_term1")):
-            b2[t] = tile([P, S], F32, "b2_%d" % t, tag)
-            nc.vector.tensor_tensor(b2[t][:], b_banks[t][:], near_term[t], ADD)
-            nc.sync.dma_start(out=b2_late[:, t, :], in_=b2[t][:, CHUNK:])
+            b2[t] = tile([P, 2 * S if t < 2 else S], F32, "b2_%d" % t, tag)
+            nc.vector.tensor_tensor(b2[t][:, :S], b_banks[t][:], near_term[t], ADD)
+            nc.sync.dma_start(out=b2_late[:, t, :], in_=b2[t][:, CHUNK:S])
 
         def make_decay(t, cols):
             nc.vector.tensor_tensor(decay[:, t, cols], a[t][:, cols], a_near[t][:, cols], MULT)
 
-        yq = tile([P, S], U32, "yq")
         ys = tile([P, S], U8, "ys")
         yg_all = tile([P, S, PACK], BF16, "yg_all")
         out_rows = out_0.rearrange("(p t) j -> p t j", t=PACK)
         out_words = out_1[0].rearrange("p n r -> p (n r)").bitcast(I32)
 
-        b2_far = {}
-        for c in (1, 2):
-            b2_far[c] = tile([P, PACK, CHUNK], F32, "b2_far%d" % c)
-            for t in sum_order:
-                nc.scalar.activation(
-                    b2_far[c][:, t, :], b2[t][:].indirect(entries(far_sb, c * CHUNK, (c + 1) * CHUNK)), COPY
-                )
+        b2_far_mid = tile([P, PACK, S - CHUNK], F32, "b2_far_mid")
+        for t, lo, hi in ((0, 0, S - CHUNK), (1, 0, S - CHUNK), (3, CHUNK, S - CHUNK), (2, HALF, S - CHUNK), (2, CHUNK, HALF)):
+            nc.scalar.activation(
+                b2_far_mid[:, t, lo:hi], b2[t][:].indirect(entries(far_sb, CHUNK + lo, CHUNK + hi)), COPY
+            )
+        b2_far = {3: b2_far_mid[:, :, HALF:], 2: b2_far_mid[:, :, CHUNK:HALF]}
 
         def weigh(c, tag):
             far_term = tile([P, PACK, CHUNK], F32, "far_term%d" % c, tag)
-            nc.vector.tensor_tensor(far_term[:], b2_far[c][:], decay[:, :, c * CHUNK : (c + 1) * CHUNK], MULT)
+            nc.vector.tensor_tensor(far_term[:], b2_far[c], decay[:, :, c * CHUNK : (c + 1) * CHUNK], MULT)
             return far_term
 
         def look_up_far(c, tag, planes):
@@ -271,9 +274,9 @@ def tile_picked_scan2_none_po_kernel(
             )
             return zg
 
-        def quantise_result(lo, hi):
+        def quantise_result(words, lo, hi):
             nc.vector.quantize_mx(
-                out=yq[:, lo:hi].bitcast(FP8X4),
+                out=words.bitcast(FP8X4),
                 scales=ys[:, lo:hi],
                 in_=yg_all[:, lo:hi, :].rearrange("p n t -> p (n t)"),
             )
@@ -307,39 +310,44 @@ def tile_picked_scan2_none_po_kernel(
 
         every = slice(0, PACK)
 
-        def empty_on_scalar(c, banks):
-            round_result(nc.scalar.copy, c, banks[0], every)
+        def store_then_round(c, banks):
             store_result(nc.scalar.copy, c, banks[0], every)
+            round_result(nc.scalar.copy, c, banks[0], every)
 
-        make_decay(0, halves[0])
+        inner = slice(CHUNK, S - CHUNK)
+        nc.vector.tensor_tensor(outer(decay[:, 0, :]), outer(a[0]), outer(a_near[0][:]), MULT)
         zg0 = turn_back(0, add_on_tensor(0, look_up_far(0, None, (3, 0, 2, 1))))
         b2_far_last = tile([P, 2, CHUNK], F32, "b2_far_last", "far_term0")
-        for t in range(2):
-            nc.scalar.activation(b2_far_last[:, t, :], b2[t][:].indirect(entries(far_sb, S - CHUNK, S)), COPY)
-        far1 = weigh(1, None)
-        make_decay(0, halves[1])
-        zg1 = add_on_vector(1, far1)
-        make_decay(1, halves[1])
-        empty_on_scalar(1, project(1, zg1, (5,)))
-        far2 = weigh(2, "far_term1")
-        empty_on_scalar(0, project(0, zg0, (4,), "zg1"))
-        zg2 = add_on_vector(2, far2)
-        empty_on_scalar(2, project(2, zg2, (6,)))
+        for t in (3, 2):
+            nc.scalar.activation(b2_far_last[:, t - 2, :], b2[t][:].indirect(entries(far_sb, CHUNK, HALF)), COPY)
+        make_decay(0, inner)
+        far3 = weigh(3, None)
+        make_decay(1, inner)
+        y3_banks = project(3, add_on_vector(3, far3), (5,))
+        round_result(nc.scalar.copy, 3, y3_banks[0], every)
+        store_result(nc.scalar.copy, 3, y3_banks[0], every)
+        zg2 = add_on_vector(2, weigh(2, "far_term3"))
+        store_then_round(0, project(0, zg0, (4,), "zg3"))
+        store_then_round(2, project(2, zg2, (6,)))
         warm_up = bank(5, [P, S])
         for t in range(2):
             product(warm_up, w3w[:, 2 * t * P : 2 * (t + 1) * P].bitcast(FP4X4), w3s[:, t * P : (t + 1) * P])
-        far3 = look_up_far(3, "zg0", (3, 2))
-        nc.vector.tensor_tensor(far3[:, :2, :], b2_far_last[:], decay[:, :2, S - CHUNK :], MULT)
-        quantise_result(0, HALF)
-        nc.sync.dma_start(out=out_words[:, :HALF], in_=yq[:, :HALF].bitcast(I32))
-        y3_banks = project(3, add_on_vector(3, far3), (7, 0))
-        round_result(nc.vector.tensor_copy, 3, y3_banks[0], slice(0, 2))
-        store_result(nc.scalar.copy, 3, y3_banks[1], slice(2, 4))
-        store_result(nc.vector.tensor_copy, 3, y3_banks[0], slice(0, 2))
-        round_result(nc.scalar.copy, 3, y3_banks[1], slice(2, 4))
-        quantise_result(S - CHUNK, S)
-        quantise_result(HALF, S - CHUNK)
-        nc.sync.dma_start(out=out_words[:, HALF:], in_=yq[:, HALF:].bitcast(I32))
+        far1 = tile([P, PACK, CHUNK], F32, "far_term1", "zg0")
+        nc.vector.tensor_tensor(far1[:, :2, :], b2_far_mid[:, :2, :CHUNK], decay[:, :2, CHUNK:HALF], MULT)
+        nc.vector.tensor_tensor(far1[:, 2:, :], b2_far_last[:], decay[:, 2:, CHUNK:HALF], MULT)
+        yq_first = tile([P, CHUNK], U32, "yq_first")
+        quantise_result(yq_first[:], S - CHUNK, S)
+        nc.sync.dma_start(out=out_words[:, S - CHUNK :], in_=yq_first[:].bitcast(I32))
+        y1_banks = project(1, add_on_vector(1, far1), (7, 0))
+        yq_rest = tile([P, S - CHUNK], U32, "yq_rest", "zg1")
+        quantise_result(yq_rest[:, :CHUNK], 0, CHUNK)
+        round_result(nc.vector.tensor_copy, 1, y1_banks[0], slice(0, 2))
+        store_result(nc.scalar.copy, 1, y1_banks[1], slice(2, 4))
+        store_result(nc.vector.tensor_copy, 1, y1_banks[0], slice(0, 2))
+        round_result(nc.scalar.copy, 1, y1_banks[1], slice(2, 4))
+        quantise_result(yq_rest[:, HALF:], HALF, S - CHUNK)
+        quantise_result(yq_rest[:, CHUNK:HALF], CHUNK, HALF)
+        nc.sync.dma_start(out=out_words[:, : S - CHUNK], in_=yq_rest[:].bitcast(I32))
         for q in range(4):
             queue = nc.scalar if q % 2 else nc.sync
             queue.dma_start(

@@ -212,7 +212,8 @@ def tile_picked_scan2_none_po_kernel(
             nc.vector.tensor_tensor(decay[:, t, cols], a[t][:, cols], a_near[t][:, cols], MULT)
 
         ys = tile([P, S], U8, "ys")
-        yg_all = tile([P, S, PACK], BF16, "yg_all")
+        yq = tile([P, S], U32, "yq")
+        yg = {c: tile([P, CHUNK, PACK], BF16, "yg%d" % c) for c in (0, 1, 3)}
         out_rows = out_0.rearrange("(p t) j -> p t j", t=PACK)
         out_words = out_1[0].rearrange("p n r -> p (n r)").bitcast(I32)
 
@@ -274,11 +275,11 @@ def tile_picked_scan2_none_po_kernel(
             )
             return zg
 
-        def quantise_result(words, lo, hi):
+        def quantise_result(c):
             nc.vector.quantize_mx(
-                out=words.bitcast(FP8X4),
-                scales=ys[:, lo:hi],
-                in_=yg_all[:, lo:hi, :].rearrange("p n t -> p (n t)"),
+                out=yq[:, c * CHUNK : (c + 1) * CHUNK].bitcast(FP8X4),
+                scales=ys[:, c * CHUNK : (c + 1) * CHUNK],
+                in_=yg[c][:].rearrange("p n t -> p (n t)"),
             )
 
         def project(c, zg, out_banks, tag=None):
@@ -302,7 +303,7 @@ def tile_picked_scan2_none_po_kernel(
         y = [tile([P, PACK, CHUNK], F32, "y%d" % c) for c in range(CHUNKS)]
 
         def round_result(copy, c, source, planes):
-            copy(out=yg_all[:, c * CHUNK : (c + 1) * CHUNK, planes], in_=source[:].rearrange("p t n -> p n t"))
+            copy(out=yg[c][:, :, planes], in_=source[:].rearrange("p t n -> p n t"))
 
         def store_result(copy, c, source, planes):
             copy(out=y[c][:, planes], in_=source[:])
@@ -310,9 +311,9 @@ def tile_picked_scan2_none_po_kernel(
 
         every = slice(0, PACK)
 
-        def store_then_round(c, banks):
-            store_result(nc.scalar.copy, c, banks[0], every)
+        def empty_on_scalar(c, banks):
             round_result(nc.scalar.copy, c, banks[0], every)
+            store_result(nc.scalar.copy, c, banks[0], every)
 
         inner = slice(CHUNK, S - CHUNK)
         nc.vector.tensor_tensor(outer(decay[:, 0, :]), outer(a[0]), outer(a_near[0][:]), MULT)
@@ -323,31 +324,27 @@ def tile_picked_scan2_none_po_kernel(
         make_decay(0, inner)
         far3 = weigh(3, None)
         make_decay(1, inner)
-        y3_banks = project(3, add_on_vector(3, far3), (5,))
-        round_result(nc.scalar.copy, 3, y3_banks[0], every)
-        store_result(nc.scalar.copy, 3, y3_banks[0], every)
+        empty_on_scalar(3, project(3, add_on_vector(3, far3), (5,)))
         zg2 = add_on_vector(2, weigh(2, "far_term3"))
-        store_then_round(0, project(0, zg0, (4,), "zg3"))
-        store_then_round(2, project(2, zg2, (6,)))
-        warm_up = bank(5, [P, S])
-        for t in range(2):
-            product(warm_up, w3w[:, 2 * t * P : 2 * (t + 1) * P].bitcast(FP4X4), w3s[:, t * P : (t + 1) * P])
+        empty_on_scalar(0, project(0, zg0, (4,), "zg3"))
+        store_result(nc.scalar.copy, 2, project(2, zg2, (6,))[0], every)
         far1 = tile([P, PACK, CHUNK], F32, "far_term1", "zg0")
         nc.vector.tensor_tensor(far1[:, :2, :], b2_far_mid[:, :2, :CHUNK], decay[:, :2, CHUNK:HALF], MULT)
         nc.vector.tensor_tensor(far1[:, 2:, :], b2_far_last[:], decay[:, 2:, CHUNK:HALF], MULT)
-        yq_first = tile([P, CHUNK], U32, "yq_first")
-        quantise_result(yq_first[:], S - CHUNK, S)
-        nc.sync.dma_start(out=out_words[:, S - CHUNK :], in_=yq_first[:].bitcast(I32))
-        y1_banks = project(1, add_on_vector(1, far1), (7, 0))
-        yq_rest = tile([P, S - CHUNK], U32, "yq_rest", "zg1")
-        quantise_result(yq_rest[:, :CHUNK], 0, CHUNK)
+        quantise_result(3)
+        nc.sync.dma_start(out=out_words[:, S - CHUNK :], in_=yq[:, S - CHUNK :].bitcast(I32))
+        zg1 = add_on_vector(1, far1)
+        quantise_result(0)
+        y1_banks = project(1, zg1, (7, 0))
+        yg[2] = tile([P, CHUNK, PACK], BF16, "yg2", "zg1")
+        round_result(nc.vector.tensor_copy, 2, y[2], every)
         round_result(nc.vector.tensor_copy, 1, y1_banks[0], slice(0, 2))
         store_result(nc.scalar.copy, 1, y1_banks[1], slice(2, 4))
         store_result(nc.vector.tensor_copy, 1, y1_banks[0], slice(0, 2))
         round_result(nc.scalar.copy, 1, y1_banks[1], slice(2, 4))
-        quantise_result(yq_rest[:, HALF:], HALF, S - CHUNK)
-        quantise_result(yq_rest[:, CHUNK:HALF], CHUNK, HALF)
-        nc.sync.dma_start(out=out_words[:, : S - CHUNK], in_=yq_rest[:].bitcast(I32))
+        quantise_result(2)
+        quantise_result(1)
+        nc.sync.dma_start(out=out_words[:, : S - CHUNK], in_=yq[:, : S - CHUNK].bitcast(I32))
         for q in range(4):
             queue = nc.scalar if q % 2 else nc.sync
             queue.dma_start(

@@ -199,7 +199,7 @@ def tile_picked_scan2_none_po_kernel(
         def outer(row):
             return row.rearrange("p (c n) -> p c n", n=CHUNK)[:, 0 : CHUNKS : CHUNKS - 1]
 
-        nc.gpsimd.tensor_tensor(outer(decay[:, 1, :]), outer(a[1]), outer(a_near[1][:]), MULT)
+        nc.gpsimd.tensor_tensor(decay[:, 1, :CHUNK], a[1][:, :CHUNK], a_near[1][:, :CHUNK], MULT)
         b2_late = tile([P, PACK, S - CHUNK], F32, "b2_late")
         b2 = {}
         sum_order = (0, 1, 3, 2)
@@ -317,13 +317,13 @@ def tile_picked_scan2_none_po_kernel(
 
         inner = slice(CHUNK, S - CHUNK)
         nc.vector.tensor_tensor(outer(decay[:, 0, :]), outer(a[0]), outer(a_near[0][:]), MULT)
+        make_decay(1, slice(CHUNK, S))
         zg0 = turn_back(0, add_on_tensor(0, look_up_far(0, None, (3, 0, 2, 1))))
         b2_far_last = tile([P, 2, CHUNK], F32, "b2_far_last", "far_term0")
         for t in (3, 2):
             nc.scalar.activation(b2_far_last[:, t - 2, :], b2[t][:].indirect(entries(far_sb, CHUNK, HALF)), COPY)
-        make_decay(0, inner)
         far3 = weigh(3, None)
-        make_decay(1, inner)
+        make_decay(0, inner)
         empty_on_scalar(3, project(3, add_on_vector(3, far3), (5,)))
         zg2 = add_on_vector(2, weigh(2, "far_term3"))
         empty_on_scalar(0, project(0, zg0, (4,), "zg3"))

@@ -126,8 +126,11 @@ def tile_picked_scan2_none_po_kernel(
         nc.vector.tensor_copy(out=w1s_early[:].rearrange("p (t h m) -> p h t m", t=2, h=2), in_=w1s_planes[:, :, 1:3])
 
         w2g = tile([P, PACK, P, PACK], BF16, "w2g")
-        w2q = [tile([P, P], U32, "w2q%d" % t) for t in range(PACK)]
-        w2s = [tile([P, P], U8, "w2s%d" % t) for t in range(PACK)]
+        w2_groups = (slice(3, 4), slice(2, 3), slice(0, 2))
+        w2q_parts = [tile([P, (g.stop - g.start) * P], U32, "w2q%d" % g.start) for g in w2_groups]
+        w2s_parts = [tile([P, (g.stop - g.start) * P], U8, "w2s%d" % g.start) for g in w2_groups]
+        w2q = [w2q_parts[2][:, :P], w2q_parts[2][:, P:], w2q_parts[1][:], w2q_parts[0][:]]
+        w2s = [w2s_parts[2][:, :P], w2s_parts[2][:, P:], w2s_parts[1][:], w2s_parts[0][:]]
         w2_dealt = w2g[:].rearrange("p t m j -> p m j t")
         w2_halves = [raw[:].rearrange("p j (m t) -> p m j t", t=PACK) for raw in w2_raw]
         nc.vector.tensor_copy(out=w2_dealt[:, : W2_FIRST // PACK], in_=w2_halves[0])
@@ -135,11 +138,13 @@ def tile_picked_scan2_none_po_kernel(
         deal_scales(nc, w3s_parts[:], w3s_raw[:])
         for pair in (slice(2, 4), slice(0, 2)):
             nc.vector.tensor_copy(out=w2_dealt[:, W2_FIRST // PACK :, :, pair], in_=w2_halves[1][:, :, :, pair])
-        for t in reversed(range(PACK)):
+        for u, planes in enumerate(w2_groups):
             nc.vector.quantize_mx(
-                out=w2q[t][:].bitcast(FP8X4), scales=w2s[t][:], in_=w2g[:, t].rearrange("p m j -> p (m j)")
+                out=w2q_parts[u][:].bitcast(FP8X4),
+                scales=w2s_parts[u][:],
+                in_=w2g[:, planes].rearrange("p t m j -> p (t m j)"),
             )
-            if t == 3:
+            if u == 0:
                 nc.vector.tensor_copy(out=w1s_last[:].rearrange("p (h m) -> p h m", h=2), in_=w1s_planes[:, :, 0])
 
         for q in range(4):
@@ -156,7 +161,7 @@ def tile_picked_scan2_none_po_kernel(
         decay = tile([P, PACK, S], F32, "decay")
         b_tables = {t: tile([P, 2 * S], F32, "b%d" % t)[:] for t in (0, 2, 3)}
         b_tables[1] = decay[:].rearrange("p t n -> p (t n)")
-        a_tables = [tile([P, 2 * S], F32, "a%d" % t) for t in range(3)]
+        a_tables = [tile([P, 2 * S], F32, "a%d" % t, "w2q3" if t == 1 else None) for t in range(3)]
         a = [table[:, :S] for table in a_tables] + [tile([P, S], F32, "a3")[:]]
         a3_table = tile([P, 2 * S], F32, "a3_table")
         near_term = [tile([P, S], F32, "near_term%d" % t)[:] for t in range(PACK)]
@@ -170,7 +175,7 @@ def tile_picked_scan2_none_po_kernel(
             nc.scalar.activation(a[t][:, cols], logit_banks[t][:, cols], SIGMOID)
 
         def make_b(t):
-            product(b_banks[t], w2q[t][:].bitcast(FP8X4), w2s[t][:])
+            product(b_banks[t], w2q[t].bitcast(FP8X4), w2s[t])
             nc.scalar.copy(out=b_tables[t][:, :S], in_=b_banks[t][:])
 
         for t in (3, 2, 1):
@@ -178,16 +183,16 @@ def tile_picked_scan2_none_po_kernel(
         gate(3, whole)
         nc.scalar.activation(a3_table[:, :S], logit_banks[3][:], SIGMOID)
         gate(2, whole)
-        gate(1, whole)
         nc.vector.tensor_tensor(decay[:, 3, :], a3_table[:].indirect(near_sb[:]), a[3], MULT)
         make_b(3)
         make_b(2)
+        gate(1, whole)
         gate_product(0)
         gate(0, whole)
         make_b(0)
         make_b(1)
 
-        a_near = [tile([P, S], F32, "a_near%d" % t, ("w2s0", "w2s1", "w2q1")[t]) for t in range(3)]
+        a_near = [tile([P, S], F32, "a_near%d" % t, ("w2s0", "w2s2", "w2q0")[t]) for t in range(3)]
         for t in (2, 1, 0):
             nc.scalar.activation(a_near[t][:], a_tables[t][:].indirect(near_sb[:]), COPY)
 

@@ -207,7 +207,7 @@ def tile_picked_scan2_none_po_kernel(
         nc.gpsimd.tensor_tensor(decay[:, 1, :CHUNK], a[1][:, :CHUNK], a_near[1][:, :CHUNK], MULT)
         b2_late = tile([P, PACK, S - CHUNK], F32, "b2_late")
         b2 = {}
-        sum_order = (0, 1, 3, 2)
+        sum_order = (0, 1, 2, 3)
         for t, tag in zip(sum_order, (None, None, "near_term0", "near_term1")):
             b2[t] = tile([P, 2 * S if t < 2 else S], F32, "b2_%d" % t, tag)
             nc.vector.tensor_tensor(b2[t][:, :S], b_banks[t][:], near_term[t], ADD)
@@ -223,7 +223,7 @@ def tile_picked_scan2_none_po_kernel(
         out_words = out_1[0].rearrange("p n r -> p (n r)").bitcast(I32)
 
         b2_far_mid = tile([P, PACK, S - CHUNK], F32, "b2_far_mid")
-        for t, lo, hi in ((0, 0, S - CHUNK), (1, 0, S - CHUNK), (3, CHUNK, S - CHUNK), (2, HALF, S - CHUNK), (2, CHUNK, HALF)):
+        for t, lo, hi in ((0, 0, S - CHUNK), (1, 0, S - CHUNK), (2, CHUNK, S - CHUNK), (3, CHUNK, HALF)):
             nc.scalar.activation(
                 b2_far_mid[:, t, lo:hi], b2[t][:].indirect(entries(far_sb, CHUNK + lo, CHUNK + hi)), COPY
             )
@@ -327,7 +327,8 @@ def tile_picked_scan2_none_po_kernel(
         b2_far_last = tile([P, 2, CHUNK], F32, "b2_far_last", "far_term0")
         for t in (3, 2):
             nc.scalar.activation(b2_far_last[:, t - 2, :], b2[t][:].indirect(entries(far_sb, CHUNK, HALF)), COPY)
-        far3 = weigh(3, None)
+        far3 = look_up_far(3, None, (3,))
+        nc.vector.tensor_tensor(far3[:, :3, :], b2_far[3][:, :3, :], decay[:, :3, S - CHUNK :], MULT)
         make_decay(0, inner)
         empty_on_scalar(3, project(3, add_on_vector(3, far3), (5,)))
         zg2 = add_on_vector(2, weigh(2, "far_term3"))

@@ -322,15 +322,17 @@ def tile_picked_scan2_none_po_kernel(
 
         inner = slice(CHUNK, S - CHUNK)
         nc.vector.tensor_tensor(outer(decay[:, 0, :]), outer(a[0]), outer(a_near[0][:]), MULT)
-        make_decay(1, slice(CHUNK, S))
+        make_decay(1, slice(S - CHUNK, S))
         zg0 = turn_back(0, add_on_tensor(0, look_up_far(0, None, (3, 0, 2, 1))))
         b2_far_last = tile([P, 2, CHUNK], F32, "b2_far_last", "far_term0")
         for t in (3, 2):
             nc.scalar.activation(b2_far_last[:, t - 2, :], b2[t][:].indirect(entries(far_sb, CHUNK, HALF)), COPY)
         far3 = look_up_far(3, None, (3,))
         nc.vector.tensor_tensor(far3[:, :3, :], b2_far[3][:, :3, :], decay[:, :3, S - CHUNK :], MULT)
+        make_decay(1, inner)
+        zg3 = add_on_vector(3, far3)
         make_decay(0, inner)
-        empty_on_scalar(3, project(3, add_on_vector(3, far3), (5,)))
+        empty_on_scalar(3, project(3, zg3, (5,)))
         zg2 = add_on_vector(2, weigh(2, "far_term3"))
         empty_on_scalar(0, project(0, zg0, (4,), "zg3"))
         store_result(nc.scalar.copy, 2, project(2, zg2, (6,))[0], every)

from contextlib import ExitStack

import concourse.mybir as mybir
from concourse.masks import make_identity

K, T, S, H, N = 512, 2048, 512, 512, 512
FLOPS = 2 * S * (2 * K * H + H * N)

F32 = mybir.dt.float32
BF16 = mybir.dt.bfloat16
I32 = mybir.dt.int32
U32 = mybir.dt.uint32
U16 = mybir.dt.uint16
U8 = mybir.dt.uint8
FP8X4 = mybir.dt.float8_e4m3fn_x4
FP4X4 = mybir.dt.float4_e2m1fn_x4
MULT = mybir.AluOpType.mult
ADD = mybir.AluOpType.add
COPY = mybir.ActivationFunctionType.Copy
SIGMOID = mybir.ActivationFunctionType.Sigmoid

P = 128
PACK = 4
LIST_ROWS = 16
HALF = S // 2
CHUNK = 128
CHUNKS = S // CHUNK
W2_FIRST = 320
ROW_PARTS = 2
LINE = 2


def load_scale_rows(queue, scale_tile, rows, quadrants=(0, 2, 1, 3)):
    for q in quadrants:
        queue.dma_start(
            out=scale_tile[32 * q : 32 * q + 4, :].bitcast(I32), in_=rows[4 * q : 4 * q + 4, :].bitcast(I32)
        )


def deal_words(nc, dealt, raw):
    nc.vector.tensor_copy(
        out=dealt.rearrange("p (t m e) -> p t m e", t=PACK, e=2),
        in_=raw.rearrange("p (m t e) -> p t m e", t=PACK, e=2),
    )


def deal_scales(nc, dealt, raw):
    nc.vector.tensor_copy(
        out=dealt.rearrange("p (t m) -> p t m", t=PACK),
        in_=raw.rearrange("p (m t) -> p t m", t=PACK),
    )


def entries(lists, lo, hi):
    return lists[:, lo // LIST_ROWS : hi // LIST_ROWS]


def tile_picked_scan2_none_po_kernel(
    tc, x_words, x_scales, w1_words, w1_scales, w2, w3_words, w3_scales, offs, near, far, out_0, out_1, out_2
):
    nc = tc.nc
    with ExitStack() as ctx:
        keep = ctx.enter_context(tc.tile_pool(name="keep", bufs=1))
        ring = ctx.enter_context(tc.tile_pool(name="ring", bufs=2))
        psum = ctx.enter_context(tc.psum_pool(name="psum", bufs=1))

        def tile(shape, dtype, name, tag=None):
            return keep.tile(shape, dtype, name=name, tag=tag or name, align_bytes=64)

        def bank(i, shape):
            return psum.tile(shape, F32, name="bank%d" % i)

        offs_sb = keep.tile([P, S // LIST_ROWS], U16, name="offs_sb")
        near_sb = keep.tile([P, S // LIST_ROWS], U16, name="near_sb")
        far_sb = keep.tile([P, S // LIST_ROWS], U16, name="far_sb")
        xw_raw = tile([P, T], I32, "xw_raw")
        xs_raw = tile([P, T], U8, "xs_raw")
        w1w_raw = tile([P, 2 * H], U8, "w1w_raw")
        w3w_raw = tile([P, 2 * N], U8, "w3w_raw")
        w1s_raw = tile([P, H], U8, "w1s_raw")
        w3s_raw = tile([P, N // ROW_PARTS], U8, "w3s_raw")
        w3s = tile([P, N], U8, "w3s")
        w2_raw = [tile([P, PACK, width], F32, "w2_raw%d" % u) for u, width in enumerate((W2_FIRST, H - W2_FIRST))]
        ident = tile([P, P], F32, "ident")

        nc.vector.memset(xs_raw[:].bitcast(I32), 0)
        nc.vector.memset(w1s_raw[:].bitcast(I32), 0)
        nc.vector.memset(w3s_raw[:].bitcast(I32), 0)
        nc.vector.memset(w3s[:].bitcast(I32), 0)
        nc.vector.memset(ident[:], 0.0)

        w2_rows = w2.rearrange("(p j) c -> p j c", j=PACK)
        nc.sync.dma_start(offs_sb[:], offs)
        nc.sync.dma_start(out=w1w_raw[:].bitcast(I32), in_=w1_words[0].bitcast(I32))
        nc.sync.dma_start(out=w3w_raw[:].bitcast(I32), in_=w3_words[0].bitcast(I32))
        load_scale_rows(nc.sync, xs_raw, x_scales[0])
        nc.sync.dma_start(out=xw_raw[:], in_=x_words[0].rearrange("p n r -> p (n r)").bitcast(I32))
        load_scale_rows(nc.sync, w1s_raw, w1_scales[0])
        nc.sync.dma_start(
            out=w3s_raw[: 16 * ROW_PARTS, :].bitcast(I32),
            in_=w3_scales[0].rearrange("j (s n) -> (j s) n", s=ROW_PARTS).bitcast(I32),
        )
        nc.sync.dma_start(out=w2_raw[0][:], in_=w2_rows[:, :, :W2_FIRST])
        nc.sync.dma_start(out=w2_raw[1][:], in_=w2_rows[:, :, W2_FIRST:])
        nc.sync.dma_start(near_sb[:], near)
        nc.sync.dma_start(far_sb[:], far)
        make_identity(nc, ident[:], nomemset=True)

        halves = (slice(0, HALF), slice(HALF, S))
        whole = slice(0, S)

        w1w = tile([P, 2 * H], U8, "w1w")
        xq = tile([P, S], U32, "xq")
        xqs = tile([P, S], U8, "xqs")
        w3w = tile([P, 2 * N], U8, "w3w")
        deal_words(nc, w1w[:], w1w_raw[:])
        deal_words(nc, w3w[:], w3w_raw[:])
        nc.vector.tensor_copy(xqs[:], xs_raw[:].indirect(offs_sb[:]))
        nc.vector.tensor_copy(xq[:], xw_raw[:].bitcast(U32).indirect(offs_sb[:]))
        w1s_first = tile([P, P], U8, "w1s_first")
        w1s_early = tile([P, 2 * P], U8, "w1s_early")
        w1s_last = tile([P, P], U8, "w1s_last", "w2_raw1")
        w1s = [w1s_last[:], w1s_early[:, :P], w1s_early[:, P:], w1s_first[:]]
        w1s_planes = w1s_raw[:].rearrange("p (h m t) -> p h t m", h=2, t=PACK)
        nc.vector.tensor_copy(out=w1s_first[:].rearrange("p (h m) -> p h m", h=2), in_=w1s_planes[:, :, 3])
        nc.vector.tensor_copy(out=w1s_early[:].rearrange("p (t h m) -> p h t m", t=2, h=2), in_=w1s_planes[:, :, 1:3])

        w2g = tile([P, PACK, P, PACK], BF16, "w2g")
        w2_groups = (slice(3, 4), slice(2, 3), slice(0, 2))
        w2q_parts = [tile([P, (g.stop - g.start) * P], U32, "w2q%d" % g.start) for g in w2_groups]
        w2s_parts = [tile([P, (g.stop - g.start) * P], U8, "w2s%d" % g.start) for g in w2_groups]
        w2q = [w2q_parts[2][:, :P], w2q_parts[2][:, P:], w2q_parts[1][:], w2q_parts[0][:]]
        w2s = [w2s_parts[2][:, :P], w2s_parts[2][:, P:], w2s_parts[1][:], w2s_parts[0][:]]
        w2_dealt = w2g[:].rearrange("p t m j -> p m j t")
        w2_halves = [raw[:].rearrange("p j (m t) -> p m j t", t=PACK) for raw in w2_raw]
        nc.vector.tensor_copy(out=w2_dealt[:, : W2_FIRST // PACK], in_=w2_halves[0])
        w3s_parts = tile([P, N // ROW_PARTS], U8, "w3s_parts")
        deal_scales(nc, w3s_parts[:], w3s_raw[:])
        for pair in (slice(2, 4), slice(0, 2)):
            nc.vector.tensor_copy(out=w2_dealt[:, W2_FIRST // PACK :, :, pair], in_=w2_halves[1][:, :, :, pair])
        for u, planes in enumerate(w2_groups):
            nc.vector.quantize_mx(
                out=w2q_parts[u][:].bitcast(FP8X4),
                scales=w2s_parts[u][:],
                in_=w2g[:, planes].rearrange("p t m j -> p (t m j)"),
            )
            if u == 0:
                nc.vector.tensor_copy(out=w1s_last[:].rearrange("p (h m) -> p h m", h=2), in_=w1s_planes[:, :, 0])

        for q in range(4):
            places = w3s[32 * q : 32 * q + 4, :].bitcast(I32).rearrange("p (t s m) -> p s t m", t=PACK, s=ROW_PARTS)
            for part in range(ROW_PARTS):
                rows = w3s_parts[4 * ROW_PARTS * q + part : 4 * ROW_PARTS * (q + 1) : ROW_PARTS, :]
                nc.sync.dma_start(out=places[:, part], in_=rows.bitcast(I32).rearrange("p (t m) -> p t m", t=PACK))

        def product(out, words, scales):
            nc.tensor.matmul_mx(
                out=out[:], lhsT=words, lhsT_scale=scales, rhs=xq[:].bitcast(FP8X4), rhs_scale=xqs[:], start=True, stop=True
            )

        decay = tile([P, PACK, S], F32, "decay")
        b_tables = {t: tile([P, 2 * S], F32, "b%d" % t)[:] for t in (0, 2, 3)}
        b_tables[1] = decay[:].rearrange("p t n -> p (t n)")
        a_tables = [tile([P, 2 * S], F32, "a%d" % t, "w2q3" if t == 1 else None) for t in range(3)]
        a = [table[:, :S] for table in a_tables] + [tile([P, S], F32, "a3")[:]]
        a3_table = tile([P, 2 * S], F32, "a3_table")
        near_term = [tile([P, S], F32, "near_term%d" % t)[:] for t in range(PACK)]
        logit_banks = [bank(t, [P, S]) for t in range(PACK)]
        b_banks = [bank(PACK + t, [P, S]) for t in range(PACK)]

        def gate_product(t):
            product(logit_banks[t], w1w[:, 2 * t * P : 2 * (t + 1) * P].bitcast(FP4X4), w1s[t])

        def gate(t, cols):
            nc.scalar.activation(a[t][:, cols], logit_banks[t][:, cols], SIGMOID)

        def make_b(t):
            product(b_banks[t], w2q[t].bitcast(FP8X4), w2s[t])
            nc.scalar.copy(out=b_tables[t][:, :S], in_=b_banks[t][:])

        for t in (3, 2, 1):
            gate_product(t)
        gate(3, whole)
        nc.scalar.activation(a3_table[:, :S], logit_banks[3][:], SIGMOID)
        gate(2, whole)
        nc.vector.tensor_tensor(decay[:, 3, :], a3_table[:].indirect(near_sb[:]), a[3], MULT)
        make_b(3)
        make_b(2)
        gate(1, whole)
        gate_product(0)
        gate(0, whole)
        make_b(0)
        make_b(1)

        a_near = [tile([P, S], F32, "a_near%d" % t, ("w2s0", "w2s2", "w2q0")[t]) for t in range(3)]
        for t in (2, 1, 0):
            nc.scalar.activation(a_near[t][:], a_tables[t][:].indirect(near_sb[:]), COPY)

        for t, cols in ((3, whole), (2, whole), (0, whole), (1, whole)):
            nc.vector.tensor_tensor(near_term[t][:, cols], b_tables[t].indirect(near_sb[:]), a[t][:, cols], MULT)

        nc.gpsimd.tensor_tensor(decay[:, 2, :], a[2], a_near[2][:], MULT)

        def outer(row):
            return row.rearrange("p (c n) -> p c n", n=CHUNK)[:, 0 : CHUNKS : CHUNKS - 1]

        nc.gpsimd.tensor_tensor(decay[:, 1, :CHUNK], a[1][:, :CHUNK], a_near[1][:, :CHUNK], MULT)
        b2_late = tile([P, PACK, S - CHUNK], F32, "b2_late")
        b2 = {}
        sum_order = (0, 1, 2, 3)
        for t, tag in zip(sum_order, (None, None, "near_term0", "near_term1")):
            b2[t] = tile([P, 2 * S if t < 2 else S], F32, "b2_%d" % t, tag)
            nc.vector.tensor_tensor(b2[t][:, :S], b_banks[t][:], near_term[t], ADD)
            nc.sync.dma_start(out=b2_late[:, t, :], in_=b2[t][:, CHUNK:S])

        def make_decay(t, cols):
            nc.vector.tensor_tensor(decay[:, t, cols], a[t][:, cols], a_near[t][:, cols], MULT)

        ys = tile([P, S], U8, "ys")
        yq = tile([P, S], U32, "yq")
        yg = {c: tile([P, CHUNK, PACK], BF16, "yg%d" % c) for c in (0, 1, 3)}
        out_rows = out_0.rearrange("(p t) j -> p t j", t=PACK)
        out_words = out_1[0].rearrange("p n r -> p (n r)").bitcast(I32)

        b2_far_mid = tile([P, PACK, S - CHUNK], F32, "b2_far_mid")
        for t, lo, hi in ((0, 0, S - CHUNK), (1, 0, S - CHUNK), (2, CHUNK, S - CHUNK), (3, CHUNK, HALF)):
            nc.scalar.activation(
                b2_far_mid[:, t, lo:hi], b2[t][:].indirect(entries(far_sb, CHUNK + lo, CHUNK + hi)), COPY
            )
        b2_far = {3: b2_far_mid[:, :, HALF:], 2: b2_far_mid[:, :, CHUNK:HALF]}

        def weigh(c, tag):
            far_term = tile([P, PACK, CHUNK], F32, "far_term%d" % c, tag)
            nc.vector.tensor_tensor(far_term[:], b2_far[c], decay[:, :, c * CHUNK : (c + 1) * CHUNK], MULT)
            return far_term

        def look_up_far(c, tag, planes):
            lo, hi = c * CHUNK, (c + 1) * CHUNK
            far_term = tile([P, PACK, CHUNK], F32, "far_term%d" % c, tag)
            for t in planes:
                nc.vector.tensor_tensor(
                    far_term[:, t, :], b2[t][:].indirect(entries(far_sb, lo, hi)), decay[:, t, lo:hi], MULT
                )
            return far_term

        def add_on_tensor(c, far_term):
            lo, hi = c * CHUNK, (c + 1) * CHUNK
            z_turned = bank(c, [P, PACK, P])
            for t in (3, 0, 2, 1):
                nc.tensor.matmul(
                    z_turned[:, t, :], lhsT=b2[t][:, lo:hi], rhs=ident[:], start=True, stop=False, is_transpose=True
                )
                nc.tensor.matmul(
                    z_turned[:, t, :], lhsT=far_term[:, t, :], rhs=ident[:], start=False, stop=True, is_transpose=True
                )
            return z_turned

        def turn_back(c, z_turned):
            rounded = ring.tile([P, 2, P, 2], BF16, name="rounded", align_bytes=64)
            nc.scalar.copy(out=rounded[:], in_=z_turned[:].rearrange("n (u e) p -> n u p e", e=2))
            pairs = rounded[:].rearrange("n u p e -> n (u p e)").bitcast(F32)
            pairs_back = bank(2 + c, [P, 2, CHUNK])
            for u in range(2):
                nc.tensor.transpose(pairs_back[:, u, :], pairs[:, u * P : (u + 1) * P], ident[:])
            zg = tile([P, CHUNK, PACK], BF16, "zg%d" % c)
            nc.scalar.copy(
                out=zg[:].rearrange("p n t -> p (n t)").bitcast(F32).rearrange("p (n u) -> p n u", u=2),
                in_=pairs_back[:].rearrange("p u n -> p n u"),
            )
            return zg

        def add_on_vector(c, far_term):
            lo = (c - 1) * CHUNK
            zg = tile([P, CHUNK, PACK], BF16, "zg%d" % c)
            nc.vector.tensor_tensor(
                zg[:].rearrange("p (n i) t -> p n t i", i=LINE),
                b2_late[:, :, lo : lo + CHUNK].rearrange("p t (n i) -> p n t i", i=LINE),
                far_term[:].rearrange("p t (n i) -> p n t i", i=LINE),
                ADD,
            )
            return zg

        def quantise_result(c):
            nc.vector.quantize_mx(
                out=yq[:, c * CHUNK : (c + 1) * CHUNK].bitcast(FP8X4),
                scales=ys[:, c * CHUNK : (c + 1) * CHUNK],
                in_=yg[c][:].rearrange("p n t -> p (n t)"),
            )

        def project(c, zg, out_banks, tag=None):
            zq = tile([P, CHUNK], U32, "zq%d" % c, tag)
            zs = tile([P, CHUNK], U8, "zs%d" % c)
            nc.vector.quantize_mx(out=zq[:].bitcast(FP8X4), scales=zs[:], in_=zg[:].rearrange("p n t -> p (n t)"))
            planes = PACK // len(out_banks)
            banks = [bank(i, [P, planes, CHUNK]) for i in out_banks]
            for t in range(PACK):
                nc.tensor.matmul_mx(
                    out=banks[t // planes][:, t % planes, :],
                    lhsT=w3w[:, 2 * t * P : 2 * (t + 1) * P].bitcast(FP4X4),
                    lhsT_scale=w3s[:, t * P : (t + 1) * P],
                    rhs=zq[:].bitcast(FP8X4),
                    rhs_scale=zs[:],
                    start=True,
                    stop=True,
                )
            return banks

        y = [tile([P, PACK, CHUNK], F32, "y%d" % c) for c in range(CHUNKS)]

        def round_result(copy, c, source, planes):
            copy(out=yg[c][:, :, planes], in_=source[:].rearrange("p t n -> p n t"))

        def store_result(copy, c, source, planes):
            copy(out=y[c][:, planes], in_=source[:])
            nc.sync.dma_start(out=out_rows[:, planes, c * CHUNK : (c + 1) * CHUNK], in_=y[c][:, planes])

        every = slice(0, PACK)

        def empty_on_scalar(c, banks):
            round_result(nc.scalar.copy, c, banks[0], every)
            store_result(nc.scalar.copy, c, banks[0], every)

        inner = slice(CHUNK, S - CHUNK)
        nc.vector.tensor_tensor(outer(decay[:, 0, :]), outer(a[0]), outer(a_near[0][:]), MULT)
        make_decay(1, slice(S - CHUNK, S))
        zg0 = turn_back(0, add_on_tensor(0, look_up_far(0, None, (3, 0, 2, 1))))
        b2_far_last = tile([P, 2, CHUNK], F32, "b2_far_last", "far_term0")
        for t in (3, 2):
            nc.scalar.activation(b2_far_last[:, t - 2, :], b2[t][:].indirect(entries(far_sb, CHUNK, HALF)), COPY)
        far3 = look_up_far(3, None, (3,))
        nc.vector.tensor_tensor(far3[:, :3, :], b2_far[3][:, :3, :], decay[:, :3, S - CHUNK :], MULT)
        make_decay(1, inner)
        zg3 = add_on_vector(3, far3)
        make_decay(0, inner)
        empty_on_scalar(3, project(3, zg3, (5,)))
        zg2 = add_on_vector(2, weigh(2, "far_term3"))
        empty_on_scalar(0, project(0, zg0, (4,), "zg3"))
        store_result(nc.scalar.copy, 2, project(2, zg2, (6,))[0], every)
        far1 = tile([P, PACK, CHUNK], F32, "far_term1", "zg0")
        nc.vector.tensor_tensor(far1[:, :2, :], b2_far_mid[:, :2, :CHUNK], decay[:, :2, CHUNK:HALF], MULT)
        nc.vector.tensor_tensor(far1[:, 2:, :], b2_far_last[:], decay[:, 2:, CHUNK:HALF], MULT)
        quantise_result(3)
        nc.sync.dma_start(out=out_words[:, S - CHUNK :], in_=yq[:, S - CHUNK :].bitcast(I32))
        zg1 = add_on_vector(1, far1)
        quantise_result(0)
        y1_banks = project(1, zg1, (7, 0))
        yg[2] = tile([P, CHUNK, PACK], BF16, "yg2", "zg1")
        round_result(nc.vector.tensor_copy, 2, y[2], every)
        round_result(nc.vector.tensor_copy, 1, y1_banks[0], slice(0, 2))
        store_result(nc.scalar.copy, 1, y1_banks[1], slice(2, 4))
        store_result(nc.vector.tensor_copy, 1, y1_banks[0], slice(0, 2))
        round_result(nc.scalar.copy, 1, y1_banks[1], slice(2, 4))
        quantise_result(2)
        quantise_result(1)
        nc.sync.dma_start(out=out_words[:, : S - CHUNK], in_=yq[:, : S - CHUNK].bitcast(I32))
        for q in range(4):
            queue = nc.scalar if q % 2 else nc.sync
            queue.dma_start(
                out=out_2[0][4 * q : 4 * q + 4, :].bitcast(I32), in_=ys[32 * q : 32 * q + 4, :].bitcast(I32)
            )
